import numpy as np, ml_dtypes
CORES = [3,11,19,27,35,43,51,59]
N = 8
BF = ml_dtypes.bfloat16
def gentries(a):
    return np.ascontiguousarray(a.reshape(8, 16, -1).transpose(0, 2, 1)).reshape(8, -1)
def gtable(e):
    e = np.asarray(e); return np.ascontiguousarray(e.reshape(8, -1, 16).transpose(0, 2, 1)).reshape(128, -1).astype(np.int32)
L, CAP, S, RO, PA = 1536, 256, 64, 2, 3
V = L + RO * CAP; W = V + (N - 1) * 2 * S + 1; NONE = W - 1
G8 = np.arange(8)[:, None]
ARR = np.concatenate([V + (d - 1) * 2 * S + np.arange(S) for d in range(1, N)])
def columns(x):
    return np.ascontiguousarray(x.reshape(N, 8, 16, -1).transpose(0, 1, 3, 2))
def flat(x):
    return np.ascontiguousarray(x.transpose(0, 1, 3, 2)).reshape(N, 128, -1)
def slots(rng, n, share):
    e = rng.integers(0, L, (N, 8, L, 16)); far = ARR[rng.integers(0, len(ARR), e.shape)]
    e = np.where(rng.random(e.shape) < share, far, e)
    return np.where(np.argsort(rng.random(e.shape), axis=-1) < n, e, NONE)
def showing(rng):
    return np.ascontiguousarray(np.argsort(rng.random((N, 8, N - 1, L)), axis=-1)[..., :S])
def pack(e, v, th, sh):
    return {"e": flat(e).astype(np.int32), "v0": flat(v).astype(np.float32).astype(BF), "th": np.ascontiguousarray(np.repeat(th, 16, axis=1)[:, :, None]).astype(np.int32),
            "sh": np.stack([gtable(a.reshape(8, -1)) for a in sh])}
def setup_inputs(rng):
    e = slots(rng, rng.integers(6, 17, (N, 8, L, 1)), 0.3)
    v = (256 * (0.25 + 0.75 * rng.random((N, 8, L, 1))) * rng.random((N, 8, L, 16))).astype(np.int64)
    base = np.array([120, 250, 400, 550, 700, 900, 1100, 1400])
    th = base[np.argsort(rng.random((N, 8)), axis=1)] + rng.integers(-50, 51, (N, 8))
    return pack(e, v, th, showing(rng))
def setup_inputs_room(rng):
    e = slots(rng, rng.integers(15, 17, (N, 8, L, 1)), 0.3)
    n = rng.choice(np.array([0, 1, CAP - 1, CAP, CAP + 1, L]), (N, 8)); n[0] = [CAP, CAP + 1, L, CAP - 1, 1, 0, CAP, CAP + 1]
    hot = np.argsort(rng.random((N, 8, L)), axis=-1) < n[:, :, None]; hot[0, 4] = False; hot[0, 4, L - 1] = True
    v = np.where(hot[..., None], rng.integers(200, 256, (N, 8, L, 16)), rng.integers(136, 200, (N, 8, L, 16)))
    return pack(e, v, np.full((N, 8), 3200), showing(rng))
def setup_inputs_ties(rng):
    e = slots(rng, rng.choice(np.array([8, 10, 12, 16]), (N, 8, L, 1)), 0.3)
    base = rng.integers(8, 128, (1, 8, 1, 16)); kind = rng.integers(1, 3, (N, 8, L, 1)); kind[:, ::2] = 2
    add = rng.integers(0, 2, (N, 8)); add[0] = 0; add[1, ::2] = 1
    th = np.sum(base, axis=-1)[..., 0] * np.where(np.arange(8) % 2 == 0, 2, 1)[None, :] + add
    return pack(e, base * kind, th, showing(rng))
def setup_inputs_ends(rng):
    e = slots(rng, rng.integers(10, 17, (N, 8, L, 1)), 0.3); v = rng.integers(60, 256, (N, 8, L, 16)); sh = showing(rng)
    e[:, 0] = rng.choice(np.array([0, L - 1, L, V - 1, V, V + S - 1, V + S, W - 2, NONE]), (N, L, 16))
    e[:, 1] = rng.integers(0, W, (N, L, 16)); e[:, 2] = ARR[rng.integers(0, len(ARR), (N, L, 16))]; e[:, 3] = rng.integers(0, L, (N, L, 16))
    e[:, 4] = rng.integers(0, L, (N, L, 1)); e[:, 4, :, 9] = NONE
    e[:, 5] = np.where(rng.random((N, L, 1)) < 0.3, NONE, e[:, 5])
    sh[:, ::2] = rng.choice(np.array([0, L - 1, L >> 1, 3]), (N, 4, N - 1, S))
    th = rng.choice(np.array([1, 2, 500, 1500]), (N, 8)); th[0, 7] = 4096; th[1, 0] = 1
    return pack(e, v, th, sh)
def setup_inputs_heavy(rng):
    e = slots(rng, rng.integers(0, 4, (N, 8, L, 1)), 0.2); v = rng.integers(1, 32, (N, 8, L, 16))
    o = 8 + np.argsort(rng.random((N, 8, L - 8)), axis=-1)[..., :64]; kind = rng.integers(0, 4, (N, 8, L))
    a = np.take_along_axis(o, rng.integers(0, 64, (N, 8, L)), 2); b = np.take_along_axis(o, rng.integers(0, 64, (N, 8, L)), 2)
    e[..., 0] = np.where((kind == 0) | (kind == 3), a, e[..., 0]); e[..., 15] = np.where((kind == 1) | (kind == 3), b, e[..., 15])
    one = np.arange(16) == rng.integers(0, 16, (N, 8, L, 1))
    e = np.where(kind[..., None] == 2, np.where(one, a[..., None], NONE), e)
    for q in range(N):
        for g in range(8):
            e[q, g, o[q, g]] = rng.choice(o[q, g], (64, 16)); v[q, g, o[q, g]] = 255
    e[:, :, 0] = NONE; v[:, :, :PA + 1] = 200
    for j in range(1, PA + 1): e[:, :, j] = j - 1
    e[:, ::2, PA, 0] = NONE
    th = rng.choice(np.array([1, 150, 250, 4080]), (N, 8)); th[0, 0] = 150; th[1, 3] = 4080; th[2, 5] = 2040; th[3, 3] = 4081; th[:, 6:] = 1
    sh = showing(rng)
    e[:, 6, :, 8:] = np.arange(L)[None, :, None]; v[:, 6] = rng.integers(1, 256, (N, L, 16))
    at = 0
    for r in range(RO):
        m = at + PA * (r + 1); e[:, 6, at] = NONE; v[:, 6, at:m + 1] = 200
        for j in range(at + 1, m + 1): e[:, 6, j] = j - 1
        e[1::2, 6, m, 0] = NONE
        at = m + 1 + CAP
    e[:, 6, PA + 1] = PA + 3; e[:, 6, PA + 1, 0] = PA + 2; v[:, 6, PA + 2] = 250; v[:, 6, PA + 3] = 255
    v[:, 6, L - 16:] = 0; e[:, 6, L - 16:] = NONE; e[:, 6, L - 16:, 3] = PA + 4; e[:, 6, L - 32:L - 16, 5] = np.arange(L - 16, L)
    t0 = (RO - 1) * CAP + 1; pool = np.concatenate([t0 + np.arange(CAP - 1), ARR])
    e[:, 7] = pool[rng.integers(0, len(pool), (N, L, 16))]; e[:, 7, :, 5:11] = NONE
    v[:, 7] = rng.integers(1, 256, (N, L, 16)); v[:, 7, t0:t0 + CAP - 1] = rng.integers(204, 256, (N, CAP - 1, 16))
    sh[:, 7] = t0 + np.argsort(rng.random((N, N - 1, CAP - 1)), axis=-1)[..., :S]; sh[:, 7, 0] = t0 + rng.integers(0, CAP - 1, (N, 1))
    e[:, 7, 0, 0] = ARR[-1]; e[:, 7, 1, 0] = V + S - 1
    e[1, 7, L - 1] = NONE; v[1, 7, L - 1] = 255; sh[1, 7, 1, 0] = L - 1; e[3, 7, 2] = V + 2 * S; v[3, 7, 2] = 255
    return pack(e, v, th, sh)
def setup_inputs_spread(rng):
    e = slots(rng, 16 - (14 * rng.random((N, 8, L, 1)) ** 2).astype(np.int64), 0.3)
    e = np.where((e < L) & (rng.random(e.shape) < 0.7), (L * rng.random(e.shape) ** 3).astype(np.int64), e)
    v = np.minimum((np.exp2(3 + 5 * rng.random((N, 8, L, 1))) * rng.random((N, 8, L, 16))).astype(np.int64), 255)
    th = np.minimum(np.maximum(np.exp2(12 * rng.random((N, 8))).astype(np.int64), 1), 4096); th[:, 2] = np.minimum(th[:, 2], 30)
    return pack(e, v, th, showing(rng))
def check_inputs(d):
    bad = []
    for k, lo, hi in (("e", 0, W - 1), ("th", 1, 4096), ("sh", 0, L - 1)):
        if np.min(d[k]) < lo or np.max(d[k]) > hi: bad.append("range of " + k)
    x = np.asarray(d["v0"]).astype(np.float64)
    if not np.all((x >= 0) & (x <= 255) & (x == np.floor(x))): bad.append("v0 is not whole numbers from 0 to 255")
    t = np.asarray(d["th"]).reshape(N, 8, 16)
    if not np.all(t == t[:, :, :1]): bad.append("th differs inside a group")
    return bad
def reference(e, v0, th, sh):
    E = np.full((N, 8, V, 16), NONE, np.int32); E[:, :, :L] = columns(e)
    v = np.zeros((N, 8, V, 16), np.int32); v[:, :, :L] = columns(v0.astype(np.float32)).astype(np.int32)
    t = th.reshape(N, 8, 16)[:, :, 0].astype(np.int64)
    half = np.full((N, 8, L), V, np.int64)
    sl = np.stack([gentries(a) for a in sh]).astype(np.int64).reshape(N, 8, N - 1, S)
    def show():
        z = np.concatenate([v, np.zeros((N, 8, 1, 16), np.int32)], axis=2); w = np.zeros((N, 8, W, 16), np.int32); w[:, :, :V] = v
        for a in range(N):
            for d in range(1, N):
                q = (a - d) % N; ix = sl[q, :, d - 1]; b = V + (d - 1) * 2 * S
                w[a, :, b:b + S] = z[q][G8, ix]; w[a, :, b + S:b + 2 * S] = z[q][G8, half[q][G8, ix]]
        return w
    for rnd in range(RO):
        for step in range(PA):
            w = show()
            for a in range(N):
                for g in range(8):
                    v[a, g] = np.minimum(v[a, g], np.add.reduce(w[a, g][E[a, g]], axis=1) >> 3)
        w = show(); fresh = np.zeros((N, 8, L), bool); new = np.full((N, 8, W), -1, np.int32)
        for a in range(N):
            for g in range(8):
                s = np.flatnonzero((half[a, g] == V) & (np.add.reduce(v[a, g, :L], axis=1) >= t[a, g]))[:CAP]
                h = L + CAP * rnd + np.arange(len(s)); old = E[a, g, s]
                C = np.add.accumulate(np.add.reduce(w[a, g][old], axis=2), axis=1)
                cut = np.argmax(2 * C >= C[:, 15:], axis=1); behind = np.arange(16)[None, :] > cut[:, None]
                E[a, g, h] = np.where(behind, old, NONE); E[a, g, s] = np.where(behind, NONE, old)
                x = (v[a, g, s] + 1) >> 1; v[a, g, s] = x; v[a, g, h] = x
                half[a, g, s] = h; fresh[a, g, s] = True; new[a, g, s] = h
        for a in range(N):
            for d in range(1, N):
                q = (a - d) % N; ix = sl[q, :, d - 1]; b = V + (d - 1) * 2 * S
                new[a, :, b:b + S] = np.where(fresh[q][G8, ix], b + S + np.arange(S)[None, :], -1)
            for g in range(8):
                n = new[a, g][E[a, g]]; has = n >= 0; empty = E[a, g] == NONE
                i = np.argmax(has, axis=1); m = np.argmax(empty, axis=1); c = np.flatnonzero(np.any(has, axis=1) & np.any(empty, axis=1))
                E[a, g, c, m[c]] = n[c, i[c]]
    return {"ye": flat(E).astype(np.float32), "yv": flat(v).astype(np.float32).astype(BF)}

@@ -1,0 +1,620 @@
+from concourse.bass import DstId, RemoteDMATransfer
+from concourse.mybir import AluOpType, AxisListType, ActivationFunctionType
+
+L, CAP, SH, N = 1536, 256, 64, 8
+V = L + 2 * CAP
+NONE = V + (N - 1) * 2 * SH
+MID = V - 1
+WW = NONE + 16
+HV = L + CAP
+OFF = {"w0": 0, "w1": 0, "w2": HV}
+NG = 5
+NE = 6
+CM = 384
+CQ = 320
+
+C0 = (384, 384, 304, 208, 128, 80, 48)
+C1 = (384, 384, 384, 288, 176, 112, 64)
+C5 = (256, 320, 320, 320, 256, 192, 128)
+C9 = (256, 320, 320, 320, 320, 256, 192, 64)
+F0 = (0.46,)
+F3 = (0.46, 0.46, 0.46, 0.2, 0.1, 0.3, 0.4)
+F7 = (0.46, 0.46, 0.46, 0.15, 0.3, 0.1, 0.2)
+F5 = (0.42, 0.42, 0.4, 0.3, 0.1, 0.0, 0.0)
+F9 = (0.4, 0.4, 0.4, 0.4, 0.35, 0.2, 0.0, 0.0)
+FW = 0.4
+
+SCRATCH = {
+    "w0": ("sbuf", [128, WW], "bfloat16"),
+    "w1": ("sbuf", [128, WW], "bfloat16"),
+    "w2": ("sbuf", [128, HV + WW], "bfloat16"),
+    "ee": ("sbuf", [128, L], "int32"),
+    "ed": ("sbuf", [128, V], "float32"),
+    "el": ("sbuf", [128, V], "uint16"),
+    "ec": ("sbuf", [128, V], "float16"),
+    "fe": ("sbuf", [128, V], "bfloat16"),
+    "emp": ("sbuf", [128, 2 * CQ], "bfloat16"),
+    "ti": ("sbuf", [128, 2 * CM], "int32"),
+    "shi": ("sbuf", [128, 28], "int32"),
+    "sl": ("sbuf", [128, 28], "uint16"),
+    "sl2": ("sbuf", [128, 28], "uint16"),
+    "sl5": ("sbuf", [128, 56], "uint16"),
+    "sl6": ("sbuf", [128, 56], "uint16"),
+    "sb0": ("sbuf", [128, 896], "bfloat16"),
+    "sb1": ("sbuf", [128, 896], "bfloat16"),
+    "thi": ("sbuf", [128, 1], "int32"),
+    "thf": ("sbuf", [128, 1], "float32"),
+    "ones": ("sbuf", [128, CM], "bfloat16"),
+    "basec": ("sbuf", [128, 96], "float32"),
+    "zz": ("sbuf", [128, 96], "float32"),
+    "iotac": ("sbuf", [128, V], "float32"),
+    "thr": ("sbuf", [128, 1], "float32"),
+    "cand": ("sbuf", [128, 96], "bfloat16"),
+    "splt": ("sbuf", [128, 96], "bfloat16"),
+    "pfx": ("sbuf", [128, 96], "float32"),
+    "rk": ("sbuf", [128, 96], "float32"),
+    "of": ("sbuf", [128, 96], "float32"),
+    "ofu": ("sbuf", [128, 96], "uint16"),
+    "self": ("sbuf", [128, 2 * L], "float32"),
+    "selh": ("sbuf", [128, 256], "float16"),
+    "sel": ("sbuf", [128, 32], "uint16"),
+    "xi": ("sbuf", [128, 256], "int32"),
+    "px": ("sbuf", [128, 512], "bfloat16"),
+    "neg": ("sbuf", [128, 256], "bfloat16"),
+    "dd": ("sbuf", [128, 256], "float32"),
+    "dl": ("sbuf", [128, 256], "uint16"),
+    "beh": ("sbuf", [128, 256], "float32"),
+    "mm_": ("sbuf", [128, 256], "float32"),
+    "newd": ("sbuf", [128, WW], "float32"),
+    "hb": ("sbuf", [128, 448], "float16"),
+    "tl0": ("sbuf", [128, 32], "uint16"),
+    "tl1": ("sbuf", [128, 32], "uint16"),
+    "yo": ("sbuf", [128, V], "float32"),
+}
+for _n in ("ga", "gm", "ii", "i8", "dc", "up", "tri", "lo", "lm", "o32", "d8k", "i2", "ith"):
+    SCRATCH[_n] = ("sbuf", [128, 128], "bfloat16")
+for _n in ("bk", "mka", "mkb", "mk", "aka", "akb", "ak"):
+    SCRATCH[_n] = ("sbuf", [128, 2048], "bfloat16")
+for _n in ("pi", "pj", "pb"):
+    SCRATCH[_n] = ("sbuf", [128, 96], "int32")
+for _k in range(NG):
+    SCRATCH["g%d" % _k] = ("sbuf", [128, 16 * CM], "bfloat16")
+for _k in range(2):
+    for _n, _t in (("f", "bfloat16"), ("ff", "bfloat16"), ("x", "float16"), ("gp", "bfloat16"), ("pr", "float16")):
+        SCRATCH["%s%d" % (_n, _k)] = ("sbuf", [128, CQ], _t)
+for _k in range(8):
+    SCRATCH["ps%d" % _k] = ("psum", [128, 512], "float32")
+
+SEMAPHORES = ["qv", "qs", "qt", "qg"] + ["ar%d" % k for k in range(1, 10)] + ["sn%d" % k for k in range(1, 10)] + ["ld%d" % k for k in range(30)]
+
+A = AluOpType
+COPY = ActivationFunctionType.Copy
+IDENT = ActivationFunctionType.Identity
+SIGM = ActivationFunctionType.Sigmoid
+SEMQ = {"v": "qv", "s": "qs", "t": "qt", "g": "qg"}
+
+
+def rank_program(g, core, T, topo):
+    rank = T.rank_of(core)
+    if rank is None:
+        return
+    eng = {"v": g.vector, "s": g.scalar, "t": g.tensor, "g": g, "y": g.sync}
+
+    cnt = {"qv": 0, "qs": 0, "qt": 0, "qg": 0}
+    know = {q: {} for q in eng}
+    acc = {}
+    total = {}
+    ndma = [0]
+
+    def need(q, tok):
+        sem, val, snap = tok
+        if know[q].get(sem, 0) >= val:
+            return
+        eng[q].wait_ge(T.sem[sem], val)
+        for s_, v_ in snap.items():
+            if know[q].get(s_, 0) < v_:
+                know[q][s_] = v_
+        know[q][sem] = val
+
+    def deps(q, reads, writes):
+        best = {}
+        for lst, wr in ((reads, False), (writes, True)):
+            for b, a0, a1 in lst:
+                ps = b[:2] == "ps"
+                for (c0, c1, kind, tok, q2) in acc.get(b, ()):
+                    if ps:
+                        if q2 == q and (q == "t" or not (wr or kind)):
+                            continue
+                        if q2 == q and (c0 >= a1 or a0 >= c1):
+                            continue
+                    elif c0 >= a1 or a0 >= c1 or not (wr or kind):
+                        continue
+                    if tok[0] not in best or best[tok[0]][1] < tok[1]:
+                        best[tok[0]] = tok
+        for t in sorted(best.values(), key=lambda t: -len(t[2])):
+            need(q, t)
+
+    def note(q, tok, reads, writes):
+        for lst, kind in ((writes, True), (reads, False)):
+            for b, a0, a1 in lst:
+                keep = []
+                for e in acc.get(b, []):
+                    inside = a0 <= e[0] and e[1] <= a1
+                    if inside and (kind or (not e[2] and e[4] == q)):
+                        continue
+                    keep.append(e)
+                keep.append((a0, a1, kind, tok, q))
+                acc[b] = keep
+
+    def iv(s):
+        if s[0] == "ind":
+            return iv(s[1]) + iv(s[2])
+        return [(s[0], s[1], s[2])]
+
+    def ap(s):
+        if s[0] == "ind":
+            return ap(s[1]).indirect(ap(s[2]))
+        if len(s) == 4:
+            return T[s[0]][:, s[1]:s[2]:s[3]]
+        return T[s[0]][:, s[1]:s[2]]
+
+    def emit(q, out, ins, fn):
+        reads, writes = [], []
+        for s in ins:
+            reads += iv(s)
+        if out[0] == "ind":
+            writes += iv(out[1])
+            reads += iv(out[2])
+        else:
+            writes += iv(out)
+        deps(q, reads, writes)
+        sem = SEMQ[q]
+        snap = dict(know[q])
+        fn(eng[q]).then_inc(T.sem[sem], 1)
+        cnt[sem] += 1
+        total[sem] = cnt[sem]
+        note(q, (sem, cnt[sem], snap), reads, writes)
+
+    def ind(win, off):
+        return ("ind", win, off)
+
+    def vcopy(o, i):
+        emit("v", o, [i], lambda e: e.tensor_copy(ap(o), ap(i)))
+
+    def vtt(o, i0, i1, op):
+        emit("v", o, [i0, i1], lambda e: e.tensor_tensor(ap(o), ap(i0), ap(i1), op))
+
+    def vts(o, i0, s1, op0, s2=None, op1=None):
+        col = isinstance(s1, tuple)
+        a1 = ap(s1) if col else s1
+        ins = [i0, s1] if col else [i0]
+        if op1 is None:
+            emit("v", o, ins, lambda e: e.tensor_scalar(ap(o), ap(i0), a1, None, op0))
+        else:
+            emit("v", o, ins, lambda e: e.tensor_scalar(ap(o), ap(i0), a1, s2, op0, op1))
+
+    def mset(o, c):
+        emit("v", o, [], lambda e: e.memset(ap(o), c))
+
+    def act(o, i, bias=0.0):
+        if bias == 0.0:
+            emit("s", o, [i], lambda e: e.activation(ap(o), ap(i), COPY))
+        else:
+            emit("s", o, [i], lambda e: e.activation(ap(o), ap(i), IDENT, bias, 1.0))
+
+    def step(o, i, bias, scale):
+        emit("s", o, [i], lambda e: e.activation(ap(o), ap(i), SIGM, bias, scale))
+
+    def mm(o, l, r, start, stop):
+        emit("t", o, [l, r], lambda e: e.matmul(ap(o), ap(l), ap(r), start, stop))
+
+    def asel(o, i, pat, op, fill, base, cm):
+        emit("g", o, [i], lambda e: e.affine_select(ap(o), ap(i), pat, op, fill, base, cm))
+
+    def iota(o, pat, base, cm, small=False):
+        if small:
+            emit("g", o, [], lambda e: e.iota(ap(o), pat, base, cm, allow_small_or_imprecise_dtypes=True))
+        else:
+            emit("g", o, [], lambda e: e.iota(ap(o), pat, base, cm))
+
+    def dma(q, o_ap, i_ap, outs, ins):
+        deps(q, ins, outs)
+        sem = "ld%d" % ndma[0]
+        ndma[0] += 1
+        snap = dict(know[q])
+        eng[q].dma_start(o_ap, i_ap).then_inc(T.sem[sem], 16)
+        total[sem] = 16
+        note("d", (sem, 16, snap), ins, outs)
+
+    def wb(k):
+        return "w%d" % (k % 3)
+
+    def col(w, a, b):
+        return (w, OFF[w] + a, OFF[w] + b)
+
+    def blk(m, i):
+        return (m, 128 * i, 128 * i + 128)
+
+    def sq(m):
+        return (m, 0, 128)
+
+    def show(k, src, lst, width, share=0.5):
+        n = 7 * width
+        lc = n // 16
+        h = int(lc * share) // 2 * 2
+        sb = "sb%d" % (k % 2)
+        vcopy((sb, 0, h * 16), ind(src, (lst, 0, h)))
+        act((sb, h * 16, n), ind(src, (lst, h, lc)))
+        reads = [(sb, 0, n)]
+        deps("g", reads, [])
+        tr, land = [], []
+        for d in range(1, N):
+            dst = T.cores[(rank + d) % N]
+            a = topo.addr(dst)
+            e = topo.engines(core, dst)[d - 1]
+            b = V + (d - 1) * 2 * SH
+            spot = col(wb(k), b, b + width)
+            land.append(spot)
+            tr.append(RemoteDMATransfer(dst_ids=[DstId(rid=a[0], pnc=a[1])], dma_engine_mask=1 << e, remote_sem=T.sem["ar%d" % k],
+                                        src=T[sb][:, (d - 1) * width:d * width], dst=ap(spot)))
+        g.remote_dma_fused(tr, local_sem=T.sem["sn%d" % k])
+        total["sn%d" % k] = 7
+        total["ar%d" % k] = 7
+        note("r", ("sn%d" % k, 7, dict(know["g"])), reads, [])
+        for spot in land:
+            note("r", ("ar%d" % k, 7, {}), [], [spot])
+
+    gi = [0]
+
+    def even(x):
+        return int(x) // 2 * 2
+
+    def at(f, i):
+        return f[min(i, len(f) - 1)]
+
+    def chunks(sizes):
+        res, a = [], 0
+        for s in sizes:
+            res.append((a, a + s))
+            a += s
+        return res
+
+    def gather(k, a, b, fv, parts=1):
+        G = "g%d" % (gi[0] % NG)
+        gi[0] += 1
+        w = b - a
+        v = even(w * fv + 1)
+        win = col(wb(k), 0, WW)
+        cuts = [even(v * i / parts) for i in range(parts)] + [v]
+        act((G, 16 * v, 16 * w), ind(win, ("el", a + v, b)))
+
+        def part(i):
+            p, q = cuts[i], cuts[i + 1]
+            if q > p:
+                vcopy((G, 16 * p, 16 * q), ind(win, ("el", a + p, a + q)))
+        if parts == 1:
+            part(0)
+        return G, part
+
+    def sums(G, ps, w, const):
+        if const:
+            mm((ps, 0, w), sq("dc"), ("ones", 0, w), True, False)
+        for i in range(16):
+            mm((ps, 0, w), sq("i8"), (G, i, 16 * w, 16), i == 0 and not const, i == 15 and const)
+
+    def mins(ps, old, new, a, b, par):
+        w = b - a
+        o = CM * (par % 2)
+        vtt(("ti", o, o + w), (ps, 0, w), col(old, a, b), A.min)
+        vcopy(col(new, a, b), ("ti", o, o + w))
+
+    def clip(k, sizes, fv, hook=None):
+        ch = chunks(sizes)
+        M = len(ch)
+        for i in range(M + 1):
+            if i < M:
+                G, _p = gather(k, ch[i][0], ch[i][1], at(fv, i))
+            if i:
+                mins("ps%d" % ((i - 1) % 4), wb(k), wb(k + 1), ch[i - 1][0], ch[i - 1][1], i - 1)
+            if i < M:
+                if hook:
+                    hook(i)
+                sums(G, "ps%d" % (i % 4), ch[i][1] - ch[i][0], True)
+
+    def sel_piece(r, w, a, b):
+        m0, m1 = a // 16, b // 16
+        nm = m1 - m0
+        for k in range(16):
+            mm(("ps4", 0, nm), blk("bk", k), col(w, a + k, b) + (16,), k == 0, k == 15 and r == 0)
+        if r:
+            mm(("ps4", 0, nm), sq("d8k"), ("splt", m0, m1), False, True)
+        vts(("cand", m0, m1), ("ps4", 0, nm), ("thf", 0, 1), A.is_ge)
+        mm(("ps6", 0, nm), sq("gm"), ("cand", m0, m1), True, True)
+        mm(("ps5", 0, nm), sq("lm"), ("cand", m0, m1), True, True)
+        init = ("pfx", m0 - 1, m0)
+        ini = ap(init) if a else 8191.0
+        emit("v", ("pfx", m0, m1), [("ps6", 0, nm), ("zz", m0, m1)] + ([init] if a else []),
+             lambda e: e.tensor_tensor_scan(ap(("pfx", m0, m1)), ap(("ps6", 0, nm)), ap(("zz", m0, m1)), ini, A.add, A.add))
+        vtt(("rk", m0, m1), ("ps5", 0, nm), ("pfx", m0, m1), A.add)
+        vtt(("of", m0, m1), ("rk", m0, m1), ("basec", m0, m1), A.min)
+        vcopy(("ofu", m0, m1), ("of", m0, m1))
+        vcopy(ind(("self", 0, 2 * L), ("ofu", m0, m1)), ("iotac", a, b))
+
+    S16 = ("sel", 0, 16)
+
+    def sel_list(r):
+        vcopy(("selh", 0, 256), ("self", 0, 256))
+        for k in range(16):
+            mm(("ps7", 0, 16), blk("bk", k), ("selh", k, 256, 16), k == 0, k == 15)
+        vts(S16, ("ps7", 0, 16), 0.0625, A.mult, 0.0, A.add)
+        if r == 0:
+            vts(("sel", 16, 32), ("ps7", 0, 16), 0.0625, A.mult, float(HV), A.add)
+
+    def split(r, k):
+        w = wb(k)
+        h0 = L + CAP * r
+        for q in range(2):
+            o = 128 * q
+            vs = even(128 * FW)
+            act(("g%d" % q, 16 * vs, 2048), ind(col(w, 0, WW), ("dl", o + vs, o + 128)))
+            vcopy(("g%d" % q, 0, 16 * vs), ind(col(w, 0, WW), ("dl", o, o + vs)))
+            for i in range(16):
+                mm(("ps6", o, o + 128), blk("ak", i), ("g%d" % q, i, 2048, 16), i == 0, i == 15)
+        vts(ind(("newd", 0, V), S16), ("iotac", h0, h0 + CAP), 1.0, A.mult, -float(NONE), A.add)
+        mset(("newd", V - 8, V), 0.0)
+        vcopy(ind(col(w, 0, V), S16), ("px", 0, 256))
+        vcopy(col(w, h0, h0 + CAP), ("px", 0, 256))
+        vts(("beh", 0, 256), ("ps6", 0, 256), ("thr", 0, 1), A.is_ge)
+        vtt(("mm_", 0, 256), ("beh", 0, 256), ("dd", 0, 256), A.mult)
+        vtt(ind(("ed", 0, V), S16), ("dd", 0, 256), ("mm_", 0, 256), A.subtract)
+        act(("ed", h0, h0 + CAP), ("mm_", 0, 256))
+
+    def pointer_pass(k, sizes, fv, last, hook=None):
+        ch = chunks(sizes)
+        M = len(ch)
+        old, new = wb(k - 1), wb(k + 1)
+        win = col(wb(k), 0, WW)
+        Gs = {}
+
+        def sb(j):
+            return "ps%d" % (j % 4)
+
+        def xb(j):
+            return ("ps4" if j % 2 else "ps5") if last else "ps5"
+
+        def prep(i):
+            a, b = ch[i]
+            vts(("el", a, b), ("ed", a, b), float(NONE), A.add)
+            Gs[i] = gather(k, a, b, at(fv, i), 2)
+
+        def empties(i):
+            a, b = ch[i]
+            w = b - a
+            o = CQ * (i % 2)
+            vts(("emp", o, o + w), ("el", a, b), float(NONE), A.is_equal)
+            vts(("ec", a, b), ("el", a, b), float(MID), A.subtract)
+            mm(("ps6", 64, 64 + w), sq("tri"), ("emp", o, o + w), True, True)
+            vts(("fe", a, b), ("ps6", 64, 64 + w), 1.0, A.is_ge)
+
+        prep(0)
+        prep(1)
+        Gs[0][1](0)
+        Gs[0][1](1)
+        empties(0)
+        for i in range(M + 3):
+            n0, n1, n2, n3 = i < M, 0 <= i - 1 < M, 0 <= i - 2 < M, 0 <= i - 3 < M
+            late = i >= M if last else i + 2 >= M
+            if n0:
+                w = ch[i][1] - ch[i][0]
+                G = Gs[i][0]
+            if n1:
+                a1, b1 = ch[i - 1]
+                w1 = b1 - a1
+                p1 = (i - 1) % 2
+                f, ff, x = "f%d" % p1, "ff%d" % p1, "x%d" % p1
+            if n2:
+                a2, b2 = ch[i - 2]
+                w2 = b2 - a2
+                p2 = i % 2
+                tl, gp, pr = "tl%d" % p2, "gp%d" % p2, "pr%d" % p2
+            if n3:
+                a3, b3 = ch[i - 3]
+                w3 = b3 - a3
+                mm(("ps7", 0, w3), sq("ii"), ("ec", a3, b3), True, False)
+                mm(("ps7", 0, w3), sq("ii"), ("pr%d" % ((i - 3) % 2), 0, w3), False, True)
+                if last:
+                    act(("yo", a3, b3), ("ps7", 0, w3), bias=float(MID))
+                    dma("y", T.ye[:, a3:b3], T.yo[:, a3:b3], [], [("yo", a3, b3)])
+                else:
+                    act(("ed", a3, b3), ("ps7", 0, w3), bias=float(MID - NONE))
+                    mm((sb(i - 3), 0, w3), sq("dc"), ("ones", 0, w3), False, False)
+                    mm((sb(i - 3), 0, w3), sq("i8"), ("gp%d" % ((i - 3) % 2), 0, w3), False, True)
+            if n0 and not last:
+                sums(G, sb(i), w, False)
+            if n1 and not last:
+                if late:
+                    step((f, 0, w1), ("ps4", 0, w1), -128.0, -1.0)
+                else:
+                    vts((f, 0, w1), ("ps4", 0, w1), 0.0, A.is_lt)
+                mm(("ps5", 0, w1), sq("tri"), (f, 0, w1), True, False)
+                mm(("ps5", 0, w1), sq("gm"), ("fe", a1, b1), False, True)
+                mm((sb(i - 1), 0, w1), sq("o32"), (f, 0, w1), False, False)
+            if i + 1 < M:
+                Gs[i + 1][1](0)
+            if n2:
+                vts((tl, 0, w2 // 16), ("ps6", 0, w2 // 16), float(MID), A.add)
+                if not last:
+                    act((gp, 0, w2), ind(win, (tl, 0, w2 // 16)))
+            if i + 2 < M:
+                prep(i + 2)
+            if i + 1 < M:
+                empties(i + 1)
+            if n0 and last:
+                mm((xb(i), 0, w), sq("gm"), ("fe", ch[i][0], ch[i][1]), True, False)
+                for q in range(16):
+                    mm((xb(i), 0, w), blk("mk", q), (G, q, 16 * w, 16), False, q == 15)
+            if n1:
+                if late:
+                    step((ff, 0, w1), (xb(i - 1), 0, w1), -300.0, 200.0)
+                else:
+                    vts((ff, 0, w1), (xb(i - 1), 0, w1), 2.0, A.is_ge)
+                vtt((x, 0, w1), (ff, 0, w1), ("ec", a1, b1), A.mult)
+            if n0 and not last:
+                for q in range(16):
+                    mm(("ps4", 0, w), blk("bk", q), (G, q, 16 * w, 16), q == 0, q == 15)
+            if n1:
+                for q in range(16):
+                    mm(("ps6", 0, w1 // 16), blk("bk", q), (x, q, w1, 16), q == 0, q == 15)
+                if not last:
+                    mm((sb(i - 1), 0, w1), sq("o32"), (ff, 0, w1), False, False)
+            if i + 1 < M:
+                Gs[i + 1][1](1)
+            if n2:
+                vtt((pr, 0, w2), ind(("newd", 0, WW), (tl, 0, w2 // 16)), ("fe", a2, b2), A.mult)
+            if n3 and not last:
+                mins(sb(i - 3), old, new, a3, b3, i - 3)
+            if hook:
+                hook(i)
+
+    dma("y", T.shi[:, :], T.sh[:, :], [("shi", 0, 28)], [])
+    dma("y", T.w1[:, 0:L // 2], T.v0[:, 0:L // 2], [("w1", 0, L // 2)], [])
+    dma("s", T.w1[:, L // 2:L], T.v0[:, L // 2:L], [("w1", L // 2, L)], [])
+    ce = L // NE
+    for j in range(NE):
+        dma("y", T.ee[:, j * ce:(j + 1) * ce], T.e[:, j * ce:(j + 1) * ce], [("ee", j * ce, (j + 1) * ce)], [])
+    dma("y", T.thi[:, :], T.th[:, :], [("thi", 0, 1)], [])
+
+    G8 = [[0, 8], [1, 16]]
+
+    def zero_window(w):
+        mset(col(w, L, V), 0.0)
+        mset(col(w, NONE, WW), 0.0)
+        for d in range(1, N):
+            b = V + (d - 1) * 2 * SH + SH
+            mset(col(w, b, b + SH), 0.0)
+
+    mset(("ones", 0, CM), 1.0)
+    asel(sq("ii"), ("ones", 0, 128), [[-1, 128]], A.is_equal, 0.0, 0, 1)
+    asel(sq("ga"), ("ones", 0, 128), [[-16, 8], [0, 16]], A.is_ge, 0.0, 0, 1)
+    asel(sq("gm"), sq("ga"), [[16, 8], [0, 16]], A.is_ge, 0.0, 15, -1)
+    mset(("w1", L, V), 0.0)
+    vcopy(("sl", 0, 28), ("shi", 0, 28))
+    show(1, ("w1", 0, V), "sl", SH)
+    vts(sq("i8"), sq("ii"), 0.125, A.mult)
+    vts(sq("dc"), sq("ii"), -0.4375, A.mult)
+    for j in range(NE):
+        vcopy(("el", j * ce, (j + 1) * ce), ("ee", j * ce, (j + 1) * ce))
+    for w in ("w1", "w2", "w0"):
+        zero_window(w)
+    mset(("w2", 0, HV), 0.0)
+    vcopy(("thf", 0, 1), ("thi", 0, 1))
+    mset(("ed", L, V), 0.0)
+    mset(("newd", 0, V), 0.0)
+    mset(("newd", NONE, WW), 0.0)
+    mset(("zz", 0, 96), 0.0)
+    mset(("neg", 0, 256), 1.0)
+    for k in range(16):
+        asel(blk("bk", k), sq("gm"), G8, A.is_equal, 0.0, -k, 0)
+    asel(sq("up"), sq("gm"), [[1, 128]], A.is_ge, 0.0, 0, -1)
+    asel(sq("lo"), sq("gm"), [[-1, 128]], A.is_gt, 0.0, 0, 1)
+    asel(sq("ith"), sq("ii"), G8, A.is_equal, 0.0, 0, 0)
+    iota(("iotac", 0, V), [[1, V]], 0, 0, True)
+    iota(("newd", V, NONE), [[1, NONE - V]], V + SH - NONE, 0, True)
+    iota(("pi", 0, 96), [[0, 96]], 0, 1)
+    iota(("pb", 0, 96), [[16, 96]], L, 0)
+
+    clip(1, C0, F0)
+    show(2, col("w2", 0, V), "sl", SH)
+    for k in range(16):
+        asel(blk("aka", k), sq("gm"), G8, A.is_gt, -1.0, -k, 0)
+    asel(("akb", 0, 2048), ("aka", 0, 2048), [[0, 16], [-16, 8], [0, 16]], A.is_ge, 0.0, 0, 1)
+    asel(("ak", 0, 2048), ("akb", 0, 2048), [[0, 16], [16, 8], [0, 16]], A.is_ge, 0.0, 15, -1)
+    for d in range(7):
+        vts(("sl5", 8 * d, 8 * d + 4), ("sl", 4 * d, 4 * d + 4), float(HV), A.add)
+        vcopy(("sl5", 8 * d + 4, 8 * d + 8), ("sl", 4 * d, 4 * d + 4))
+        vcopy(("sl6", 8 * d, 8 * d + 4), ("sl", 4 * d, 4 * d + 4))
+    vts(("ed", 0, L), ("ee", 0, L), -float(NONE), A.add)
+    vts(sq("d8k"), sq("ii"), -8192.0, A.mult)
+    vtt(sq("lm"), sq("d8k"), sq("lo"), A.subtract)
+    vts(sq("i2"), sq("ii"), 2.0, A.mult)
+    vtt(sq("tri"), sq("i2"), sq("up"), A.subtract)
+    vts(sq("o32"), sq("gm"), 32.0, A.mult)
+    clip(2, C0, F0)
+    show(3, ("w0", 0, V), "sl", SH)
+    mset(("mka", 0, 2048), -1.0)
+    K3 = [[-1, 16], [0, 8], [1, 16]]
+    asel(("mkb", 0, 2048), ("mka", 0, 2048), K3, A.is_gt, 1.0, 0, 0)
+    asel(("mka", 0, 2048), ("mkb", 0, 2048), K3, A.is_ge, 0.0, 0, 0)
+    asel(("mk", 0, 2048), ("mka", 0, 2048), [[0, 16], [-16, 8], [-1, 16]], A.is_equal, 0.0, 0, 1)
+    emit("v", ("thr", 0, 1), [sq("ith")], lambda e: e.tensor_reduce(ap(("thr", 0, 1)), ap(sq("ith")), AxisListType.X, A.add))
+    vts(("pj", 0, 96), ("pi", 0, 96), 15, A.bitwise_and)
+    vtt(("basec", 0, 96), ("pj", 0, 96), ("pb", 0, 96), A.add)
+    vcopy(("self", 0, 256), ("iotac", L, L + CAP))
+
+    c0 = chunks(C0)
+    H = 1024
+
+    def hook3(i):
+        if i:
+            act(col("w2", c0[i - 1][0], c0[i - 1][1]), ("w1", c0[i - 1][0], c0[i - 1][1]))
+        if i == 3:
+            sel_piece(0, "w1", 0, H)
+
+    clip(3, C0, F3, hook3)
+    show(4, ("w1", 0, V), "sl", SH)
+    act(col("w2", c0[-1][0], c0[-1][1]), ("w1", c0[-1][0], c0[-1][1]))
+    sel_piece(0, "w1", H, L)
+    sel_list(0)
+    vts(("xi", 0, 256), ind(("w1", 0, V), S16), 0.5, A.mult, 0.25, A.add)
+    act(("dd", 0, 256), ind(("ed", 0, V), S16))
+    vcopy(("px", 0, 256), ("xi", 0, 256))
+    vts(("px", 256, 512), ("xi", 0, 256), -256.0, A.add)
+    vcopy(ind(("w2", 0, HV + V), ("sel", 0, 32)), ("px", 0, 512))
+    show(5, ("w2", 0, HV + V), "sl5", 2 * SH)
+    vts(("dl", 0, 256), ("dd", 0, 256), float(NONE), A.add)
+    vcopy(col("w2", L, L + CAP), ("px", 0, 256))
+    split(0, 4)
+
+    def hook5(i):
+        if i == 2:
+            vts(("hb", 0, 448), ind(("newd", 0, V), ("sl", 0, 28)), float(MID - NONE), A.min)
+        if i == 3:
+            for k in range(16):
+                mm(("ps6", 32, 60), blk("bk", k), ("hb", k, 448, 16), k == 0, k == 15)
+            for d in range(7):
+                vts(("sl6", 8 * d + 4, 8 * d + 8), ("ps6", 32 + 4 * d, 36 + 4 * d), 0.0625, A.mult, float(NONE), A.add)
+
+    pointer_pass(5, C5, F5, False, hook5)
+    show(6, ("w0", 0, V), "sl6", 2 * SH)
+    for a, b in chunks(C1):
+        vts(("el", a, b), ("ed", a, b), float(NONE), A.add)
+    vts(("splt", 0, 96), ("of", 0, 96), 256.0, A.is_lt)
+    vcopy(("self", 0, 256), ("iotac", L + CAP, L + 2 * CAP))
+    clip(6, C1, F0)
+    show(7, ("w1", 0, V), "sl6", 2 * SH)
+    zero_window("w0")
+    mset(("w0", 0, L), 0.0)
+
+    def hook7(i):
+        if i == 3:
+            sel_piece(1, "w2", 0, H)
+        if i == 5:
+            sel_piece(1, "w2", H, L)
+
+    clip(7, C1, F7, hook7)
+    show(8, col("w2", 0, V), "sl6", 2 * SH, 0.3)
+    sel_list(1)
+    vcopy(ind(("w0", 0, V), S16), ("neg", 0, 256))
+    mset(("w0", L + CAP, V), 0.0)
+    show(9, ("w0", 0, V), "sl", SH)
+    act(("dd", 0, 256), ind(("ed", 0, V), S16))
+    vts(("dl", 0, 256), ("dd", 0, 256), float(NONE), A.add)
+    vts(("xi", 0, 256), ind(col("w2", 0, V), S16), 0.5, A.mult, 0.25, A.add)
+    vcopy(("px", 0, 256), ("xi", 0, 256))
+    split(1, 8)
+    dma("y", T.yv[:, :], T.w2[:, HV:HV + V], [], [("w2", HV, HV + V)])
+    pointer_pass(9, C9, F9, True)
+
+    for sem in sorted(total):
+        if know["y"].get(sem, 0) < total[sem]:
+            g.sync.wait_ge(T.sem[sem], total[sem])

@@ -2,112 +2,719 @@ from concourse.bass import DstId, RemoteDMATransfer
 from concourse.mybir import AluOpType, AxisListType, ActivationFunctionType
 
 L, CAP, SH, N = 1536, 256, 64, 8
+HL, HC = L // 2, CAP // 2
 V = L + 2 * CAP
 NONE = V + (N - 1) * 2 * SH
 MID = V - 1
+PAD = 16
 WW = NONE + 16
-HV = L + CAP
-OFF = {"w0": 0, "w1": 0, "w2": HV}
+DUM = HL + 2 * HC
+BIG = 4096.0
+MAGIC = 12582912.0
 NG = 5
-NE = 6
-CM = 384
-CQ = 320
+NT = 3
+CM = 256
+PIECE = 32
+RUN = 9
 
-C0 = (384, 384, 304, 208, 128, 80, 48)
-C1 = (384, 384, 384, 288, 176, 112, 64)
-C5 = (256, 320, 320, 320, 256, 192, 128)
-C9 = (256, 320, 320, 320, 320, 256, 192, 64)
-F0 = (0.46,)
-F3 = (0.46, 0.46, 0.46, 0.2, 0.1, 0.3, 0.4)
-F7 = (0.46, 0.46, 0.46, 0.15, 0.3, 0.1, 0.2)
-F5 = (0.42, 0.42, 0.4, 0.3, 0.1, 0.0, 0.0)
-F9 = (0.4, 0.4, 0.4, 0.4, 0.35, 0.2, 0.0, 0.0)
-FW = 0.4
+C0 = ((0, 192), (192, 192), (384, 128), (512, 128), (640, 128))
+C1 = C0 + ((768, 128),)
+C5 = ((0, 256), (256, 256), (512, 128), (640, 128), (768, 128))
+C9 = ((768, 128), (896, 128), (0, 256), (256, 256), (512, 192), (704, 64))
+TAILS = (512, 640)
 
-SCRATCH = {
-    "w0": ("sbuf", [128, WW], "bfloat16"),
-    "w1": ("sbuf", [128, WW], "bfloat16"),
-    "w2": ("sbuf", [128, HV + WW], "bfloat16"),
-    "ee": ("sbuf", [128, L], "int32"),
-    "ed": ("sbuf", [128, V], "float32"),
-    "el": ("sbuf", [128, V], "uint16"),
-    "ec": ("sbuf", [128, V], "float16"),
-    "fe": ("sbuf", [128, V], "bfloat16"),
-    "emp": ("sbuf", [128, 2 * CQ], "bfloat16"),
-    "ti": ("sbuf", [128, 2 * CM], "int32"),
-    "shi": ("sbuf", [128, 28], "int32"),
-    "sl": ("sbuf", [128, 28], "uint16"),
-    "sl2": ("sbuf", [128, 28], "uint16"),
-    "sl5": ("sbuf", [128, 56], "uint16"),
-    "sl6": ("sbuf", [128, 56], "uint16"),
-    "sb0": ("sbuf", [128, 896], "bfloat16"),
-    "sb1": ("sbuf", [128, 896], "bfloat16"),
-    "thi": ("sbuf", [128, 1], "int32"),
-    "thf": ("sbuf", [128, 1], "float32"),
-    "ones": ("sbuf", [128, CM], "bfloat16"),
-    "basec": ("sbuf", [128, 96], "float32"),
-    "zz": ("sbuf", [128, 96], "float32"),
-    "iotac": ("sbuf", [128, V], "float32"),
-    "thr": ("sbuf", [128, 1], "float32"),
-    "cand": ("sbuf", [128, 96], "bfloat16"),
-    "splt": ("sbuf", [128, 96], "bfloat16"),
-    "pfx": ("sbuf", [128, 96], "float32"),
-    "rk": ("sbuf", [128, 96], "float32"),
-    "of": ("sbuf", [128, 96], "float32"),
-    "ofu": ("sbuf", [128, 96], "uint16"),
-    "self": ("sbuf", [128, 2 * L], "float32"),
-    "selh": ("sbuf", [128, 256], "float16"),
-    "sel": ("sbuf", [128, 32], "uint16"),
-    "xi": ("sbuf", [128, 256], "int32"),
-    "px": ("sbuf", [128, 512], "bfloat16"),
-    "neg": ("sbuf", [128, 256], "bfloat16"),
-    "dd": ("sbuf", [128, 256], "float32"),
-    "dl": ("sbuf", [128, 256], "uint16"),
-    "beh": ("sbuf", [128, 256], "float32"),
-    "mm_": ("sbuf", [128, 256], "float32"),
-    "newd": ("sbuf", [128, WW], "float32"),
-    "hb": ("sbuf", [128, 448], "float16"),
-    "tl0": ("sbuf", [128, 32], "uint16"),
-    "tl1": ("sbuf", [128, 32], "uint16"),
-    "yo": ("sbuf", [128, V], "float32"),
-}
-for _n in ("ga", "gm", "ii", "i8", "dc", "up", "tri", "lo", "lm", "o32", "d8k", "i2", "ith"):
-    SCRATCH[_n] = ("sbuf", [128, 128], "bfloat16")
-for _n in ("bk", "mka", "mkb", "mk", "aka", "akb", "ak"):
-    SCRATCH[_n] = ("sbuf", [128, 2048], "bfloat16")
-for _n in ("pi", "pj", "pb"):
-    SCRATCH[_n] = ("sbuf", [128, 96], "int32")
+SCRATCH = {}
+
+
+def _buf(name, cols, dtype, where="sbuf"):
+    SCRATCH[name] = (where, [128, cols], dtype)
+
+
+for _x in "ab":
+    for _n in ("w0", "w1", "w2", "nw", "w9"):
+        _buf(_n + _x, PAD + WW, "bfloat16")
+    for _n, _c, _t in (("xs", V, "bfloat16"), ("ed", V, "float32"), ("el", DUM, "uint16"), ("ec", DUM, "float16"),
+                       ("em", DUM, "bfloat16"), ("he", DUM, "bfloat16"), ("ee", HL, "int32"), ("shi", 28, "int32"), ("sl", 28, "uint16"),
+                       ("sl6", 56, "uint16"), ("sb0", 896, "bfloat16"), ("sb1", 896, "bfloat16"), ("thi", 1, "int32"),
+                       ("thf", 1, "float32"), ("splt", 96, "bfloat16"), ("px", 512, "bfloat16"),
+                       ("s16", 16, "uint16"), ("m16", 16, "uint16"), ("ddn", CAP, "float32"), ("ddz", CAP, "float32"),
+                       ("dn", HC, "float32"), ("dl", HC, "uint16"), ("gw", 16 * HC, "bfloat16"), ("beh", CAP, "bfloat16"),
+                       ("bb", CAP, "float32")):
+        _buf(_n + _x, _c, _t)
+for _n, _c, _t in (("ones", 512, "bfloat16"), ("neg", 512, "bfloat16"), ("basec", 96, "float32"), ("zz", 96, "float32"),
+                   ("iotac", HL + 2 * CAP, "float32"), ("cols", 8, "float32"), ("cand", 96, "bfloat16"), ("pfx", 96, "float32"),
+                   ("rk", 96, "float32"), ("of", 96, "float32"), ("ofu", 48, "uint16"), ("self", 2 * L, "float32"),
+                   ("selh", CAP, "float16"), ("val", 16, "float16"),
+                   ("df", 32, "float16"), ("xi", CAP, "float32"), ("hb", 448, "bfloat16"),
+                   ("qk", 2048, "bfloat16"), ("e8", 512, "bfloat16"), ("cd", 960, "bfloat16"), ("hz", 192, "float32"),
+                   ("i32", 128, "float32"), ("pi", 96, "int32"), ("pj", 96, "int32"), ("pb", 96, "int32"),
+                   ("bk", 2048, "bfloat16"), ("ak", 2048, "bfloat16"), ("mk", 2048, "bfloat16"), ("tk", 1024, "bfloat16")):
+    _buf(_n, _c, _t)
+SQ = ("ga", "gm", "ngm", "ii", "i8", "dc", "mp", "mn", "up", "t4", "lo", "lm", "o32", "d8k", "i4k", "i8k", "ith",
+      "sel0", "sel1", "sw", "pm")
+_buf("mx", 128 * len(SQ), "bfloat16")
 for _k in range(NG):
-    SCRATCH["g%d" % _k] = ("sbuf", [128, 16 * CM], "bfloat16")
-for _k in range(2):
-    for _n, _t in (("f", "bfloat16"), ("ff", "bfloat16"), ("x", "float16"), ("gp", "bfloat16"), ("pr", "float16")):
-        SCRATCH["%s%d" % (_n, _k)] = ("sbuf", [128, CQ], _t)
+    _buf("g%d" % _k, 16 * CM, "bfloat16")
+for _n, _c, _t in (("f", CM, "bfloat16"), ("z", CM, "bfloat16"), ("lq", CM, "float32"), ("x", CM, "float16"), ("gp", CM, "bfloat16"),
+                   ("pr", CM, "bfloat16"), ("tl", 16, "uint16")):
+    _buf(_n, NT * _c, _t)
 for _k in range(8):
-    SCRATCH["ps%d" % _k] = ("psum", [128, 512], "float32")
+    _buf("ps%d" % _k, 512, "float32", "psum")
 
-SEMAPHORES = ["qv", "qs", "qt", "qg"] + ["ar%d" % k for k in range(1, 10)] + ["sn%d" % k for k in range(1, 10)] + ["ld%d" % k for k in range(30)]
+NDMA = 80
+SEMAPHORES = (["qv", "qs", "qt", "qg"] + ["%s%d%s" % (s, k, x) for s in ("ar", "sn") for k in range(1, 10) for x in "ab"]
+              + ["ld%d" % k for k in range(NDMA)])
 
 A = AluOpType
 COPY = ActivationFunctionType.Copy
 IDENT = ActivationFunctionType.Identity
-SIGM = ActivationFunctionType.Sigmoid
+RELU = ActivationFunctionType.Relu
 SEMQ = {"v": "qv", "s": "qs", "t": "qt", "g": "qg"}
+
+CYC, PE, GATH, SCAT, WAKE, AHEAD = 0.85, 0.5, 1.27, 3.2, 150.0, 300.0
+T_WAY, T_ROWS, T_BYTE, T_FIRST, BEHIND = 1200.0, 2000.0, 0.04, 2500.0, 7000.0
+
+
+def size(name):
+    return 2 if SCRATCH[name][2] in ("bfloat16", "float16", "uint16") else 4
+
+
+def width(s):
+    if s[0] == "ind":
+        return 16 * width(s[2])
+    return len(range(s[1], s[2], s[3] if len(s) > 3 else 1))
+
+
+def ranges(s):
+    if s[0] == "ind":
+        return ranges(s[1]) + ranges(s[2])
+    return [(s[0], s[1], s[2]) + (s[4:6] if len(s) == 6 else (0, 128))]
+
+
+def natural(m, u):
+    if m < HL:
+        return HL * u + m
+    r = (m - HL) // HC
+    return L + CAP * r + HC * u + (m - HL - HC * r)
+
+
+def plan():
+    ops, acc, bank, spare = [], {}, {}, [False]
+
+    def add(how, reads, writes, late=None, low=False, grp=None, free=False):
+        i = len(ops)
+        deps = {}
+        for lst, wr in ((reads, False), (writes, True)):
+            for b, a0, a1, p0, p1 in lst:
+                if b[:2] == "ps":
+                    if b in bank and bank[b] != i:
+                        deps.setdefault(bank[b], False)
+                    bank[b] = i
+                    continue
+                if not free:
+                    for c0, c1, q0, q1, kind, j in acc.get(b, ()):
+                        if c0 < a1 and a0 < c1 and q0 < p1 and p0 < q1 and (wr or kind) and j != i:
+                            deps[j] = True
+        for lst, wr in ((writes, True), (reads, False)):
+            for b, a0, a1, p0, p1 in lst:
+                if b[:2] != "ps":
+                    old = acc.get(b, [])
+                    if wr:
+                        old = [e for e in old if not (a0 <= e[0] and e[1] <= a1 and p0 <= e[2] and e[3] <= p1)]
+                    acc[b] = old + [(a0, a1, p0, p1, wr, i)]
+        ops.append({"how": how, "deps": deps, "late": late, "prio": 10 ** 6 if low or spare[0] else i, "grp": grp})
+        return i
+
+    def rw(out, ins):
+        reads = [r for s in ins for r in ranges(s)]
+        if out[0] == "ind":
+            return reads + ranges(out[2]), ranges(out[1])
+        return reads, ranges(out)
+
+    def cost(q, out, ins, tt=False):
+        n = width(out)
+        if out[0] == "ind":
+            return 50 + n * SCAT
+        if ins and ins[0][0] == "ind":
+            return (65 if q == "s" else 50) + n * GATH
+        full = [s for s in [out] + ins if width(s) == n]
+        if q == "s":
+            k = 1.0
+        elif tt:
+            k = 1.0 if any(s[0][:2] == "ps" for s in ins) else 2.0
+        else:
+            k = 0.5 if all(size(s[0]) == 2 for s in full) else 1.0
+        return max(64, n * k) * CYC
+
+    def one(q, out, ins, call, tt=False, low=False):
+        r, w = rw(out, ins)
+        return add({q: (cost(q, out, ins, tt), [call])}, r, w, low=low)
+
+    def either(out, ins, vcall, scall, grp=None):
+        r, w = rw(out, ins)
+        return add({"v": (cost("v", out, ins), [vcall]), "s": (cost("s", out, ins), [scall])}, r, w, grp=grp)
+
+    def ind(win, off):
+        return ("ind", win, off)
+
+    def tiles(*xs):
+        return [x for x in xs if isinstance(x, tuple)]
+
+    def vcopy(o, i):
+        one("v", o, [i], ("copy", o, i))
+
+    def copy(o, i, bias=0.0, grp=None):
+        if bias == 0.0:
+            either(o, [i], ("copy", o, i), ("act", o, i, COPY, 0.0), grp)
+        else:
+            either(o, [i] + tiles(bias), ("ts", o, i, bias, None, A.add, None), ("act", o, i, IDENT, bias), grp)
+
+    def vtt(o, i0, i1, op):
+        one("v", o, [i0, i1], ("tt", o, i0, i1, op), True)
+
+    def vts(o, i0, s1, op0, s2=None, op1=None):
+        one("v", o, [i0] + tiles(s1, s2), ("ts", o, i0, s1, s2, op0, op1))
+
+    def mset(o, c):
+        if not spare[0]:
+            one("v", o, [], ("set", o, c))
+            return
+        for a in range(o[1], o[2], 512):
+            p = (o[0], a, min(a + 512, o[2]))
+            src = ("ones", 0, width(p))
+            if cost("s", p, []) > cost("v", p, []):
+                one("v", p, [], ("set", p, c))
+            else:
+                add({"v": (cost("v", p, []), [("set", p, c)]), "s": (cost("s", p, []), [("act", p, src, IDENT, c, 0.0)])},
+                    ranges(src), ranges(p))
+
+    def scaled(o, i, c):
+        either(o, [i] + tiles(c), ("ts", o, i, c, None, A.mult, None), ("act", o, i, IDENT, 0.0, c))
+
+    def state(b, a, w):
+        return (b, a + (0 if a < HL else 2 * CAP), a + w + (0 if a < HL else 2 * CAP))
+
+    def mms(lst):
+        if len(lst) > RUN and width(lst[0][2]) > 96:
+            for n in range(0, len(lst), RUN):
+                mms(lst[n:n + RUN])
+            return
+        r, w, t = [], [], 0.0
+        for o, l, rh, st, sp in lst:
+            r += ranges(l) + ranges(rh)
+            w += ranges(o)
+            t += max(64, width(rh)) * PE * (4 if size(l[0]) == 4 else 1)
+        add({"t": (t, [("mm",) + m for m in lst])}, r, w)
+
+    def mm(o, l, r, start=True, stop=True):
+        mms([(o, l, r, start, stop)])
+
+    def asel(o, i, pat, op, fill, base, cm, low=True):
+        add({"g": (190 + 2 * width(o) * CYC, [("asel", o, i, pat, op, fill, base, cm)])}, ranges(i), ranges(o), low=low)
+
+    def iota(o, pat, base, cm, low=True):
+        add({"g": (150 + 2 * width(o) * CYC, [("iota", o, pat, base, cm)])}, [], ranges(o), low=low)
+
+    ndma = [0]
+
+    def dma(pairs, q="y"):
+        r = [x for o, i in pairs if i[0] != "hbm" for x in ranges(i)]
+        w = [x for o, i in pairs if o[0] != "hbm" for x in ranges(o)]
+        sem = "ld%d" % ndma[0]
+        ndma[0] += 1
+        n = sum(width(i if o[0] == "hbm" else o) * size((i if o[0] == "hbm" else o)[0]) for o, i in pairs)
+        add({q: (60.0 * len(pairs), [("dma", o, i) for o, i in pairs])}, r, w, late=(sem, 16 * len(pairs), T_WAY, 120.0 * len(pairs) + 0.16 * n))
+
+    def wb(x, k):
+        return "w9" + x if k == 9 else "w%d%s" % (k % 3, x)
+
+    def col(w, a, b, *rest):
+        return (w, PAD + a, PAD + b) + rest
+
+    def part(s, u):
+        return s[:3] + (1, 64 * u, 64 * u + 64)
+
+    def blk(m, i):
+        return (m, 128 * i, 128 * i + 128)
+
+    def sq(m):
+        return blk("mx", SQ.index(m))
+
+    def show(x, k, lst, wd, top=V):
+        n = 7 * wd
+        sb = "sb%d%s" % (k % 2, x)
+        win = col(wb(x, k), 0, top)
+        if k == 9:
+            vtt((sb, 0, n), ind(win, (lst, 0, n // 16)), ("cd", 512, 960), A.min)
+        else:
+            h = n // 64 * 2
+            copy((sb, 0, h * 16), ind(win, (lst, 0, h)))
+            copy((sb, h * 16, n), ind(win, (lst, h, n // 16)))
+        first = T_FIRST if (x, k) == ("a", 1) else 0.0
+        land = [col(wb(x, k), V + d * 2 * SH, V + d * 2 * SH + wd) for d in range(N - 1)]
+        i = add({"g": (300.0 + first, [("far", x, k, sb, wd, land)])}, ranges((sb, 0, n)), [],
+                late=("sn%d%s" % (k, x), 7, first + T_WAY, T_ROWS + T_BYTE * 256 * wd))
+        j = add({}, [], [r for s in land for r in ranges(s)], late=("ar%d%s" % (k, x), 7), free=True)
+        ops[j]["with"] = i
+
+    gi, si = [0], [0]
+
+    def gather(x, k, a, w):
+        G = "g%d" % (gi[0] % NG)
+        gi[0] += 1
+        win = col(wb(x, k), 0, WW)
+        for p in range(0, w, PIECE):
+            q = min(p + PIECE, w)
+            copy((G, 16 * p, 16 * q), ind(win, ("el" + x, a + p, a + q)), grp=gi[0])
+        return G
+
+    def over_slots(ps, m, G, w, start=True, stop=True):
+        return [(ps, sq(m) if m == "i8" else blk(m, i), (G, i, 16 * w, 16), start and i == 0, stop and i == 15) for i in range(16)]
+
+    def rounding(ps, w):
+        return [(ps, sq("mp"), ("ones", 0, w), False, False), (ps, sq("mn"), ("ones", 0, w), False, True)]
+
+    def spread(x, ks, a, w):
+        TAIL = TAILS[ks[0] > 5]
+        if a >= TAIL:
+            mms([(("ps7", w * u, w * u + w), sq("sel%d" % u), state("xs" + x, a, w), True, True) for u in range(2)])
+            for u in range(2):
+                copy(col(wb(x, ks[0]), natural(a, u), natural(a, u) + w), ("ps7", w * u, w * u + w))
+        for k, top in zip(ks, (TAIL, HL)):
+            if top == a + w:
+                dma([(part(col(wb(x, k), HL * u, HL * u + top), h), part(("xs" + x, 0, top), u)) for u in range(2) for h in range(2)])
+
+    def clip(x, k, chunks, ks):
+        for n, (a, w) in enumerate(chunks):
+            G = gather(x, k, a, w)
+            ps = ("ps%d" % (si[0] % 4), 0, w)
+            si[0] += 1
+            mms([(ps, sq("dc"), ("ones", 0, w), True, False)] + over_slots(ps, "i8", G, w, False, False) + rounding(ps, w))
+            vtt(state("xs" + x, a, w), ps, state("xs" + x, a, w), A.min)
+            spread(x, ks, a, w)
+
+    def select(x, r, k):
+        w, ps = wb(x, k), "ps5" if x == "a" else "ps6"
+        copy(("self", 0, CAP), ("iotac", HL + CAP * r, HL + CAP * r + CAP))
+        mms([((ps, 0, 96), blk("bk", i), col(w, i, L, 16), i == 0, i == 15 and r == 0) for i in range(16)]
+            + ([((ps, 0, 96), sq("d8k"), ("splt" + x, 0, 96), False, True)] if r else []))
+        vts(("cand", 0, 96), (ps, 0, 96), ("thf" + x, 0, 1), A.is_ge)
+        mms([((ps, 96, 192), sq("gm"), ("cand", 0, 96), True, True), ((ps, 192, 288), sq("lm"), ("cand", 0, 96), True, True)])
+        one("v", ("pfx", 0, 96), [(ps, 96, 192), ("zz", 0, 96)], ("scan", ("pfx", 0, 96), (ps, 96, 192), ("zz", 0, 96), 8191.0))
+        vtt(("rk", 0, 96), (ps, 192, 288), ("pfx", 0, 96), A.add)
+        vtt(("of", 0, 96), ("rk", 0, 96), ("basec", 0, 96), A.min)
+        for u in range(2):
+            vcopy(part(("ofu", 0, 48), u), part(("of", 48 * u, 48 * u + 48), u))
+        vcopy(ind(("self", 0, 2 * L), ("ofu", 0, 48)), ("iotac", 0, HL))
+        vcopy(("selh", 0, CAP), ("self", 0, CAP))
+        mms([((ps, 288, 304), blk("bk", i), ("selh", i, CAP, 16), i == 0, i == 15) for i in range(16)])
+        vts(("val", 0, 16), (ps, 288, 304), 0.0625, A.mult)
+        vts(("m16" + x, 0, 16), (ps, 288, 304), 0.0625, A.mult, ("cols", 6, 7), A.subtract)
+        mms([((ps, 304, 320), sq("sw"), ("val", 0, 16), True, False), ((ps, 304, 320), sq("ii"), ("df", 16 * r, 16 * r + 16), False, True)])
+        vcopy(("s16" + x, 0, 16), (ps, 304, 320))
+        if r == 0:
+            vts(("splt" + x, 0, 96), ("of", 0, 96), float(CAP), A.is_lt)
+
+    def split(x, r, k):
+        w, ps = wb(x, k), "ps5" if x == "a" else "ps6"
+        S16, M16, px = ("s16" + x, 0, 16), ("m16" + x, 0, 16), ("px" + x, 0, CAP)
+        h0, m0 = L + CAP * r, HL + 2 * CAP + HC * r
+        ed = "ed" + x
+        codes = col(("nw" if r == 0 else "w9") + x, 0, V)
+        xi, hb, b7 = ("xi", 0, CAP), ("hb", 0, 448), ("cols", 7, 8)
+
+        def halved():
+            src = ind(col(w, 0, V), S16)
+            either(xi, [src], ("ts", xi, src, 0.5, 0.25, A.mult, A.add), ("act", xi, src, IDENT, 0.25, 0.5))
+            vts(px, xi, MAGIC, A.add, -MAGIC, A.add)
+
+        copy(("ddz" + x, 0, CAP), ind((ed, 0, V), M16), -float(NONE))
+        vcopy(ind(codes, S16), ("cd", CAP * r, CAP * r + CAP))
+        mms([((ps, 352, 480), ("hz", 64 - 64 * u, 192 - 64 * u), ("ddz" + x, HC * u, HC * u + HC), u == 0, u == 1) for u in range(2)])
+        vts(("dl" + x, 0, HC), (ps, 352, 480), float(NONE), A.add)
+        copy(("dn" + x, 0, HC), (ps, 352, 480), float(NONE))
+        if r:
+            mset(col("w9" + x, h0, V), 0.0)
+            show(x, 9, ("sl" + x), SH)
+        else:
+            w5 = wb(x, k + 1)
+            src = ind(codes, ("sl" + x, 0, 28))
+            either(hb, [src, b7], ("ts", hb, src, b7, 0.0, A.add, A.max), ("act", hb, src, RELU, b7))
+            halved()
+            vts(("px" + x, CAP, 2 * CAP), xi, MAGIC, A.add, -MAGIC - 256.0, A.add)
+            mms([((ps, 320, 348), blk("bk", i), ("hb", i, 448, 16), i == 0, i == 15) for i in range(16)])
+            vcopy(ind(col(w5, 0, V), S16), ("px" + x, CAP, 2 * CAP))
+            copy(col(w5, h0, h0 + CAP), px)
+            for c in range(4):
+                vts(("sl6" + x, 4 + c, 56, 8), (ps, 320 + c, 348, 4), -0.25, A.mult, float(MID), A.add)
+            show(x, 5, "sl6" + x, 2 * SH)
+        gi[0] += NG
+        for p in range(0, HC, 32):
+            copy(("gw" + x, 16 * p, 16 * p + 512), ind(col(w, 0, WW), ("dl" + x, p, p + 32)), grp=gi[0])
+        copy(("ddn" + x, 0, CAP), ind((ed, 0, V), M16))
+        mms(over_slots((ps, 0, HC), "ak", "gw" + x, HC))
+        vts(("beh" + x, 0, HC), (ps, 0, HC), ("cols", 0, 1), A.is_ge, float(NONE), A.mult)
+        vts(("beh" + x, HC, CAP), (ps, 0, HC), ("cols", 0, 1), A.is_lt, float(NONE), A.mult)
+        mms([((ps, HC + HC * u, CAP + HC * u), sq("sel%d" % u), ("beh" + x, 0, HC), True, True) for u in range(2)])
+        vtt((ed, m0, m0 + HC), ("dn" + x, 0, HC), ("beh" + x, HC, CAP), A.max)
+        copy(("bb" + x, 0, CAP), (ps, HC, HC + CAP))
+        vtt(ind((ed, 0, V), M16), ("ddn" + x, 0, CAP), ("bb" + x, 0, CAP), A.max)
+        lists(x, r, C5 if r == 0 else C9)
+        if r:
+            halved()
+        vcopy(ind(("xs" + x, 0, V), M16), px)
+        for u in range(2):
+            copy(part(("xs" + x, m0, m0 + HC), u), part(("px" + x, HC * u, HC * u + HC), u))
+
+    pi = [0]
+
+    def lists(x, r, chunks):
+        for a, w in ((0, 256), (256, 512), (HL, HC + HC * r))[::1 - 2 * r]:
+            vcopy(("el" + x, a, a + w), state("ed" + x, a, w))
+        for a, w in ((0, 384), (384, 512 + HC * r)):
+            el, ec, em, he = [(b + x, a, a + w) for b in ("el", "ec", "em", "he")]
+            vts(em, el, float(NONE), A.is_equal, -1.0, A.mult)
+            if r == 0:
+                ps = ("ps5" if x == "a" else "ps6", 0, w)
+                vts(ec, el, float(MID), A.subtract)
+                mm(ps, sq("gm"), em)
+                vts(he, ps, -1.0, A.is_le, -2.0, A.add)
+
+    def pointer_clip(x, k, chunks):
+        for n, (a, w) in enumerate(chunks):
+            p = pi[0] % NT
+            el, ec, em, he = [(b + x, a, a + w) for b in ("el", "ec", "em", "he")]
+            ed, xs = state("ed" + x, a, w), state("xs" + x, a, w)
+            f, z, lo, xx, gp, pr = [(b, CM * p, CM * p + w) for b in ("f", "z", "lq", "x", "gp", "pr")]
+            tl = ("tl", 16 * p, 16 * p + w // 16)
+            ps, pq = ("ps2", 0, w), ("ps%d" % (pi[0] % 2), 0, w)
+            pi[0] += 1
+            G = gather(x, k, a, w)
+            mms(over_slots(pq, "qk", G, w))
+            vts(f, pq, -1024.0, A.is_lt)
+            vts(z, pq, 2048 * MAGIC, A.add, -2048 * MAGIC, A.add)
+            vtt(lo, pq, z, A.subtract)
+            mms([(("ps3", 0, w), sq("ii"), ec, True, False), (("ps3", 0, w), sq("i4k"), he, False, False),
+                 (("ps3", 0, w), sq("t4"), f, False, True)])
+            vts(xx, ("ps3", 0, w), -2048.0, A.max)
+            mms([(("ps4", 0, w // 16), blk("bk", i), ("x", xx[1] + i, xx[2], 16), i == 0, i == 15) for i in range(16)])
+            vts(tl, ("ps4", 0, w // 16), float(15 * 2048 + MID + PAD), A.add)
+            copy(gp, ind((wb(x, k), 0, PAD + WW), tl), 252.5)
+            copy(pr, ind(("nw" + x, 0, PAD + WW), tl), ("cols", 1, 2))
+            mms([(ps, ("i32", 0, 128), lo, True, False), (ps, sq("o32"), f, False, False), (ps, sq("i8"), gp, False, False)]
+                + rounding(ps, w))
+            vtt(xs, ps, xs, A.min)
+            mms([(("ps7", 0, w), sq("t4"), em, True, False), (("ps7", 0, w), sq("pm"), pr, False, True)])
+            vtt(ed, ("ps7", 0, w), ed, A.min)
+            spread(x, [k + 1], a, w)
+            vcopy(el, ed)
+
+    def pointer_last(x, chunks):
+        row = 64 * "ab".index(x)
+        for a, w in chunks:
+            p = pi[0] % 2
+            pi[0] += 1
+            em, ed = ("em" + x, a, a + w), state("ed" + x, a, w)
+            xx = ("x", CM * p, CM * p + w)
+            ps, pt = ("ps%d" % p, 0, w), ("ps%d" % (2 + p), 0, w)
+            G = gather(x, 9, a, w)
+            mms(over_slots(ps, "mk", G, w))
+            vts(xx, ps, 0.0, A.max, -(NONE + BIG) / 16, A.add)
+            mms([(pt, sq("t4"), em, True, False), (pt, sq("ngm"), xx, False, True)])
+            vtt(ed, pt, ed, A.min)
+            dma([(("hbm", "ye", (row, row + 64), (natural(a, u), natural(a, u) + w)), part(ed, u)) for u in range(2)])
+
+    for n, x in enumerate("ab"):
+        rows = (64 * n, 64 * n + 64)
+        dma([(part(("shi" + x, 0, 28), u), ("hbm", "sh", rows, (0, 28))) for u in range(2)])
+        dma([(part(col(wb(x, 1), 0, L), 0), ("hbm", "v0", rows, (0, L)))])
+        dma([(part(col(wb(x, 1), 0, L), 1), ("hbm", "v0", rows, (0, L)))], "s" if n == 0 else "y")
+        dma([(part(("ee" + x, 0, HL), u), ("hbm", "e", rows, (HL * u, HL * u + HL))) for u in range(2)])
+        dma([(part(("xs" + x, 0, HL), u), ("hbm", "v0", rows, (HL * u, HL * u + HL))) for u in range(2)])
+    for n, x in enumerate("ab"):
+        dma([(part(("thi" + x, 0, 1), u), ("hbm", "th", (64 * n, 64 * n + 64), (0, 1))) for u in range(2)])
+
+    G8 = [[0, 8], [1, 16]]
+    o128 = ("ones", 0, 128)
+
+    def zero_window(w):
+        mset(col(w, L, V), 0.0)
+        mset(col(w, NONE, WW), 0.0)
+        for d in range(N - 1):
+            b = V + d * 2 * SH + SH
+            mset(col(w, b, b + SH), 0.0)
+
+    mset(("ones", 0, 512), 1.0)
+    asel(sq("ii"), o128, [[-1, 128]], A.is_equal, 0.0, 0, 1, False)
+    for u in range(2):
+        asel(sq("sel%d" % u), o128, [[0, 2], [-1, 64]], A.is_equal, 0.0, -64 * u, 1, False)
+    asel(sq("ga"), o128, [[-16, 8], [0, 16]], A.is_ge, 0.0, 0, 1, False)
+    asel(sq("gm"), sq("ga"), [[16, 8], [0, 16]], A.is_ge, 0.0, 15, -1, False)
+    for x in "ab":
+        vcopy(("sl" + x, 0, 28), ("shi" + x, 0, 28))
+        show(x, 1, "sl" + x, SH, L)
+    for n, c in (("i8", 0.125), ("dc", -0.4375), ("mp", MAGIC), ("mn", -MAGIC), ("d8k", -8192.0), ("i4k", BIG), ("i8k", 2 * BIG)):
+        scaled(sq(n), sq("ii"), c)
+    spare[0] = True
+    copy(("i32", 0, 128), sq("ii"))
+    for x in "ab":
+        vcopy(("el" + x, 0, HL), ("ee" + x, 0, HL))
+        for k in (1, 2, 3):
+            zero_window(wb(x, k))
+    spare[0] = False
+    for k in range(16):
+        asel(blk("bk", k), sq("gm"), G8, A.is_equal, 0.0, -k, 0)
+    asel(sq("up"), sq("gm"), [[1, 128]], A.is_ge, 0.0, 0, -1)
+    asel(sq("lo"), sq("gm"), [[-1, 128]], A.is_gt, 0.0, 0, 1)
+    asel(sq("ith"), sq("ii"), G8, A.is_equal, 0.0, 0, 0)
+    for a in (0, HL // 2):
+        iota(("iotac", a, a + HL // 2), [[1, HL // 2]], a, 0)
+    iota(("iotac", HL, HL + 2 * CAP), [[1, 2 * CAP]], L, 0)
+    iota(("pi", 0, 96), [[0, 96]], 0, 1)
+    iota(("pb", 0, 96), [[16, 96]], L, 0)
+    iota(("self", 0, 512), [[-272, 2], [-16, 16], [0, 16]], 1392, 0)
+    iota(("self", 512, 960), [[-128, 7], [-16, 4], [0, 16]], 816, 0)
+    iota(("self", 1024, 1536), [[16, 2], [0, 16], [-1, 16]], 16, 0)
+    iota(("self", 1536, 1984), [[0, 28], [-1, 16]], 16, 0)
+    mset(("hz", 0, 192), 0.0)
+    i0 = sq("ii")[1]
+    vtt(("hz", 64, 128), ("mx", i0, i0 + 64), ("mx", i0 + 64, i0 + 128), A.add)
+    mset(("neg", 0, 512), -512.0)
+
+    def by_slot(m, src, steps):
+        for a in range(0, 2048, 512):
+            t0, t1, out = ("tk", 0, 512), ("tk", 512, 1024), (m, a, a + 512)
+            cur = src
+            for op, fill in steps:
+                nxt = t1 if cur == t0 else t0
+                asel(nxt, cur, [[-1, 4], [0, 8], [1, 16]], op, fill, -(a // 128), 0)
+                cur = nxt
+            nxt = t1 if cur == t0 else t0
+            asel(nxt, cur, [[0, 4], [-16, 8], [0, 16]], A.is_ge, 0.0, 0, 1)
+            asel(out, nxt, [[0, 4], [16, 8], [0, 16]], A.is_ge, 0.0, 15, -1)
+
+    by_slot("ak", ("ones", 0, 512), [(A.is_gt, -1.0)])
+    mset(("e8", 0, 512), 0.125)
+    for a in range(0, 2048, 512):
+        asel(("tk", 0, 512), ("e8", 0, 512), [[0, 4], [-1, 128]], A.is_equal, 0.0, 0, 1)
+        asel(("qk", a, a + 512), ("tk", 0, 512), [[-255, 4], [-16, 8], [256, 16]], A.not_equal, 2048.0, -15 - 255 * (a // 128), 1)
+    by_slot("mk", ("neg", 0, 512), [(A.is_gt, 0.25), (A.is_ge, 0.0)])
+
+    def more_constants():
+        vtt(sq("lm"), sq("d8k"), sq("lo"), A.subtract)
+        vts(sq("t4"), sq("up"), -BIG, A.mult)
+        vtt(sq("t4"), sq("t4"), sq("i8k"), A.add)
+        vts(sq("o32"), sq("gm"), 32.0, A.mult)
+        vts(sq("ngm"), sq("gm"), -1.0, A.mult)
+        vtt(sq("sw"), sq("sel0"), sq("sel1"), A.add)
+        one("v", ("cols", 0, 1), [sq("ith")], ("sum", ("cols", 0, 1), sq("ith")))
+        vts(("pj", 0, 96), ("pi", 0, 96), 15, A.bitwise_and)
+        vtt(("basec", 0, 96), ("pj", 0, 96), ("pb", 0, 96), A.add)
+        mset(("zz", 0, 96), 0.0)
+        r16 = ("pj", 0, 1)
+        vts(("cols", 1, 2), r16, 8.0, A.is_ge, (NONE + BIG) / 16, A.mult)
+        vts(("cols", 2, 3), r16, 4.0, A.is_lt)
+        vts(("cols", 3, 4), r16, 8.0, A.is_lt)
+        vtt(("cols", 4, 5), ("cols", 3, 4), ("cols", 2, 3), A.subtract)
+        vts(("cols", 5, 6), ("cols", 3, 4), -2.25, A.mult, 2.0, A.add)
+        vts(("cols", 6, 7), ("pi", 0, 1), 64.0, A.is_ge, float(HL), A.mult)
+        vts(("cols", 7, 8), ("cols", 2, 3), -895.0, A.mult, -1.0, A.add)
+        vts(sq("pm"), sq("gm"), ("cols", 5, 6), A.mult)
+        for a in range(0, 960, 320):
+            hi, lo = ("self", a, a + 320), ("self", 1024 + a, 1344 + a)
+            scaled(hi, hi, ("cols", 2, 3))
+            scaled(lo, lo, ("cols", 4, 5))
+            vtt(("cd", a, a + 320), hi, lo, A.add)
+        vts(("df", 0, 32), ("basec", 0, 32), -1.0, A.mult)
+        copy(("iotac", 0, HL), ("iotac", 0, HL), ("cols", 6, 7))
+
+    def tables(x):
+        vcopy(("ed" + x, 0, HL), ("ee" + x, 0, HL))
+        mset(("ed" + x, HL, V), float(NONE))
+        vcopy(("thf" + x, 0, 1), ("thi" + x, 0, 1))
+        mset((wb(x, 5), 0, PAD), -256.0)
+        mset(("nw" + x, 0, PAD + WW), 0.0)
+        for d in range(N - 1):
+            copy(col("nw" + x, V + 2 * SH * d, V + 2 * SH * d + SH), ("cd", 512 + SH * d, 512 + SH * d + SH))
+        for c in range(4):
+            vcopy(("sl6" + x, c, 56, 8), ("sl" + x, c, 28, 4))
+
+    def step(x, k):
+        if k == 5:
+            pointer_clip(x, 5, C5)
+        else:
+            clip(x, k, C0 if k < 4 else C1, [4, 5] if k == 3 else [k + 1])
+        show(x, k + 1, ("sl" if k < 4 else "sl6") + x, SH if k < 4 else 2 * SH, L if k < 4 else V)
+
+    spare[0] = True
+    more_constants()
+    for x in "ab":
+        tables(x)
+        zero_window("w9" + x)
+        mset(col("w9" + x, 0, L), 0.0)
+    spare[0] = False
+    for k in (1, 2, 3, 5, 6, 7):
+        for x in "ab":
+            step(x, k)
+            if k in (3, 7):
+                select(x, k // 4, k + 1)
+                split(x, k // 4, k + 1)
+            if k == 7:
+                row = 64 * "ab".index(x)
+                dma([(("hbm", "yv", (row, row + 64), (natural(a, u), natural(a, u) + w)), part(state("xs" + x, a, w), u))
+                     for a, w in ((0, HL), (HL, HC), (HL + HC, HC)) for u in range(2)])
+    for x in "ab":
+        pointer_last(x, C9)
+    for o in reversed(ops):
+        for j in o["deps"]:
+            if ops[j]["prio"] > len(ops):
+                ops[j]["need"] = min(ops[j].get("need", 10 ** 6), o.get("need", o["prio"]))
+    for o in ops:
+        o["prio"] = o.get("need", o["prio"])
+    return ops
+
+
+def arrange(ops):
+    n = len(ops)
+    after = [[] for _ in range(n)]
+    left = [0] * n
+    for i, o in enumerate(ops):
+        pre = set(o["deps"]) | ({o["with"]} if "with" in o else set())
+        left[i] = len(pre)
+        for j in pre:
+            after[j].append(i)
+    ready = [0.0] * n
+    end = [0.0] * n
+    free = {q: 0.0 for q in "vstgy"}
+    pool = {q: set() for q in free}
+    todo = {q: sum(q in o["how"] for o in ops) for q in free}
+    order, rows, sent = [], [0.0], [-1500.0]
+
+    def release(i):
+        o = ops[i]
+        if not o["how"]:
+            finish(i, None, ops[o["with"]]["start"])
+            return
+        ready[i] = max([0.0] + [end[j] + (WAKE if hard or ops[j]["q"] not in o["how"] else 0.0) for j, hard in o["deps"].items()])
+        for q in o["how"]:
+            pool[q].add(i)
+
+    def finish(i, q, t):
+        o = ops[i]
+        o["q"], o["start"] = q, t
+        busy = o["how"][q][0] if q else 0.0
+        if not q:
+            end[i] = end[o["with"]] + T_WAY
+        elif o["late"]:
+            rows[0] = max(rows[0], t + o["late"][2]) + o["late"][3]
+            end[i] = rows[0] + (0.0 if q == "g" else T_WAY)
+        else:
+            end[i] = t + busy
+        if q == "g" and o["late"]:
+            sent[0] = t + busy
+        if q:
+            free[q] = t + busy
+            for p in o["how"]:
+                pool[p].discard(i)
+                todo[p] -= 1
+        order.append(i)
+        for j in after[i]:
+            left[j] -= 1
+            if left[j] == 0:
+                release(j)
+
+    for i in [i for i in range(n) if left[i] == 0]:
+        release(i)
+    while any(todo.values()):
+        q = min((p for p in free if todo[p]), key=lambda p: (free[p], not pool[p]))
+        t = free[q]
+        now = [i for i in pool[q] if ready[i] <= t]
+        if q == "g":
+            now = [i for i in now if ops[i]["late"] or t + ops[i]["how"][q][0] <= sent[0] + BEHIND or t > sent[0] + 4 * BEHIND]
+        if not now:
+            free[q] = min([ready[i] for i in pool[q] if ready[i] > t] + [free[p] for p in free if free[p] > t and todo[p]] + [t + 200.0])
+            continue
+        best = min(now, key=lambda i: ops[i]["prio"])
+        soon = [i for i in pool[q] if t < ready[i] <= t + AHEAD and len(ops[i]["how"]) == 1 and ops[i]["prio"] < ops[best]["prio"]]
+        if soon and ops[best]["how"][q][0] > AHEAD:
+            best = min(soon, key=lambda i: ready[i])
+            t = ready[best]
+        elif q == "s" and ops[best]["grp"] is not None:
+            best = max(i for i in now if ops[i]["grp"] == ops[best]["grp"])
+        finish(best, q, t)
+    order.sort(key=lambda i: ops[i]["start"])
+    return order, max(end)
+
+
+PLAN = []
 
 
 def rank_program(g, core, T, topo):
     rank = T.rank_of(core)
     if rank is None:
         return
+    if not PLAN:
+        ops_ = plan()
+        PLAN.extend([ops_, arrange(ops_)[0]])
+    ops, order = PLAN
     eng = {"v": g.vector, "s": g.scalar, "t": g.tensor, "g": g, "y": g.sync}
 
-    cnt = {"qv": 0, "qs": 0, "qt": 0, "qg": 0}
-    know = {q: {} for q in eng}
-    acc = {}
-    total = {}
-    ndma = [0]
+    def ap(s):
+        if not isinstance(s, tuple):
+            return s
+        if s[0] == "ind":
+            return ap(s[1]).indirect(ap(s[2]))
+        if s[0] == "hbm":
+            return T[s[1]][s[2][0]:s[2][1], s[3][0]:s[3][1]]
+        if len(s) == 6:
+            return T[s[0]][s[4]:s[5], s[1]:s[2]]
+        if len(s) == 4:
+            return T[s[0]][:, s[1]:s[2]:s[3]]
+        return T[s[0]][:, s[1]:s[2]]
 
-    def need(q, tok):
-        sem, val, snap = tok
+    def far(x, k, sb, wd, land):
+        tr = []
+        for d in range(1, N):
+            dst = T.cores[(rank + d) % N]
+            a = topo.addr(dst)
+            tr.append(RemoteDMATransfer(dst_ids=[DstId(rid=a[0], pnc=a[1])], dma_engine_mask=1 << topo.engines(core, dst)[d - 1],
+                                        remote_sem=T.sem["ar%d%s" % (k, x)], src=T[sb][:, (d - 1) * wd:d * wd], dst=ap(land[d - 1])))
+        g.remote_dma_fused(tr, local_sem=T.sem["sn%d%s" % (k, x)])
+
+    def issue(e, c):
+        k, a = c[0], [ap(s) for s in c[1:]]
+        if k == "copy":
+            return e.tensor_copy(a[0], a[1])
+        if k == "tt":
+            return e.tensor_tensor(a[0], a[1], a[2], a[3])
+        if k == "ts":
+            return e.tensor_scalar(*(a[:5] if a[5] is None else a))
+        if k == "set":
+            return e.memset(a[0], a[1])
+        if k == "act":
+            return e.activation(a[0], a[1], a[2]) if a[2] == COPY else e.activation(*(a + [1.0])[:5])
+        if k == "mm":
+            return e.matmul(*a)
+        if k == "scan":
+            return e.tensor_tensor_scan(a[0], a[1], a[2], a[3], A.add, A.add)
+        if k == "sum":
+            return e.tensor_reduce(a[0], a[1], AxisListType.X, A.add)
+        if k == "asel":
+            return e.affine_select(*a)
+        if k == "iota":
+            if SCRATCH[c[1][0]][2] == "int32":
+                return e.iota(*a)
+            return e.iota(*a, allow_small_or_imprecise_dtypes=True)
+        return e.dma_start(a[0], a[1])
+
+    queue = {q: [i for i in order if ops[i]["q"] == q] for q in eng}
+    place = {i: n for q in queue for n, i in enumerate(queue[q])}
+    cnt = {q: 0 for q in SEMQ}
+    know = {q: {} for q in eng}
+    tok, total = {}, {}
+
+    def need(q, t):
+        sem, val, snap = t
         if know[q].get(sem, 0) >= val:
             return
         eng[q].wait_ge(T.sem[sem], val)
@@ -116,504 +723,47 @@ def rank_program(g, core, T, topo):
                 know[q][s_] = v_
         know[q][sem] = val
 
-    def deps(q, reads, writes):
+    for i in order:
+        o = ops[i]
+        q = o["q"]
+        if i in tok:
+            continue
+        if q is None:
+            tok[i] = (o["late"][0], o["late"][1], {})
+            total[o["late"][0]] = o["late"][1]
+            continue
+        run, calls = [i], o["how"][q][1]
+        if o["grp"] is not None:
+            for j in queue[q][place[i] + 1:]:
+                if ops[j]["grp"] != o["grp"] or abs(j - run[-1]) != 1 or j in run or not all(d in tok for d in ops[j]["deps"]):
+                    break
+                run.append(j)
+            lo, hi = ops[min(run)]["how"][q][1][0], ops[max(run)]["how"][q][1][0]
+            calls = [(lo[0], lo[1][:2] + hi[1][2:], lo[2][:2] + (lo[2][2][:2] + hi[2][2][2:],)) + lo[3:]]
         best = {}
-        for lst, wr in ((reads, False), (writes, True)):
-            for b, a0, a1 in lst:
-                ps = b[:2] == "ps"
-                for (c0, c1, kind, tok, q2) in acc.get(b, ()):
-                    if ps:
-                        if q2 == q and (q == "t" or not (wr or kind)):
-                            continue
-                        if q2 == q and (c0 >= a1 or a0 >= c1):
-                            continue
-                    elif c0 >= a1 or a0 >= c1 or not (wr or kind):
-                        continue
-                    if tok[0] not in best or best[tok[0]][1] < tok[1]:
-                        best[tok[0]] = tok
+        for j in run:
+            for d, hard in ops[j]["deps"].items():
+                if (hard or ops[d]["q"] != q) and (tok[d][0] not in best or best[tok[d][0]][1] < tok[d][1]):
+                    best[tok[d][0]] = tok[d]
         for t in sorted(best.values(), key=lambda t: -len(t[2])):
             need(q, t)
-
-    def note(q, tok, reads, writes):
-        for lst, kind in ((writes, True), (reads, False)):
-            for b, a0, a1 in lst:
-                keep = []
-                for e in acc.get(b, []):
-                    inside = a0 <= e[0] and e[1] <= a1
-                    if inside and (kind or (not e[2] and e[4] == q)):
-                        continue
-                    keep.append(e)
-                keep.append((a0, a1, kind, tok, q))
-                acc[b] = keep
-
-    def iv(s):
-        if s[0] == "ind":
-            return iv(s[1]) + iv(s[2])
-        return [(s[0], s[1], s[2])]
-
-    def ap(s):
-        if s[0] == "ind":
-            return ap(s[1]).indirect(ap(s[2]))
-        if len(s) == 4:
-            return T[s[0]][:, s[1]:s[2]:s[3]]
-        return T[s[0]][:, s[1]:s[2]]
-
-    def emit(q, out, ins, fn):
-        reads, writes = [], []
-        for s in ins:
-            reads += iv(s)
-        if out[0] == "ind":
-            writes += iv(out[1])
-            reads += iv(out[2])
-        else:
-            writes += iv(out)
-        deps(q, reads, writes)
-        sem = SEMQ[q]
         snap = dict(know[q])
-        fn(eng[q]).then_inc(T.sem[sem], 1)
-        cnt[sem] += 1
-        total[sem] = cnt[sem]
-        note(q, (sem, cnt[sem], snap), reads, writes)
-
-    def ind(win, off):
-        return ("ind", win, off)
-
-    def vcopy(o, i):
-        emit("v", o, [i], lambda e: e.tensor_copy(ap(o), ap(i)))
-
-    def vtt(o, i0, i1, op):
-        emit("v", o, [i0, i1], lambda e: e.tensor_tensor(ap(o), ap(i0), ap(i1), op))
-
-    def vts(o, i0, s1, op0, s2=None, op1=None):
-        col = isinstance(s1, tuple)
-        a1 = ap(s1) if col else s1
-        ins = [i0, s1] if col else [i0]
-        if op1 is None:
-            emit("v", o, ins, lambda e: e.tensor_scalar(ap(o), ap(i0), a1, None, op0))
-        else:
-            emit("v", o, ins, lambda e: e.tensor_scalar(ap(o), ap(i0), a1, s2, op0, op1))
-
-    def mset(o, c):
-        emit("v", o, [], lambda e: e.memset(ap(o), c))
-
-    def act(o, i, bias=0.0):
-        if bias == 0.0:
-            emit("s", o, [i], lambda e: e.activation(ap(o), ap(i), COPY))
-        else:
-            emit("s", o, [i], lambda e: e.activation(ap(o), ap(i), IDENT, bias, 1.0))
-
-    def step(o, i, bias, scale):
-        emit("s", o, [i], lambda e: e.activation(ap(o), ap(i), SIGM, bias, scale))
-
-    def mm(o, l, r, start, stop):
-        emit("t", o, [l, r], lambda e: e.matmul(ap(o), ap(l), ap(r), start, stop))
-
-    def asel(o, i, pat, op, fill, base, cm):
-        emit("g", o, [i], lambda e: e.affine_select(ap(o), ap(i), pat, op, fill, base, cm))
-
-    def iota(o, pat, base, cm, small=False):
-        if small:
-            emit("g", o, [], lambda e: e.iota(ap(o), pat, base, cm, allow_small_or_imprecise_dtypes=True))
-        else:
-            emit("g", o, [], lambda e: e.iota(ap(o), pat, base, cm))
-
-    def dma(q, o_ap, i_ap, outs, ins):
-        deps(q, ins, outs)
-        sem = "ld%d" % ndma[0]
-        ndma[0] += 1
-        snap = dict(know[q])
-        eng[q].dma_start(o_ap, i_ap).then_inc(T.sem[sem], 16)
-        total[sem] = 16
-        note("d", (sem, 16, snap), ins, outs)
-
-    def wb(k):
-        return "w%d" % (k % 3)
-
-    def col(w, a, b):
-        return (w, OFF[w] + a, OFF[w] + b)
-
-    def blk(m, i):
-        return (m, 128 * i, 128 * i + 128)
-
-    def sq(m):
-        return (m, 0, 128)
-
-    def show(k, src, lst, width, share=0.5):
-        n = 7 * width
-        lc = n // 16
-        h = int(lc * share) // 2 * 2
-        sb = "sb%d" % (k % 2)
-        vcopy((sb, 0, h * 16), ind(src, (lst, 0, h)))
-        act((sb, h * 16, n), ind(src, (lst, h, lc)))
-        reads = [(sb, 0, n)]
-        deps("g", reads, [])
-        tr, land = [], []
-        for d in range(1, N):
-            dst = T.cores[(rank + d) % N]
-            a = topo.addr(dst)
-            e = topo.engines(core, dst)[d - 1]
-            b = V + (d - 1) * 2 * SH
-            spot = col(wb(k), b, b + width)
-            land.append(spot)
-            tr.append(RemoteDMATransfer(dst_ids=[DstId(rid=a[0], pnc=a[1])], dma_engine_mask=1 << e, remote_sem=T.sem["ar%d" % k],
-                                        src=T[sb][:, (d - 1) * width:d * width], dst=ap(spot)))
-        g.remote_dma_fused(tr, local_sem=T.sem["sn%d" % k])
-        total["sn%d" % k] = 7
-        total["ar%d" % k] = 7
-        note("r", ("sn%d" % k, 7, dict(know["g"])), reads, [])
-        for spot in land:
-            note("r", ("ar%d" % k, 7, {}), [], [spot])
-
-    gi = [0]
-
-    def even(x):
-        return int(x) // 2 * 2
-
-    def at(f, i):
-        return f[min(i, len(f) - 1)]
-
-    def chunks(sizes):
-        res, a = [], 0
-        for s in sizes:
-            res.append((a, a + s))
-            a += s
-        return res
-
-    def gather(k, a, b, fv, parts=1):
-        G = "g%d" % (gi[0] % NG)
-        gi[0] += 1
-        w = b - a
-        v = even(w * fv + 1)
-        win = col(wb(k), 0, WW)
-        cuts = [even(v * i / parts) for i in range(parts)] + [v]
-        act((G, 16 * v, 16 * w), ind(win, ("el", a + v, b)))
-
-        def part(i):
-            p, q = cuts[i], cuts[i + 1]
-            if q > p:
-                vcopy((G, 16 * p, 16 * q), ind(win, ("el", a + p, a + q)))
-        if parts == 1:
-            part(0)
-        return G, part
-
-    def sums(G, ps, w, const):
-        if const:
-            mm((ps, 0, w), sq("dc"), ("ones", 0, w), True, False)
-        for i in range(16):
-            mm((ps, 0, w), sq("i8"), (G, i, 16 * w, 16), i == 0 and not const, i == 15 and const)
-
-    def mins(ps, old, new, a, b, par):
-        w = b - a
-        o = CM * (par % 2)
-        vtt(("ti", o, o + w), (ps, 0, w), col(old, a, b), A.min)
-        vcopy(col(new, a, b), ("ti", o, o + w))
-
-    def clip(k, sizes, fv, hook=None):
-        ch = chunks(sizes)
-        M = len(ch)
-        for i in range(M + 1):
-            if i < M:
-                G, _p = gather(k, ch[i][0], ch[i][1], at(fv, i))
-            if i:
-                mins("ps%d" % ((i - 1) % 4), wb(k), wb(k + 1), ch[i - 1][0], ch[i - 1][1], i - 1)
-            if i < M:
-                if hook:
-                    hook(i)
-                sums(G, "ps%d" % (i % 4), ch[i][1] - ch[i][0], True)
-
-    def sel_piece(r, w, a, b):
-        m0, m1 = a // 16, b // 16
-        nm = m1 - m0
-        for k in range(16):
-            mm(("ps4", 0, nm), blk("bk", k), col(w, a + k, b) + (16,), k == 0, k == 15 and r == 0)
-        if r:
-            mm(("ps4", 0, nm), sq("d8k"), ("splt", m0, m1), False, True)
-        vts(("cand", m0, m1), ("ps4", 0, nm), ("thf", 0, 1), A.is_ge)
-        mm(("ps6", 0, nm), sq("gm"), ("cand", m0, m1), True, True)
-        mm(("ps5", 0, nm), sq("lm"), ("cand", m0, m1), True, True)
-        init = ("pfx", m0 - 1, m0)
-        ini = ap(init) if a else 8191.0
-        emit("v", ("pfx", m0, m1), [("ps6", 0, nm), ("zz", m0, m1)] + ([init] if a else []),
-             lambda e: e.tensor_tensor_scan(ap(("pfx", m0, m1)), ap(("ps6", 0, nm)), ap(("zz", m0, m1)), ini, A.add, A.add))
-        vtt(("rk", m0, m1), ("ps5", 0, nm), ("pfx", m0, m1), A.add)
-        vtt(("of", m0, m1), ("rk", m0, m1), ("basec", m0, m1), A.min)
-        vcopy(("ofu", m0, m1), ("of", m0, m1))
-        vcopy(ind(("self", 0, 2 * L), ("ofu", m0, m1)), ("iotac", a, b))
-
-    S16 = ("sel", 0, 16)
-
-    def sel_list(r):
-        vcopy(("selh", 0, 256), ("self", 0, 256))
-        for k in range(16):
-            mm(("ps7", 0, 16), blk("bk", k), ("selh", k, 256, 16), k == 0, k == 15)
-        vts(S16, ("ps7", 0, 16), 0.0625, A.mult, 0.0, A.add)
-        if r == 0:
-            vts(("sel", 16, 32), ("ps7", 0, 16), 0.0625, A.mult, float(HV), A.add)
-
-    def split(r, k):
-        w = wb(k)
-        h0 = L + CAP * r
-        for q in range(2):
-            o = 128 * q
-            vs = even(128 * FW)
-            act(("g%d" % q, 16 * vs, 2048), ind(col(w, 0, WW), ("dl", o + vs, o + 128)))
-            vcopy(("g%d" % q, 0, 16 * vs), ind(col(w, 0, WW), ("dl", o, o + vs)))
-            for i in range(16):
-                mm(("ps6", o, o + 128), blk("ak", i), ("g%d" % q, i, 2048, 16), i == 0, i == 15)
-        vts(ind(("newd", 0, V), S16), ("iotac", h0, h0 + CAP), 1.0, A.mult, -float(NONE), A.add)
-        mset(("newd", V - 8, V), 0.0)
-        vcopy(ind(col(w, 0, V), S16), ("px", 0, 256))
-        vcopy(col(w, h0, h0 + CAP), ("px", 0, 256))
-        vts(("beh", 0, 256), ("ps6", 0, 256), ("thr", 0, 1), A.is_ge)
-        vtt(("mm_", 0, 256), ("beh", 0, 256), ("dd", 0, 256), A.mult)
-        vtt(ind(("ed", 0, V), S16), ("dd", 0, 256), ("mm_", 0, 256), A.subtract)
-        act(("ed", h0, h0 + CAP), ("mm_", 0, 256))
-
-    def pointer_pass(k, sizes, fv, last, hook=None):
-        ch = chunks(sizes)
-        M = len(ch)
-        old, new = wb(k - 1), wb(k + 1)
-        win = col(wb(k), 0, WW)
-        Gs = {}
-
-        def sb(j):
-            return "ps%d" % (j % 4)
-
-        def xb(j):
-            return ("ps4" if j % 2 else "ps5") if last else "ps5"
-
-        def prep(i):
-            a, b = ch[i]
-            vts(("el", a, b), ("ed", a, b), float(NONE), A.add)
-            Gs[i] = gather(k, a, b, at(fv, i), 2)
-
-        def empties(i):
-            a, b = ch[i]
-            w = b - a
-            o = CQ * (i % 2)
-            vts(("emp", o, o + w), ("el", a, b), float(NONE), A.is_equal)
-            vts(("ec", a, b), ("el", a, b), float(MID), A.subtract)
-            mm(("ps6", 64, 64 + w), sq("tri"), ("emp", o, o + w), True, True)
-            vts(("fe", a, b), ("ps6", 64, 64 + w), 1.0, A.is_ge)
-
-        prep(0)
-        prep(1)
-        Gs[0][1](0)
-        Gs[0][1](1)
-        empties(0)
-        for i in range(M + 3):
-            n0, n1, n2, n3 = i < M, 0 <= i - 1 < M, 0 <= i - 2 < M, 0 <= i - 3 < M
-            late = i >= M if last else i + 2 >= M
-            if n0:
-                w = ch[i][1] - ch[i][0]
-                G = Gs[i][0]
-            if n1:
-                a1, b1 = ch[i - 1]
-                w1 = b1 - a1
-                p1 = (i - 1) % 2
-                f, ff, x = "f%d" % p1, "ff%d" % p1, "x%d" % p1
-            if n2:
-                a2, b2 = ch[i - 2]
-                w2 = b2 - a2
-                p2 = i % 2
-                tl, gp, pr = "tl%d" % p2, "gp%d" % p2, "pr%d" % p2
-            if n3:
-                a3, b3 = ch[i - 3]
-                w3 = b3 - a3
-                mm(("ps7", 0, w3), sq("ii"), ("ec", a3, b3), True, False)
-                mm(("ps7", 0, w3), sq("ii"), ("pr%d" % ((i - 3) % 2), 0, w3), False, True)
-                if last:
-                    act(("yo", a3, b3), ("ps7", 0, w3), bias=float(MID))
-                    dma("y", T.ye[:, a3:b3], T.yo[:, a3:b3], [], [("yo", a3, b3)])
+        if o["late"]:
+            sem, val = o["late"][:2]
+            for c in calls:
+                if c[0] == "far":
+                    far(*c[1:])
                 else:
-                    act(("ed", a3, b3), ("ps7", 0, w3), bias=float(MID - NONE))
-                    mm((sb(i - 3), 0, w3), sq("dc"), ("ones", 0, w3), False, False)
-                    mm((sb(i - 3), 0, w3), sq("i8"), ("gp%d" % ((i - 3) % 2), 0, w3), False, True)
-            if n0 and not last:
-                sums(G, sb(i), w, False)
-            if n1 and not last:
-                if late:
-                    step((f, 0, w1), ("ps4", 0, w1), -128.0, -1.0)
-                else:
-                    vts((f, 0, w1), ("ps4", 0, w1), 0.0, A.is_lt)
-                mm(("ps5", 0, w1), sq("tri"), (f, 0, w1), True, False)
-                mm(("ps5", 0, w1), sq("gm"), ("fe", a1, b1), False, True)
-                mm((sb(i - 1), 0, w1), sq("o32"), (f, 0, w1), False, False)
-            if i + 1 < M:
-                Gs[i + 1][1](0)
-            if n2:
-                vts((tl, 0, w2 // 16), ("ps6", 0, w2 // 16), float(MID), A.add)
-                if not last:
-                    act((gp, 0, w2), ind(win, (tl, 0, w2 // 16)))
-            if i + 2 < M:
-                prep(i + 2)
-            if i + 1 < M:
-                empties(i + 1)
-            if n0 and last:
-                mm((xb(i), 0, w), sq("gm"), ("fe", ch[i][0], ch[i][1]), True, False)
-                for q in range(16):
-                    mm((xb(i), 0, w), blk("mk", q), (G, q, 16 * w, 16), False, q == 15)
-            if n1:
-                if late:
-                    step((ff, 0, w1), (xb(i - 1), 0, w1), -300.0, 200.0)
-                else:
-                    vts((ff, 0, w1), (xb(i - 1), 0, w1), 2.0, A.is_ge)
-                vtt((x, 0, w1), (ff, 0, w1), ("ec", a1, b1), A.mult)
-            if n0 and not last:
-                for q in range(16):
-                    mm(("ps4", 0, w), blk("bk", q), (G, q, 16 * w, 16), q == 0, q == 15)
-            if n1:
-                for q in range(16):
-                    mm(("ps6", 0, w1 // 16), blk("bk", q), (x, q, w1, 16), q == 0, q == 15)
-                if not last:
-                    mm((sb(i - 1), 0, w1), sq("o32"), (ff, 0, w1), False, False)
-            if i + 1 < M:
-                Gs[i + 1][1](1)
-            if n2:
-                vtt((pr, 0, w2), ind(("newd", 0, WW), (tl, 0, w2 // 16)), ("fe", a2, b2), A.mult)
-            if n3 and not last:
-                mins(sb(i - 3), old, new, a3, b3, i - 3)
-            if hook:
-                hook(i)
-
-    dma("y", T.shi[:, :], T.sh[:, :], [("shi", 0, 28)], [])
-    dma("y", T.w1[:, 0:L // 2], T.v0[:, 0:L // 2], [("w1", 0, L // 2)], [])
-    dma("s", T.w1[:, L // 2:L], T.v0[:, L // 2:L], [("w1", L // 2, L)], [])
-    ce = L // NE
-    for j in range(NE):
-        dma("y", T.ee[:, j * ce:(j + 1) * ce], T.e[:, j * ce:(j + 1) * ce], [("ee", j * ce, (j + 1) * ce)], [])
-    dma("y", T.thi[:, :], T.th[:, :], [("thi", 0, 1)], [])
-
-    G8 = [[0, 8], [1, 16]]
-
-    def zero_window(w):
-        mset(col(w, L, V), 0.0)
-        mset(col(w, NONE, WW), 0.0)
-        for d in range(1, N):
-            b = V + (d - 1) * 2 * SH + SH
-            mset(col(w, b, b + SH), 0.0)
-
-    mset(("ones", 0, CM), 1.0)
-    asel(sq("ii"), ("ones", 0, 128), [[-1, 128]], A.is_equal, 0.0, 0, 1)
-    asel(sq("ga"), ("ones", 0, 128), [[-16, 8], [0, 16]], A.is_ge, 0.0, 0, 1)
-    asel(sq("gm"), sq("ga"), [[16, 8], [0, 16]], A.is_ge, 0.0, 15, -1)
-    mset(("w1", L, V), 0.0)
-    vcopy(("sl", 0, 28), ("shi", 0, 28))
-    show(1, ("w1", 0, V), "sl", SH)
-    vts(sq("i8"), sq("ii"), 0.125, A.mult)
-    vts(sq("dc"), sq("ii"), -0.4375, A.mult)
-    for j in range(NE):
-        vcopy(("el", j * ce, (j + 1) * ce), ("ee", j * ce, (j + 1) * ce))
-    for w in ("w1", "w2", "w0"):
-        zero_window(w)
-    mset(("w2", 0, HV), 0.0)
-    vcopy(("thf", 0, 1), ("thi", 0, 1))
-    mset(("ed", L, V), 0.0)
-    mset(("newd", 0, V), 0.0)
-    mset(("newd", NONE, WW), 0.0)
-    mset(("zz", 0, 96), 0.0)
-    mset(("neg", 0, 256), 1.0)
-    for k in range(16):
-        asel(blk("bk", k), sq("gm"), G8, A.is_equal, 0.0, -k, 0)
-    asel(sq("up"), sq("gm"), [[1, 128]], A.is_ge, 0.0, 0, -1)
-    asel(sq("lo"), sq("gm"), [[-1, 128]], A.is_gt, 0.0, 0, 1)
-    asel(sq("ith"), sq("ii"), G8, A.is_equal, 0.0, 0, 0)
-    iota(("iotac", 0, V), [[1, V]], 0, 0, True)
-    iota(("newd", V, NONE), [[1, NONE - V]], V + SH - NONE, 0, True)
-    iota(("pi", 0, 96), [[0, 96]], 0, 1)
-    iota(("pb", 0, 96), [[16, 96]], L, 0)
-
-    clip(1, C0, F0)
-    show(2, col("w2", 0, V), "sl", SH)
-    for k in range(16):
-        asel(blk("aka", k), sq("gm"), G8, A.is_gt, -1.0, -k, 0)
-    asel(("akb", 0, 2048), ("aka", 0, 2048), [[0, 16], [-16, 8], [0, 16]], A.is_ge, 0.0, 0, 1)
-    asel(("ak", 0, 2048), ("akb", 0, 2048), [[0, 16], [16, 8], [0, 16]], A.is_ge, 0.0, 15, -1)
-    for d in range(7):
-        vts(("sl5", 8 * d, 8 * d + 4), ("sl", 4 * d, 4 * d + 4), float(HV), A.add)
-        vcopy(("sl5", 8 * d + 4, 8 * d + 8), ("sl", 4 * d, 4 * d + 4))
-        vcopy(("sl6", 8 * d, 8 * d + 4), ("sl", 4 * d, 4 * d + 4))
-    vts(("ed", 0, L), ("ee", 0, L), -float(NONE), A.add)
-    vts(sq("d8k"), sq("ii"), -8192.0, A.mult)
-    vtt(sq("lm"), sq("d8k"), sq("lo"), A.subtract)
-    vts(sq("i2"), sq("ii"), 2.0, A.mult)
-    vtt(sq("tri"), sq("i2"), sq("up"), A.subtract)
-    vts(sq("o32"), sq("gm"), 32.0, A.mult)
-    clip(2, C0, F0)
-    show(3, ("w0", 0, V), "sl", SH)
-    mset(("mka", 0, 2048), -1.0)
-    K3 = [[-1, 16], [0, 8], [1, 16]]
-    asel(("mkb", 0, 2048), ("mka", 0, 2048), K3, A.is_gt, 1.0, 0, 0)
-    asel(("mka", 0, 2048), ("mkb", 0, 2048), K3, A.is_ge, 0.0, 0, 0)
-    asel(("mk", 0, 2048), ("mka", 0, 2048), [[0, 16], [-16, 8], [-1, 16]], A.is_equal, 0.0, 0, 1)
-    emit("v", ("thr", 0, 1), [sq("ith")], lambda e: e.tensor_reduce(ap(("thr", 0, 1)), ap(sq("ith")), AxisListType.X, A.add))
-    vts(("pj", 0, 96), ("pi", 0, 96), 15, A.bitwise_and)
-    vtt(("basec", 0, 96), ("pj", 0, 96), ("pb", 0, 96), A.add)
-    vcopy(("self", 0, 256), ("iotac", L, L + CAP))
-
-    c0 = chunks(C0)
-    H = 1024
-
-    def hook3(i):
-        if i:
-            act(col("w2", c0[i - 1][0], c0[i - 1][1]), ("w1", c0[i - 1][0], c0[i - 1][1]))
-        if i == 3:
-            sel_piece(0, "w1", 0, H)
-
-    clip(3, C0, F3, hook3)
-    show(4, ("w1", 0, V), "sl", SH)
-    act(col("w2", c0[-1][0], c0[-1][1]), ("w1", c0[-1][0], c0[-1][1]))
-    sel_piece(0, "w1", H, L)
-    sel_list(0)
-    vts(("xi", 0, 256), ind(("w1", 0, V), S16), 0.5, A.mult, 0.25, A.add)
-    act(("dd", 0, 256), ind(("ed", 0, V), S16))
-    vcopy(("px", 0, 256), ("xi", 0, 256))
-    vts(("px", 256, 512), ("xi", 0, 256), -256.0, A.add)
-    vcopy(ind(("w2", 0, HV + V), ("sel", 0, 32)), ("px", 0, 512))
-    show(5, ("w2", 0, HV + V), "sl5", 2 * SH)
-    vts(("dl", 0, 256), ("dd", 0, 256), float(NONE), A.add)
-    vcopy(col("w2", L, L + CAP), ("px", 0, 256))
-    split(0, 4)
-
-    def hook5(i):
-        if i == 2:
-            vts(("hb", 0, 448), ind(("newd", 0, V), ("sl", 0, 28)), float(MID - NONE), A.min)
-        if i == 3:
-            for k in range(16):
-                mm(("ps6", 32, 60), blk("bk", k), ("hb", k, 448, 16), k == 0, k == 15)
-            for d in range(7):
-                vts(("sl6", 8 * d + 4, 8 * d + 8), ("ps6", 32 + 4 * d, 36 + 4 * d), 0.0625, A.mult, float(NONE), A.add)
-
-    pointer_pass(5, C5, F5, False, hook5)
-    show(6, ("w0", 0, V), "sl6", 2 * SH)
-    for a, b in chunks(C1):
-        vts(("el", a, b), ("ed", a, b), float(NONE), A.add)
-    vts(("splt", 0, 96), ("of", 0, 96), 256.0, A.is_lt)
-    vcopy(("self", 0, 256), ("iotac", L + CAP, L + 2 * CAP))
-    clip(6, C1, F0)
-    show(7, ("w1", 0, V), "sl6", 2 * SH)
-    zero_window("w0")
-    mset(("w0", 0, L), 0.0)
-
-    def hook7(i):
-        if i == 3:
-            sel_piece(1, "w2", 0, H)
-        if i == 5:
-            sel_piece(1, "w2", H, L)
-
-    clip(7, C1, F7, hook7)
-    show(8, col("w2", 0, V), "sl6", 2 * SH, 0.3)
-    sel_list(1)
-    vcopy(ind(("w0", 0, V), S16), ("neg", 0, 256))
-    mset(("w0", L + CAP, V), 0.0)
-    show(9, ("w0", 0, V), "sl", SH)
-    act(("dd", 0, 256), ind(("ed", 0, V), S16))
-    vts(("dl", 0, 256), ("dd", 0, 256), float(NONE), A.add)
-    vts(("xi", 0, 256), ind(col("w2", 0, V), S16), 0.5, A.mult, 0.25, A.add)
-    vcopy(("px", 0, 256), ("xi", 0, 256))
-    split(1, 8)
-    dma("y", T.yv[:, :], T.w2[:, HV:HV + V], [], [("w2", HV, HV + V)])
-    pointer_pass(9, C9, F9, True)
+                    issue(eng[q], c).then_inc(T.sem[sem], 16)
+        else:
+            sem = SEMQ[q]
+            for c in calls:
+                issue(eng[q], c).then_inc(T.sem[sem], 1)
+            cnt[q] += len(calls)
+            val = cnt[q]
+        total[sem] = val
+        for j in run:
+            tok[j] = (sem, val, snap)
 
     for sem in sorted(total):
         if know["y"].get(sem, 0) < total[sem]:

@@ -9,19 +9,24 @@ MID = V - 1
 PAD = 16
 WW = NONE + 16
 DUM = HL + 2 * HC
+EH = 3 * HL + 2 * CAP
 BIG = 4096.0
 MAGIC = 12582912.0
+MARK = 129.0
+HIGH = 16384.0
+OFF = 1548.0
 NG = 5
-NT = 3
 CM = 256
 PIECE = 32
-RUN = 9
+RUN = 3
+BLK = (112, 128)
 
 C0 = ((0, 192), (192, 192), (384, 128), (512, 128), (640, 128))
-C1 = C0 + ((768, 128),)
-C5 = ((0, 256), (256, 256), (512, 128), (640, 128), (768, 128))
+C1 = ((0, 256), (256, 256), (512, 128), (640, 128), (768, 128))
+C5 = (((0, 256),), ((256, 256), (512, 128)), ((640, 128), (768, 128)))
 C9 = ((768, 128), (896, 128), (0, 256), (256, 256), (512, 192), (704, 64))
-TAILS = (512, 640)
+TOPS = ((512,), (640,))
+RND = (512, 640)
 
 SCRATCH = {}
 
@@ -31,48 +36,47 @@ def _buf(name, cols, dtype, where="sbuf"):
 
 
 for _x in "ab":
-    for _n in ("w0", "w1", "w2", "nw", "w9"):
+    for _n in ("w0", "w1", "w2", "w9"):
         _buf(_n + _x, PAD + WW, "bfloat16")
-    for _n, _c, _t in (("xs", V, "bfloat16"), ("ed", V, "float32"), ("el", DUM, "uint16"), ("ec", DUM, "float16"),
-                       ("em", DUM, "bfloat16"), ("he", DUM, "bfloat16"), ("ee", HL, "int32"), ("shi", 28, "int32"), ("sl", 28, "uint16"),
-                       ("sl6", 56, "uint16"), ("sb0", 896, "bfloat16"), ("sb1", 896, "bfloat16"), ("thi", 1, "int32"),
-                       ("thf", 1, "float32"), ("splt", 96, "bfloat16"), ("px", 512, "bfloat16"),
-                       ("s16", 16, "uint16"), ("m16", 16, "uint16"), ("ddn", CAP, "float32"), ("ddz", CAP, "float32"),
-                       ("dn", HC, "float32"), ("dl", HC, "uint16"), ("gw", 16 * HC, "bfloat16"), ("beh", CAP, "bfloat16"),
-                       ("bb", CAP, "float32")):
+    for _n, _c, _t in (("xs", EH, "bfloat16"), ("xh", HL + HC, "float16"), ("ed", EH + CAP, "int32"), ("el", DUM, "uint16"),
+                       ("ec", HL + HC, "float16"), ("em", DUM, "bfloat16"), ("shb", 28, "uint16"), ("shm", 448, "bfloat16"), ("shi", 28, "int32"),
+                       ("sl", 28, "uint16"), ("sl6", 56, "uint16"), ("sb0", 896, "bfloat16"), ("sb1", 896, "bfloat16"),
+                       ("thi", 1, "int32"), ("thf", 1, "float32"), ("splt", 96, "bfloat16"), ("px", 512, "bfloat16"),
+                       ("s16", 16, "uint16"), ("dlo", 8, "uint16"), ("m16", 16, "uint16"), ("dl", HC, "uint16"),
+                       ("gw", 16 * HC, "bfloat16")):
         _buf(_n + _x, _c, _t)
-for _n, _c, _t in (("ones", 512, "bfloat16"), ("neg", 512, "bfloat16"), ("basec", 96, "float32"), ("zz", 96, "float32"),
-                   ("iotac", HL + 2 * CAP, "float32"), ("cols", 8, "float32"), ("cand", 96, "bfloat16"), ("pfx", 96, "float32"),
-                   ("rk", 96, "float32"), ("of", 96, "float32"), ("ofu", 48, "uint16"), ("self", 2 * L, "float32"),
-                   ("selh", CAP, "float16"), ("val", 16, "float16"),
-                   ("df", 32, "float16"), ("xi", CAP, "float32"), ("hb", 448, "bfloat16"),
-                   ("qk", 2048, "bfloat16"), ("e8", 512, "bfloat16"), ("cd", 960, "bfloat16"), ("hz", 192, "float32"),
-                   ("i32", 128, "float32"), ("pi", 96, "int32"), ("pj", 96, "int32"), ("pb", 96, "int32"),
-                   ("bk", 2048, "bfloat16"), ("ak", 2048, "bfloat16"), ("mk", 2048, "bfloat16"), ("tk", 1024, "bfloat16")):
+for _n, _c, _t in (("ones", 512, "bfloat16"), ("neg", 512, "bfloat16"), ("zz", 128, "bfloat16"), ("cols", 16, "float32"),
+                   ("cand", 240, "bfloat16"), ("cs", 144, "bfloat16"), ("rk", 128, "float32"), ("acc", 8, "float32"),
+                   ("bj", 8, "uint16"), ("cmp", HC, "bfloat16"), ("jrow", HC, "float32"), ("jb", 8, "float32"),
+                   ("shf", 8, "float16"), ("xi", CAP, "float32"), ("hb", 448, "bfloat16"), ("of", 96, "bfloat16"),
+                   ("beh", HC, "bfloat16"), ("dd", 2 * CAP, "int32"),
+                   ("i16", 32, "bfloat16"), ("shj", 56, "int32"), ("shr", 28, "uint16"),
+                   ("qk", 2048, "bfloat16"), ("lo", 896, "float16"), ("cd", 960, "bfloat16"), ("n8", 128, "float32"),
+                   ("pi", 2, "int32"), ("bk", 2048, "bfloat16"), ("ak", 2048, "bfloat16"), ("mk", 2048, "bfloat16"),
+                   ("tk", 1024, "bfloat16"), ("z", 896, "bfloat16"), ("f", 896, "bfloat16"), ("x", 896, "float16"),
+                   ("gp", 896, "bfloat16"), ("pr", 896, "bfloat16"), ("tl", 56, "uint16"), ("eo", 3 * CM, "float32")):
     _buf(_n, _c, _t)
-SQ = ("ga", "gm", "ngm", "ii", "i8", "dc", "mp", "mn", "up", "t4", "lo", "lm", "o32", "d8k", "i4k", "i8k", "ith",
-      "sel0", "sel1", "sw", "pm")
+SQ = ("ga", "gm", "ngm", "ii", "ni", "ino", "mp", "mn", "i7", "i8", "c1k", "up", "su", "nb", "t3", "t4", "om", "d8k", "n4k", "m8k", "ith",
+      "sel0", "sel1", "pm", "da", "db")
 _buf("mx", 128 * len(SQ), "bfloat16")
 for _k in range(NG):
     _buf("g%d" % _k, 16 * CM, "bfloat16")
-for _n, _c, _t in (("f", CM, "bfloat16"), ("z", CM, "bfloat16"), ("lq", CM, "float32"), ("x", CM, "float16"), ("gp", CM, "bfloat16"),
-                   ("pr", CM, "bfloat16"), ("tl", 16, "uint16")):
-    _buf(_n, NT * _c, _t)
 for _k in range(8):
     _buf("ps%d" % _k, 512, "float32", "psum")
 
-NDMA = 80
+NDMA = 100
 SEMAPHORES = (["qv", "qs", "qt", "qg"] + ["%s%d%s" % (s, k, x) for s in ("ar", "sn") for k in range(1, 10) for x in "ab"]
               + ["ld%d" % k for k in range(NDMA)])
 
 A = AluOpType
 COPY = ActivationFunctionType.Copy
 IDENT = ActivationFunctionType.Identity
-RELU = ActivationFunctionType.Relu
+SIGN = ActivationFunctionType.Sign
 SEMQ = {"v": "qv", "s": "qs", "t": "qt", "g": "qg"}
 
-CYC, PE, GATH, SCAT, WAKE, AHEAD = 0.85, 0.5, 1.27, 3.2, 150.0, 300.0
-T_WAY, T_ROWS, T_BYTE, T_FIRST, BEHIND = 1200.0, 2000.0, 0.04, 2500.0, 7000.0
+CYC, PE, GATH, SCAT, VFIX, SFIX, JOIN = 0.83, 0.5, 1.27, 2.2, 35.0, 45.0, 55.0
+WAKE, AHEAD, URGENT = 120.0, 300.0, 450.0
+T_WAY, T_ROWS, T_BYTE, T_FIRST, BEHIND = 1200.0, 2800.0, 0.04, 2500.0, 6000.0
 
 
 def size(name):
@@ -99,7 +103,7 @@ def natural(m, u):
 
 
 def plan():
-    ops, acc, bank, spare = [], {}, {}, [False]
+    ops, acc, bank, spare, urgent = [], {}, {}, [False], [False]
 
     def add(how, reads, writes, late=None, low=False, grp=None, free=False):
         i = len(ops)
@@ -122,7 +126,8 @@ def plan():
                     if wr:
                         old = [e for e in old if not (a0 <= e[0] and e[1] <= a1 and p0 <= e[2] and e[3] <= p1)]
                     acc[b] = old + [(a0, a1, p0, p1, wr, i)]
-        ops.append({"how": how, "deps": deps, "late": late, "prio": 10 ** 6 if low or spare[0] else i, "grp": grp})
+        ops.append({"how": how, "deps": deps, "late": late, "prio": 10 ** 6 if low or spare[0] else i, "grp": grp,
+                    "urgent": urgent[0] and grp is None})
         return i
 
     def rw(out, ins):
@@ -136,7 +141,7 @@ def plan():
         if out[0] == "ind":
             return 50 + n * SCAT
         if ins and ins[0][0] == "ind":
-            return (65 if q == "s" else 50) + n * GATH
+            return (65 if q == "s" else 50) + n * GATH * (2 if tt else 1)
         full = [s for s in [out] + ins if width(s) == n]
         if q == "s":
             k = 1.0
@@ -144,7 +149,7 @@ def plan():
             k = 1.0 if any(s[0][:2] == "ps" for s in ins) else 2.0
         else:
             k = 0.5 if all(size(s[0]) == 2 for s in full) else 1.0
-        return max(64, n * k) * CYC
+        return max(64, n * k) * CYC + (SFIX if q == "s" else VFIX)
 
     def one(q, out, ins, call, tt=False, low=False):
         r, w = rw(out, ins)
@@ -176,13 +181,13 @@ def plan():
         one("v", o, [i0] + tiles(s1, s2), ("ts", o, i0, s1, s2, op0, op1))
 
     def mset(o, c):
-        if not spare[0]:
+        if not spare[0] or len(o) == 6 or SCRATCH[o[0]][2] == "int32":
             one("v", o, [], ("set", o, c))
             return
         for a in range(o[1], o[2], 512):
             p = (o[0], a, min(a + 512, o[2]))
             src = ("ones", 0, width(p))
-            if cost("s", p, []) > cost("v", p, []):
+            if width(p) > 64:
                 one("v", p, [], ("set", p, c))
             else:
                 add({"v": (cost("v", p, []), [("set", p, c)]), "s": (cost("s", p, []), [("act", p, src, IDENT, c, 0.0)])},
@@ -191,8 +196,9 @@ def plan():
     def scaled(o, i, c):
         either(o, [i] + tiles(c), ("ts", o, i, c, None, A.mult, None), ("act", o, i, IDENT, 0.0, c))
 
-    def state(b, a, w):
-        return (b, a + (0 if a < HL else 2 * CAP), a + w + (0 if a < HL else 2 * CAP))
+    def slots(x, a, w):
+        a += HL if a < HL else EH - HL
+        return ("ed" + x, a, a + w)
 
     def mms(lst):
         if len(lst) > RUN and width(lst[0][2]) > 96:
@@ -209,6 +215,9 @@ def plan():
     def mm(o, l, r, start=True, stop=True):
         mms([(o, l, r, start, stop)])
 
+    def total(o, terms, start=True, stop=True):
+        mms([(o, l, r, start and n == 0, stop and n == len(terms) - 1) for n, (l, r) in enumerate(terms)])
+
     def asel(o, i, pat, op, fill, base, cm, low=True):
         add({"g": (190 + 2 * width(o) * CYC, [("asel", o, i, pat, op, fill, base, cm)])}, ranges(i), ranges(o), low=low)
 
@@ -217,13 +226,16 @@ def plan():
 
     ndma = [0]
 
-    def dma(pairs, q="y"):
+    def dma(pairs, q="y", after=None):
         r = [x for o, i in pairs if i[0] != "hbm" for x in ranges(i)]
         w = [x for o, i in pairs if o[0] != "hbm" for x in ranges(o)]
         sem = "ld%d" % ndma[0]
         ndma[0] += 1
-        n = sum(width(i if o[0] == "hbm" else o) * size((i if o[0] == "hbm" else o)[0]) for o, i in pairs)
-        add({q: (60.0 * len(pairs), [("dma", o, i) for o, i in pairs])}, r, w, late=(sem, 16 * len(pairs), T_WAY, 120.0 * len(pairs) + 0.16 * n))
+        on = [i if o[0] == "hbm" else o for o, i in pairs]
+        n = sum(width(s) * size(s[0]) * (1 if len(s) == 6 else 2) for s in on)
+        j = add({q: (60.0 * len(pairs), [("dma", o, i) for o, i in pairs])}, r, w, late=(sem, 16 * len(pairs), T_WAY, 120.0 * len(pairs) + 0.16 * n))
+        if after is not None:
+            ops[j]["deps"][after] = True
 
     def wb(x, k):
         return "w9" + x if k == 9 else "w%d%s" % (k % 3, x)
@@ -240,6 +252,11 @@ def plan():
     def sq(m):
         return blk("mx", SQ.index(m))
 
+    def cl(n):
+        return ("cols", n, n + 1)
+
+    looked = []
+
     def show(x, k, lst, wd, top=V):
         n = 7 * wd
         sb = "sb%d%s" % (k % 2, x)
@@ -252,10 +269,12 @@ def plan():
             copy((sb, h * 16, n), ind(win, (lst, h, n // 16)))
         first = T_FIRST if (x, k) == ("a", 1) else 0.0
         land = [col(wb(x, k), V + d * 2 * SH, V + d * 2 * SH + wd) for d in range(N - 1)]
-        i = add({"g": (300.0 + first, [("far", x, k, sb, wd, land)])}, ranges((sb, 0, n)), [],
+        i = add({"g": (300.0 + first, [("far", x, k, sb, wd, land)])}, ranges((sb, 0, n)) + (ranges(col("w9" + x, 0, WW)) if k == 7 else []), [],
                 late=("sn%d%s" % (k, x), 7, first + T_WAY, T_ROWS + T_BYTE * 256 * wd))
+        ops[i]["deps"].update({j: True for j in looked if k == 6})
         j = add({}, [], [r for s in land for r in ranges(s)], late=("ar%d%s" % (k, x), 7), free=True)
         ops[j]["with"] = i
+        return i
 
     gi, si = [0], [0]
 
@@ -268,171 +287,198 @@ def plan():
             copy((G, 16 * p, 16 * q), ind(win, ("el" + x, a + p, a + q)), grp=gi[0])
         return G
 
-    def over_slots(ps, m, G, w, start=True, stop=True):
-        return [(ps, sq(m) if m == "i8" else blk(m, i), (G, i, 16 * w, 16), start and i == 0, stop and i == 15) for i in range(16)]
+    def sums(w):
+        si[0] += 1
+        return ("ps%d" % (si[0] % 4), 0, w)
 
-    def rounding(ps, w):
-        return [(ps, sq("mp"), ("ones", 0, w), False, False), (ps, sq("mn"), ("ones", 0, w), False, True)]
+    def over_slots(m, G, w):
+        return [(sq(m) if m == "i8" else blk(m, i), (G, i, 16 * w, 16)) for i in range(16)]
 
-    def spread(x, ks, a, w):
-        TAIL = TAILS[ks[0] > 5]
-        if a >= TAIL:
-            mms([(("ps7", w * u, w * u + w), sq("sel%d" % u), state("xs" + x, a, w), True, True) for u in range(2)])
+    def spread(x, k, a, w):
+        tops, xh = TOPS[k > 5], ("xh" + x, a, a + w)
+        if a >= tops[-1]:
+            mms([(("ps7", w * u, w * u + w), sq("sel%d" % u), xh, True, True) for u in range(2)])
             for u in range(2):
-                copy(col(wb(x, ks[0]), natural(a, u), natural(a, u) + w), ("ps7", w * u, w * u + w))
-        for k, top in zip(ks, (TAIL, HL)):
-            if top == a + w:
-                dma([(part(col(wb(x, k), HL * u, HL * u + top), h), part(("xs" + x, 0, top), u)) for u in range(2) for h in range(2)])
+                copy(col(wb(x, k), natural(a, u), natural(a, u) + w), ("ps7", w * u, w * u + w), -OFF)
+        if (a < tops[-1] or k == 4) and a >= RND[k > 5]:
+            vts(("xs" + x, HL + a, HL + a + w), xh, -OFF, A.add)
+        if a + w in tops:
+            lo = ((0,) + tops)[tops.index(a + w)]
+            dma([(part(col(wb(x, k), HL * u + lo, HL * u + a + w), h), part(("xs" + x, HL + lo, HL + a + w), u))
+                 for u in range(2) for h in range(2)])
 
-    def clip(x, k, chunks, ks):
-        for n, (a, w) in enumerate(chunks):
+    def smaller(x, k, a, w, terms):
+        ps, own = sums(w), ("xh" + x, a, a + w)
+        if a < RND[k > 4]:
+            terms, own = terms + [(sq("mp"), ("ones", 0, w)), (sq("mn"), ("ones", 0, w))], ("xs" + x, HL + a, HL + a + w)
+        total(ps, terms)
+        vtt(own, ps, own, A.min)
+        spread(x, k + 1, a, w)
+
+    def clip(x, k, chunks):
+        for a, w in chunks:
             G = gather(x, k, a, w)
-            ps = ("ps%d" % (si[0] % 4), 0, w)
-            si[0] += 1
-            mms([(ps, sq("dc"), ("ones", 0, w), True, False)] + over_slots(ps, "i8", G, w, False, False) + rounding(ps, w))
-            vtt(state("xs" + x, a, w), ps, state("xs" + x, a, w), A.min)
-            spread(x, ks, a, w)
+            smaller(x, k, a, w, [(sq("c1k"), ("ones", 0, w))] + over_slots("i8", G, w))
 
     def select(x, r, k):
-        w, ps = wb(x, k), "ps5" if x == "a" else "ps6"
-        copy(("self", 0, CAP), ("iotac", HL + CAP * r, HL + CAP * r + CAP))
-        mms([((ps, 0, 96), blk("bk", i), col(w, i, L, 16), i == 0, i == 15 and r == 0) for i in range(16)]
-            + ([((ps, 0, 96), sq("d8k"), ("splt" + x, 0, 96), False, True)] if r else []))
-        vts(("cand", 0, 96), (ps, 0, 96), ("thf" + x, 0, 1), A.is_ge)
-        mms([((ps, 96, 192), sq("gm"), ("cand", 0, 96), True, True), ((ps, 192, 288), sq("lm"), ("cand", 0, 96), True, True)])
-        one("v", ("pfx", 0, 96), [(ps, 96, 192), ("zz", 0, 96)], ("scan", ("pfx", 0, 96), (ps, 96, 192), ("zz", 0, 96), 8191.0))
-        vtt(("rk", 0, 96), (ps, 192, 288), ("pfx", 0, 96), A.add)
-        vtt(("of", 0, 96), ("rk", 0, 96), ("basec", 0, 96), A.min)
-        for u in range(2):
-            vcopy(part(("ofu", 0, 48), u), part(("of", 48 * u, 48 * u + 48), u))
-        vcopy(ind(("self", 0, 2 * L), ("ofu", 0, 48)), ("iotac", 0, HL))
-        vcopy(("selh", 0, CAP), ("self", 0, CAP))
-        mms([((ps, 288, 304), blk("bk", i), ("selh", i, CAP, 16), i == 0, i == 15) for i in range(16)])
-        vts(("val", 0, 16), (ps, 288, 304), 0.0625, A.mult)
-        vts(("m16" + x, 0, 16), (ps, 288, 304), 0.0625, A.mult, ("cols", 6, 7), A.subtract)
-        mms([((ps, 304, 320), sq("sw"), ("val", 0, 16), True, False), ((ps, 304, 320), sq("ii"), ("df", 16 * r, 16 * r + 16), False, True)])
-        vcopy(("s16" + x, 0, 16), (ps, 304, 320))
+        w, nb, c0 = wb(x, k), BLK[r], BLK[0] * r
+        urgent[0] = r == 0
+        cand, own = ("cand", c0, c0 + nb), ("cand", c0, c0 + 96)
+        total(("ps5", 128, 224), [(blk("bk", i), col(w, i, L, 16)) for i in range(16)] + ([(sq("d8k"), ("splt" + x, 0, 96))] if r else []))
+        vts(own, ("ps5", 128, 224), ("thf" + x, 0, 1), A.is_ge)
+        one("v", ("cs", 8, 8 + nb), [cand, ("zz", 0, nb)], ("scan", ("cs", 8, 8 + nb), cand, ("zz", 0, nb), 0.0))
+        mm(("ps5", 0, nb), sq("gm"), ("cs", 8, 8 + nb))
+        total(("ps7", 0, nb), [(sq("gm"), ("cs", 7, 7 + nb)), (sq("up"), cand)])
         if r == 0:
-            vts(("splt" + x, 0, 96), ("of", 0, 96), float(CAP), A.is_lt)
+            total(("ps7", 128, 224), [(sq("gm"), ("cs", 7, 103)), (sq("su"), own), (sq("d8k"), own)])
+        for m in range(HC // 16):
+            o, i, b, s = ("gw" + x, 128 * m, 128 * m + nb), ("ps5", 0, nb), ("jb", m, m + 1), ("acc", m, m + 1)
+            add({"s": (nb * CYC + 40, [("act", o, i, SIGN, b, 1.0, s)])}, ranges(i) + ranges(b), ranges(o) + ranges(s))
+        copy(("rk", 0, nb), ("ps7", 0, nb))
+        if r == 0:
+            vts(("of", 0, 96), ("ps7", 128, 224), 8192.0, A.add, float(CAP), A.min)
+        vts(("bj", 0, 8), ("acc", 0, 8), -0.5, A.mult, nb / 2, A.add)
+        vtt(("cmp", 0, HC), ind(("rk", 0, nb), ("bj", 0, 8)), ("jrow", 0, HC), A.is_le)
+        total(("ps5", 224, 232), [(("n8", 0, 128), ("acc", 0, 8))] + [(blk("bk", i), ("cmp", i, HC, 16)) for i in range(16)])
+        vts(("shf", 0, 8), ("ps5", 224, 232), 8.0 * nb, A.add)
+        vts(("dlo" + x, 0, 8), ("ps5", 224, 232), cl(9 + r), A.add)
+        mms([(("ps5", 240 + 8 * u, 248 + 8 * u), sq("sel%d" % u), ("shf", 0, 8), True, True) for u in range(2)])
+        vcopy(("s16" + x, 0, 16), ("ps5", 240, 256))
+
+    def shown_halves(x):
+        copy(("hb", 0, 448), ind(("of", 0, 96), ("shb" + x, 0, 28)))
+        mm(("ps4", 0, 448), sq("ii"), ("hb", 0, 448))
+        vtt(("hb", 0, 448), ("ps4", 0, 448), ("shm" + x, 0, 448), A.min)
+        total(("ps4", 448, 476), [(blk("bk", i), ("hb", i, 448, 16)) for i in range(16)])
+        for c in range(4):
+            vts(("sl6" + x, 4 + c, 56, 8), ("ps4", 448 + c, 476, 4), float(L), A.add)
 
     def split(x, r, k):
-        w, ps = wb(x, k), "ps5" if x == "a" else "ps6"
-        S16, M16, px = ("s16" + x, 0, 16), ("m16" + x, 0, 16), ("px" + x, 0, CAP)
-        h0, m0 = L + CAP * r, HL + 2 * CAP + HC * r
-        ed = "ed" + x
-        codes = col(("nw" if r == 0 else "w9") + x, 0, V)
-        xi, hb, b7 = ("xi", 0, CAP), ("hb", 0, 448), ("cols", 7, 8)
+        w, ps = wb(x, k), "ps5"
+        S16, px = ("s16" + x, 0, 16), ("px" + x, 0, CAP)
+        h0, m0 = L + CAP * r, HL + HC * r
+        old = ind(("ed" + x, 0, EH), ("dlo" + x, 0, 8))
+        codes = col(w if r == 0 else "w9" + x, 0, V)
+        xi, beh, M16 = ("xi", 0, CAP), ("beh", 0, HC), ("m16" + x, 0, 16)
 
         def halved():
             src = ind(col(w, 0, V), S16)
             either(xi, [src], ("ts", xi, src, 0.5, 0.25, A.mult, A.add), ("act", xi, src, IDENT, 0.25, 0.5))
+            if r == 0:
+                vts(("px" + x, CAP, 2 * CAP), xi, MAGIC, A.add, -MAGIC - MARK, A.add)
             vts(px, xi, MAGIC, A.add, -MAGIC, A.add)
 
-        copy(("ddz" + x, 0, CAP), ind((ed, 0, V), M16), -float(NONE))
-        vcopy(ind(codes, S16), ("cd", CAP * r, CAP * r + CAP))
-        mms([((ps, 352, 480), ("hz", 64 - 64 * u, 192 - 64 * u), ("ddz" + x, HC * u, HC * u + HC), u == 0, u == 1) for u in range(2)])
-        vts(("dl" + x, 0, HC), (ps, 352, 480), float(NONE), A.add)
-        copy(("dn" + x, 0, HC), (ps, 352, 480), float(NONE))
         if r:
+            vcopy(ind(codes, S16), ("cd", CAP, 2 * CAP))
             mset(col("w9" + x, h0, V), 0.0)
-            show(x, 9, ("sl" + x), SH)
+            sent = show(x, 9, ("sl" + x), SH)
         else:
             w5 = wb(x, k + 1)
-            src = ind(codes, ("sl" + x, 0, 28))
-            either(hb, [src, b7], ("ts", hb, src, b7, 0.0, A.add, A.max), ("act", hb, src, RELU, b7))
             halved()
-            vts(("px" + x, CAP, 2 * CAP), xi, MAGIC, A.add, -MAGIC - 256.0, A.add)
-            mms([((ps, 320, 348), blk("bk", i), ("hb", i, 448, 16), i == 0, i == 15) for i in range(16)])
             vcopy(ind(col(w5, 0, V), S16), ("px" + x, CAP, 2 * CAP))
             copy(col(w5, h0, h0 + CAP), px)
-            for c in range(4):
-                vts(("sl6" + x, 4 + c, 56, 8), (ps, 320 + c, 348, 4), -0.25, A.mult, float(MID), A.add)
-            show(x, 5, "sl6" + x, 2 * SH)
+            shown_halves(x)
+            sent = show(x, 5, "sl6" + x, 2 * SH)
+        urgent[0] = False
+        vcopy(("dl" + x, 0, HC), old)
+        vts(M16, ("ps5", 240, 256), cl(11), A.add)
+        if r == 0:
+            vts(("splt" + x, 0, 96), ("of", 0, 96), float(CAP), A.is_lt)
         gi[0] += NG
         for p in range(0, HC, 32):
             copy(("gw" + x, 16 * p, 16 * p + 512), ind(col(w, 0, WW), ("dl" + x, p, p + 32)), grp=gi[0])
-        copy(("ddn" + x, 0, CAP), ind((ed, 0, V), M16))
-        mms(over_slots((ps, 0, HC), "ak", "gw" + x, HC))
-        vts(("beh" + x, 0, HC), (ps, 0, HC), ("cols", 0, 1), A.is_ge, float(NONE), A.mult)
-        vts(("beh" + x, HC, CAP), (ps, 0, HC), ("cols", 0, 1), A.is_lt, float(NONE), A.mult)
-        mms([((ps, HC + HC * u, CAP + HC * u), sq("sel%d" % u), ("beh" + x, 0, HC), True, True) for u in range(2)])
-        vtt((ed, m0, m0 + HC), ("dn" + x, 0, HC), ("beh" + x, HC, CAP), A.max)
-        copy(("bb" + x, 0, CAP), (ps, HC, HC + CAP))
-        vtt(ind((ed, 0, V), M16), ("ddn" + x, 0, CAP), ("bb" + x, 0, CAP), A.max)
-        lists(x, r, C5 if r == 0 else C9)
+        vcopy(("dd", 0, CAP), ind(("ed" + x, 0, EH), M16))
+        total((ps, 0, HC), over_slots("ak", "gw" + x, HC))
+        vts(beh, (ps, 0, HC), cl(0), A.is_ge, float(NONE), A.mult)
+        mms([((ps, HC + HC * u, CAP + HC * u), sq("sel%d" % u), beh, True, True) for u in range(2)])
+        total((ps, 3 * HC, 4 * HC), [(sq("ino"), o128), (sq("ni"), beh)])
+        vtt(("dd", CAP, 2 * CAP), (ps, HC, HC + CAP), ("dd", 0, CAP), A.max)
+        vcopy(ind(("ed" + x, 0, EH), M16), ("dd", CAP, 2 * CAP))
+        for u in range(2):
+            vtt(part(slots(x, m0, HC), u), part((ps, 3 * HC, 4 * HC), u), part(("dd", HC * u, HC * u + HC), u), A.max)
+        lists(x, r)
         if r:
             halved()
-        vcopy(ind(("xs" + x, 0, V), M16), px)
-        for u in range(2):
-            copy(part(("xs" + x, m0, m0 + HC), u), part(("px" + x, HC * u, HC * u + HC), u))
+            vcopy(ind(col(w, 0, V), S16), px)
+            copy(col(w, h0, V), px)
+            row = 64 * "ab".index(x)
+            dma([(("hbm", "yv", (row, row + 64), (a, a + V // 2)), part(col(w, a, a + V // 2), u)) for u, a in ((0, 0), (1, V // 2))])
+        else:
+            vcopy(ind(("xs" + x, 0, EH), M16), px)
+            vts(("xh" + x, RND[1], HL), ("xs" + x, HL + RND[1], L), OFF, A.add)
+            for u in range(2):
+                vts(part(("xh" + x, HL, HL + HC), u), part(("px" + x, HC * u, HC * u + HC), u), OFF, A.add)
+            vcopy(ind(codes, S16), ("cd", 0, CAP))
+            dma([(col(w, V + 2 * SH * d, V + 2 * SH * d + SH), ("cd", 512 + SH * d, 512 + SH * d + SH)) for d in range(N - 1)],
+                after=sent)
+
+    def lists(x, r):
+        for a, w in ((0, 256), (256, 512), (HL + HC * r, HC))[::1 - 2 * r]:
+            vcopy(("el" + x, a, a + w), slots(x, a, w))
+        n = HL + HC + HC * r
+        vts(("em" + x, 0, n), ("el" + x, 0, n), float(NONE), A.is_equal, -1.0, A.mult)
+        if r == 0:
+            vts(("ec" + x, 0, n), ("el" + x, 0, n), float(MID), A.subtract)
+            for a, w in ((0, 384), (384, 512)):
+                ec = ("ec" + x, a, a + w)
+                total(("ps5", 0, w), [(sq("n4k"), ("ones", 0, w)), (sq("m8k"), ("em" + x, a, a + w))])
+                vtt(ec, ("ps5", 0, w), ec, A.min)
+
+    def pointer_clip(x, k, spans):
+        for span in spans:
+            a0, a1 = span[0][0], span[-1][0] + span[-1][1]
+            for a, w in span:
+                f, z, lo, xx = [(b, a, a + w) for b in ("f", "z", "lo", "x")]
+                G = gather(x, k, a, w)
+                pq = sums(w)
+                total(pq, [(sq("i7"), ("ones", 0, w))] + over_slots("qk", G, w))
+                vts(z, pq, HIGH * MAGIC, A.add, -HIGH * MAGIC, A.add)
+                vts(f, z, 0.0, A.is_lt, OFF / (2 * MARK), A.add)
+                vtt(lo, pq, z, A.subtract)
+                total(("ps4", 0, w), [(sq("ii"), ("ec" + x, a, a + w)), (sq("t4"), f)])
+                vts(xx, ("ps4", 0, w), cl(12), A.add, -2048.0, A.max)
+            n = (a1 - a0) // 16
+            total(("ps6", 0, n), [(blk("bk", i), ("x", a0 + i, a1, 16)) for i in range(16)])
+            vts(("tl", a0 // 16, a1 // 16), ("ps6", 0, n), float(15 * 2048 + MID + PAD), A.add)
+            for a, w in span:
+                tl = ("tl", a // 16, (a + w) // 16)
+                copy(("gp", a, a + w), ind((wb(x, k), 0, PAD + WW), tl), MARK - 7 - 3.5)
+                copy(("pr", a, a + w), ind((wb(x, k - 1), 0, PAD + WW), tl), cl(1))
+                looked.append(len(ops) - 1)
+            for a, w in span:
+                f, lo, gp = [(b, a, a + w) for b in ("f", "lo", "gp")]
+                smaller(x, k, a, w, [(sq("i8"), lo), (sq("om"), f), (sq("i8"), gp)])
+                ed = slots(x, a, w)
+                total(("ps6", 0, w), [(sq("t4"), ("em" + x, a, a + w)), (sq("pm"), ("pr", a, a + w))])
+                vtt(ed, ("ps6", 0, w), ed, A.min)
+                vcopy(("el" + x, a, a + w), ed)
 
     pi = [0]
-
-    def lists(x, r, chunks):
-        for a, w in ((0, 256), (256, 512), (HL, HC + HC * r))[::1 - 2 * r]:
-            vcopy(("el" + x, a, a + w), state("ed" + x, a, w))
-        for a, w in ((0, 384), (384, 512 + HC * r)):
-            el, ec, em, he = [(b + x, a, a + w) for b in ("el", "ec", "em", "he")]
-            vts(em, el, float(NONE), A.is_equal, -1.0, A.mult)
-            if r == 0:
-                ps = ("ps5" if x == "a" else "ps6", 0, w)
-                vts(ec, el, float(MID), A.subtract)
-                mm(ps, sq("gm"), em)
-                vts(he, ps, -1.0, A.is_le, -2.0, A.add)
-
-    def pointer_clip(x, k, chunks):
-        for n, (a, w) in enumerate(chunks):
-            p = pi[0] % NT
-            el, ec, em, he = [(b + x, a, a + w) for b in ("el", "ec", "em", "he")]
-            ed, xs = state("ed" + x, a, w), state("xs" + x, a, w)
-            f, z, lo, xx, gp, pr = [(b, CM * p, CM * p + w) for b in ("f", "z", "lq", "x", "gp", "pr")]
-            tl = ("tl", 16 * p, 16 * p + w // 16)
-            ps, pq = ("ps2", 0, w), ("ps%d" % (pi[0] % 2), 0, w)
-            pi[0] += 1
-            G = gather(x, k, a, w)
-            mms(over_slots(pq, "qk", G, w))
-            vts(f, pq, -1024.0, A.is_lt)
-            vts(z, pq, 2048 * MAGIC, A.add, -2048 * MAGIC, A.add)
-            vtt(lo, pq, z, A.subtract)
-            mms([(("ps3", 0, w), sq("ii"), ec, True, False), (("ps3", 0, w), sq("i4k"), he, False, False),
-                 (("ps3", 0, w), sq("t4"), f, False, True)])
-            vts(xx, ("ps3", 0, w), -2048.0, A.max)
-            mms([(("ps4", 0, w // 16), blk("bk", i), ("x", xx[1] + i, xx[2], 16), i == 0, i == 15) for i in range(16)])
-            vts(tl, ("ps4", 0, w // 16), float(15 * 2048 + MID + PAD), A.add)
-            copy(gp, ind((wb(x, k), 0, PAD + WW), tl), 252.5)
-            copy(pr, ind(("nw" + x, 0, PAD + WW), tl), ("cols", 1, 2))
-            mms([(ps, ("i32", 0, 128), lo, True, False), (ps, sq("o32"), f, False, False), (ps, sq("i8"), gp, False, False)]
-                + rounding(ps, w))
-            vtt(xs, ps, xs, A.min)
-            mms([(("ps7", 0, w), sq("t4"), em, True, False), (("ps7", 0, w), sq("pm"), pr, False, True)])
-            vtt(ed, ("ps7", 0, w), ed, A.min)
-            spread(x, [k + 1], a, w)
-            vcopy(el, ed)
 
     def pointer_last(x, chunks):
         row = 64 * "ab".index(x)
         for a, w in chunks:
-            p = pi[0] % 2
+            p = pi[0] % 3
             pi[0] += 1
-            em, ed = ("em" + x, a, a + w), state("ed" + x, a, w)
-            xx = ("x", CM * p, CM * p + w)
-            ps, pt = ("ps%d" % p, 0, w), ("ps%d" % (2 + p), 0, w)
+            xx, eo = ("x", CM * p, CM * p + w), ("eo", CM * p, CM * p + w)
+            ps, pt = sums(w), ("ps%d" % (4 + pi[0] % 2 * 2), 0, w)
             G = gather(x, 9, a, w)
-            mms(over_slots(ps, "mk", G, w))
+            total(ps, over_slots("mk", G, w))
             vts(xx, ps, 0.0, A.max, -(NONE + BIG) / 16, A.add)
-            mms([(pt, sq("t4"), em, True, False), (pt, sq("ngm"), xx, False, True)])
-            vtt(ed, pt, ed, A.min)
-            dma([(("hbm", "ye", (row, row + 64), (natural(a, u), natural(a, u) + w)), part(ed, u)) for u in range(2)])
+            total(pt, [(sq("t4"), ("em" + x, a, a + w)), (sq("ngm"), xx)])
+            vtt(eo, pt, slots(x, a, w), A.min)
+            dma([(("hbm", "ye", (row, row + 64), (natural(a, u), natural(a, u) + w)), part(eo, u)) for u in range(2)])
 
     for n, x in enumerate("ab"):
         rows = (64 * n, 64 * n + 64)
         dma([(part(("shi" + x, 0, 28), u), ("hbm", "sh", rows, (0, 28))) for u in range(2)])
         dma([(part(col(wb(x, 1), 0, L), 0), ("hbm", "v0", rows, (0, L)))])
         dma([(part(col(wb(x, 1), 0, L), 1), ("hbm", "v0", rows, (0, L)))], "s" if n == 0 else "y")
-        dma([(part(("ee" + x, 0, HL), u), ("hbm", "e", rows, (HL * u, HL * u + HL))) for u in range(2)])
-        dma([(part(("xs" + x, 0, HL), u), ("hbm", "v0", rows, (HL * u, HL * u + HL))) for u in range(2)])
     for n, x in enumerate("ab"):
-        dma([(part(("thi" + x, 0, 1), u), ("hbm", "th", (64 * n, 64 * n + 64), (0, 1))) for u in range(2)])
+        rows = (64 * n, 64 * n + 64)
+        dma([(part(slots(x, 0, HL), u), ("hbm", "e", rows, (HL * u, HL * u + HL))) for u in range(2)])
+        dma([(part(("xs" + x, HL, L), u), ("hbm", "v0", rows, (HL * u, HL * u + HL))) for u in range(2)])
+        dma([(part(("thi" + x, 0, 1), u), ("hbm", "th", rows, (0, 1))) for u in range(2)])
 
     G8 = [[0, 8], [1, 16]]
     o128 = ("ones", 0, 128)
@@ -453,33 +499,42 @@ def plan():
     for x in "ab":
         vcopy(("sl" + x, 0, 28), ("shi" + x, 0, 28))
         show(x, 1, "sl" + x, SH, L)
-    for n, c in (("i8", 0.125), ("dc", -0.4375), ("mp", MAGIC), ("mn", -MAGIC), ("d8k", -8192.0), ("i4k", BIG), ("i8k", 2 * BIG)):
-        scaled(sq(n), sq("ii"), c)
     spare[0] = True
-    copy(("i32", 0, 128), sq("ii"))
+    for n, c in (("i8", 0.125), ("d8k", -8192.0), ("n4k", -BIG), ("i7", 7.0), ("ni", -1.0), ("ino", float(NONE)), ("mp", MAGIC)):
+        scaled(sq(n), sq("ii"), c)
+    for p0, p1, c in ((0, 32, 48.0), (32, 64, (OFF - 0.4375) / 32 - 48.0), (64, 128, 0.0)):
+        mset(sq("c1k") + (1, p0, p1), c)
+    mset(sq("mn"), 0.0)
+    for p0, c in ((0, -MAGIC), (32, -1536.0), (64, 1536.0 - OFF)):
+        mset(sq("mn") + (1, p0, p0 + 1), c)
+    scaled(("n8", 0, 128), sq("ii"), -8.0)
     for x in "ab":
-        vcopy(("el" + x, 0, HL), ("ee" + x, 0, HL))
+        vcopy(("el" + x, 0, HL), slots(x, 0, HL))
+        vts(("xh" + x, RND[0], HL), ("xs" + x, HL + RND[0], L), OFF, A.add)
         for k in (1, 2, 3):
             zero_window(wb(x, k))
+        mset((wb(x, 4), 0, PAD), 0.0)
     spare[0] = False
     for k in range(16):
         asel(blk("bk", k), sq("gm"), G8, A.is_equal, 0.0, -k, 0)
     asel(sq("up"), sq("gm"), [[1, 128]], A.is_ge, 0.0, 0, -1)
-    asel(sq("lo"), sq("gm"), [[-1, 128]], A.is_gt, 0.0, 0, 1)
+    asel(sq("su"), sq("gm"), [[1, 128]], A.is_gt, 0.0, 0, -1)
     asel(sq("ith"), sq("ii"), G8, A.is_equal, 0.0, 0, 0)
-    for a in (0, HL // 2):
-        iota(("iotac", a, a + HL // 2), [[1, HL // 2]], a, 0)
-    iota(("iotac", HL, HL + 2 * CAP), [[1, 2 * CAP]], L, 0)
-    iota(("pi", 0, 96), [[0, 96]], 0, 1)
-    iota(("pb", 0, 96), [[16, 96]], L, 0)
-    iota(("self", 0, 512), [[-272, 2], [-16, 16], [0, 16]], 1392, 0)
-    iota(("self", 512, 960), [[-128, 7], [-16, 4], [0, 16]], 816, 0)
-    iota(("self", 1024, 1536), [[16, 2], [0, 16], [-1, 16]], 16, 0)
-    iota(("self", 1536, 1984), [[0, 28], [-1, 16]], 16, 0)
-    mset(("hz", 0, 192), 0.0)
-    i0 = sq("ii")[1]
-    vtt(("hz", 64, 128), ("mx", i0, i0 + 64), ("mx", i0 + 64, i0 + 128), A.add)
-    mset(("neg", 0, 512), -512.0)
+    iota(("pi", 0, 1), [[0, 1]], 0, 1, False)
+    iota(("i16", 16, 32), [[1, 16]], 0, 0, False)
+    iota(("jrow", 0, HC), [[1, HC]], 0, 0, False)
+    iota(("jb", 0, 8), [[-16, 8]], 0, 0, False)
+    iota(("gwa", 0, 512), [[-272, 2], [-16, 16], [0, 16]], 1392, 0, False)
+    iota(("gwa", 1024, 1536), [[16, 2], [0, 16], [-1, 16]], 16, 0, False)
+    iota(("gwa", 512, 960), [[-128, 7], [-16, 4], [0, 16]], 816, 0, False)
+    iota(("gwa", 1536, 1984), [[0, 28], [-1, 16]], 16, 0, False)
+    for x in "ab":
+        rows = (64 * "ab".index(x), 64 * "ab".index(x) + 64)
+        for a, b in ((0, HL), (L, L + 640), (L + 640, EH)):
+            iota(("ed" + x, a, b), [[0, b - a]], NONE, 0)
+        for a in range(0, WW, 592):
+            iota(col("w9" + x, a, a + 592), [[0, 592]], 0, 0)
+        dma([(part(("ed" + x, L * u, L * u + HL), 1 - u), ("hbm", "e", rows, (HL * u, HL * u + HL))) for u in range(2)])
 
     def by_slot(m, src, steps):
         for a in range(0, 2048, 512):
@@ -493,49 +548,58 @@ def plan():
             asel(nxt, cur, [[0, 4], [-16, 8], [0, 16]], A.is_ge, 0.0, 0, 1)
             asel(out, nxt, [[0, 4], [16, 8], [0, 16]], A.is_ge, 0.0, 15, -1)
 
+    spare[0] = True
+    mset(("neg", 0, 512), -512.0)
     by_slot("ak", ("ones", 0, 512), [(A.is_gt, -1.0)])
-    mset(("e8", 0, 512), 0.125)
     for a in range(0, 2048, 512):
-        asel(("tk", 0, 512), ("e8", 0, 512), [[0, 4], [-1, 128]], A.is_equal, 0.0, 0, 1)
-        asel(("qk", a, a + 512), ("tk", 0, 512), [[-255, 4], [-16, 8], [256, 16]], A.not_equal, 2048.0, -15 - 255 * (a // 128), 1)
+        asel(("tk", 0, 512), ("ones", 0, 512), [[0, 4], [-1, 128]], A.is_equal, 0.0, 0, 1)
+        asel(("qk", a, a + 512), ("tk", 0, 512), [[-255, 4], [-16, 8], [256, 16]], A.not_equal, HIGH, -15 - 255 * (a // 128), 1)
     by_slot("mk", ("neg", 0, 512), [(A.is_gt, 0.25), (A.is_ge, 0.0)])
 
     def more_constants():
-        vtt(sq("lm"), sq("d8k"), sq("lo"), A.subtract)
-        vts(sq("t4"), sq("up"), -BIG, A.mult)
-        vtt(sq("t4"), sq("t4"), sq("i8k"), A.add)
-        vts(sq("o32"), sq("gm"), 32.0, A.mult)
-        vts(sq("ngm"), sq("gm"), -1.0, A.mult)
-        vtt(sq("sw"), sq("sel0"), sq("sel1"), A.add)
-        one("v", ("cols", 0, 1), [sq("ith")], ("sum", ("cols", 0, 1), sq("ith")))
-        vts(("pj", 0, 96), ("pi", 0, 96), 15, A.bitwise_and)
-        vtt(("basec", 0, 96), ("pj", 0, 96), ("pb", 0, 96), A.add)
-        mset(("zz", 0, 96), 0.0)
-        r16 = ("pj", 0, 1)
-        vts(("cols", 1, 2), r16, 8.0, A.is_ge, (NONE + BIG) / 16, A.mult)
-        vts(("cols", 2, 3), r16, 4.0, A.is_lt)
-        vts(("cols", 3, 4), r16, 8.0, A.is_lt)
-        vtt(("cols", 4, 5), ("cols", 3, 4), ("cols", 2, 3), A.subtract)
-        vts(("cols", 5, 6), ("cols", 3, 4), -2.25, A.mult, 2.0, A.add)
-        vts(("cols", 6, 7), ("pi", 0, 1), 64.0, A.is_ge, float(HL), A.mult)
-        vts(("cols", 7, 8), ("cols", 2, 3), -895.0, A.mult, -1.0, A.add)
-        vts(sq("pm"), sq("gm"), ("cols", 5, 6), A.mult)
-        for a in range(0, 960, 320):
-            hi, lo = ("self", a, a + 320), ("self", 1024 + a, 1344 + a)
-            scaled(hi, hi, ("cols", 2, 3))
-            scaled(lo, lo, ("cols", 4, 5))
-            vtt(("cd", a, a + 320), hi, lo, A.add)
-        vts(("df", 0, 32), ("basec", 0, 32), -1.0, A.mult)
-        copy(("iotac", 0, HL), ("iotac", 0, HL), ("cols", 6, 7))
+        for n, c in (("nb", -BIG), ("om", MARK / 8), ("ngm", -1.0), ("m8k", -2 * BIG)):
+            scaled(sq(n), sq("gm"), c)
+        asel(sq("t3"), sq("nb"), [[1, 128]], A.is_ge, 0.0, 0, -1)
+        asel(sq("t4"), sq("t3"), [[-1, 128]], A.not_equal, BIG, 0, 1)
+        one("v", cl(0), [sq("ith")], ("sum", cl(0), sq("ith")))
+        r16 = ("pi", 1, 2)
+        vts(r16, ("pi", 0, 1), 15, A.bitwise_and)
+        mset(("zz", 0, 128), 0.0)
+        mset(("cs", 0, 8), 0.0)
+        mset(("cand", 96, 112), 1.0)
+        mset(("cand", 208, 224), 0.0)
+        mset(("cand", 224, 240), 1.0)
+        vts(cl(1), r16, 8.0, A.is_ge, (NONE + BIG) / 16, A.mult)
+        vts(cl(2), r16, 4.0, A.is_lt)
+        vts(cl(3), r16, 8.0, A.is_lt)
+        vtt(cl(4), cl(3), cl(2), A.subtract)
+        vts(cl(5), cl(3), -2.25, A.mult, 2.0, A.add)
+        vts(cl(6), ("pi", 0, 1), 64.0, A.is_ge, -float(HL), A.mult)
+        vcopy(cl(8), r16)
+        for r in range(2):
+            vts(cl(9 + r), cl(6), 8.0 * BLK[r] + HL, A.add)
+        vts(cl(11), cl(6), float(HL), A.add)
+        vts(cl(12), r16, BIG * OFF / (2 * MARK), A.mult, -BIG - BIG * OFF / (2 * MARK), A.add)
+        vts(cl(7), ("pi", 0, 1), 64.0, A.is_ge, float(HC), A.mult)
+        vts(cl(13), cl(7), 0.5, A.add)
+        vts(("jb", 0, 8), ("jb", 0, 8), cl(8), A.subtract, cl(13), A.subtract)
+        copy(("jrow", 0, HC), ("jrow", 0, HC), cl(7))
+        scaled(sq("pm"), sq("gm"), cl(5))
+        scaled(sq("da"), sq("ii"), cl(2))
+        scaled(sq("db"), sq("ii"), cl(4))
+        for a, w in ((0, 512), (512, 448)):
+            total(("ps6", 0, w), [(sq("da"), ("gwa", a, a + w)), (sq("db"), ("gwa", 1024 + a, 1024 + a + w))])
+            copy(("cd", a, a + w), ("ps6", 0, w))
+        vts(("i16", 0, 16), ("i16", 16, 32), cl(8), A.is_equal, float(CAP), A.mult)
 
     def tables(x):
-        vcopy(("ed" + x, 0, HL), ("ee" + x, 0, HL))
-        mset(("ed" + x, HL, V), float(NONE))
+        vts(("shj", 0, 28), ("shi" + x, 0, 28), 4, A.logical_shift_right)
+        vcopy(("shb" + x, 0, 28), ("shj", 0, 28))
+        vts(("shj", 28, 56), ("shi" + x, 0, 28), 15, A.bitwise_and)
+        vcopy(("shr", 0, 28), ("shj", 28, 56))
+        copy(("shm" + x, 0, 448), ind(("i16", 0, 16), ("shr", 0, 28)))
         vcopy(("thf" + x, 0, 1), ("thi" + x, 0, 1))
-        mset((wb(x, 5), 0, PAD), -256.0)
-        mset(("nw" + x, 0, PAD + WW), 0.0)
-        for d in range(N - 1):
-            copy(col("nw" + x, V + 2 * SH * d, V + 2 * SH * d + SH), ("cd", 512 + SH * d, 512 + SH * d + SH))
+        mset((wb(x, 5), 0, PAD), -MARK)
         for c in range(4):
             vcopy(("sl6" + x, c, 56, 8), ("sl" + x, c, 28, 4))
 
@@ -543,15 +607,16 @@ def plan():
         if k == 5:
             pointer_clip(x, 5, C5)
         else:
-            clip(x, k, C0 if k < 4 else C1, [4, 5] if k == 3 else [k + 1])
-        show(x, k + 1, ("sl" if k < 4 else "sl6") + x, SH if k < 4 else 2 * SH, L if k < 4 else V)
+            clip(x, k, C0 if k < 4 else C1)
+        sent = show(x, k + 1, ("sl" if k < 4 else "sl6") + x, SH if k < 4 else 2 * SH, L if k < 4 else V)
+        if k == 5:
+            dma([(part(("ed" + x, L * u, L * u + HL), 1 - u), part(slots(x, 0, HL), u)) for u in range(2)], after=sent)
+        if k == 3:
+            dma([(col(wb(x, 5), 0, L), col(wb(x, 4), 0, L))])
 
-    spare[0] = True
     more_constants()
     for x in "ab":
         tables(x)
-        zero_window("w9" + x)
-        mset(col("w9" + x, 0, L), 0.0)
     spare[0] = False
     for k in (1, 2, 3, 5, 6, 7):
         for x in "ab":
@@ -559,10 +624,6 @@ def plan():
             if k in (3, 7):
                 select(x, k // 4, k + 1)
                 split(x, k // 4, k + 1)
-            if k == 7:
-                row = 64 * "ab".index(x)
-                dma([(("hbm", "yv", (row, row + 64), (natural(a, u), natural(a, u) + w)), part(state("xs" + x, a, w), u))
-                     for a, w in ((0, HL), (HL, HC), (HL + HC, HC)) for u in range(2)])
     for x in "ab":
         pointer_last(x, C9)
     for o in reversed(ops):
@@ -588,6 +649,7 @@ def arrange(ops):
     free = {q: 0.0 for q in "vstgy"}
     pool = {q: set() for q in free}
     todo = {q: sum(q in o["how"] for o in ops) for q in free}
+    last = {q: 0 for q in list(free) + [None]}
     order, rows, sent = [], [0.0], [-1500.0]
 
     def release(i):
@@ -603,6 +665,9 @@ def arrange(ops):
         o = ops[i]
         o["q"], o["start"] = q, t
         busy = o["how"][q][0] if q else 0.0
+        if q and o["grp"] is not None and abs(last[q] - i) == 1 and ops[last[q]]["grp"] == o["grp"]:
+            busy -= JOIN
+        last[q] = i
         if not q:
             end[i] = end[o["with"]] + T_WAY
         elif o["late"]:
@@ -635,7 +700,8 @@ def arrange(ops):
             free[q] = min([ready[i] for i in pool[q] if ready[i] > t] + [free[p] for p in free if free[p] > t and todo[p]] + [t + 200.0])
             continue
         best = min(now, key=lambda i: ops[i]["prio"])
-        soon = [i for i in pool[q] if t < ready[i] <= t + AHEAD and len(ops[i]["how"]) == 1 and ops[i]["prio"] < ops[best]["prio"]]
+        soon = [i for i in pool[q] if ops[i]["prio"] < ops[best]["prio"] and t < ready[i] <= t + (
+            URGENT if ops[i]["urgent"] else AHEAD if len(ops[i]["how"]) == 1 else 0.0)]
         if soon and ops[best]["how"][q][0] > AHEAD:
             best = min(soon, key=lambda i: ready[i])
             t = ready[best]
@@ -692,6 +758,8 @@ def rank_program(g, core, T, topo):
         if k == "set":
             return e.memset(a[0], a[1])
         if k == "act":
+            if len(a) == 6:
+                return e.activation(*a[:5], accum_out=a[5])
             return e.activation(a[0], a[1], a[2]) if a[2] == COPY else e.activation(*(a + [1.0])[:5])
         if k == "mm":
             return e.matmul(*a)

from concourse.bass import DstId, RemoteDMATransfer
from concourse.mybir import AluOpType, AxisListType, ActivationFunctionType

L, CAP, SH, N = 1536, 256, 64, 8
HL, HC = L // 2, CAP // 2
V = L + 2 * CAP
NONE = V + (N - 1) * 2 * SH
MID = V - 1
PAD = 16
WW = NONE + 16
DUM = HL + 2 * HC
EH = 3 * HL + 2 * CAP
BIG = 4096.0
MAGIC = 12582912.0
MARK = 129.0
HIGH = 16384.0
OFF = 1548.0
NG = 5
CM = 256
PIECE = 32
RUN = 3
BLK = (112, 128)

C0 = ((0, 192), (192, 192), (384, 128), (512, 128), (640, 128))
C1 = ((0, 256), (256, 256), (512, 128), (640, 128), (768, 128))
C5 = (((0, 256),), ((256, 256), (512, 128)), ((640, 128), (768, 128)))
C9 = ((768, 128), (896, 128), (0, 256), (256, 256), (512, 192), (704, 64))
TOPS = ((512,), (640,))
RND = (512, 640)

SCRATCH = {}


def _buf(name, cols, dtype, where="sbuf"):
    SCRATCH[name] = (where, [128, cols], dtype)


for _x in "ab":
    for _n in ("w0", "w1", "w2", "w9"):
        _buf(_n + _x, PAD + WW, "bfloat16")
    for _n, _c, _t in (("xs", EH, "bfloat16"), ("xh", HL + HC, "float16"), ("ed", EH + CAP, "int32"), ("el", DUM, "uint16"),
                       ("ec", HL + HC, "float16"), ("em", DUM, "bfloat16"), ("shb", 28, "uint16"), ("shm", 448, "bfloat16"), ("shi", 28, "int32"),
                       ("sl", 28, "uint16"), ("sl6", 56, "uint16"), ("sb0", 896, "bfloat16"), ("sb1", 896, "bfloat16"),
                       ("thi", 1, "int32"), ("thf", 1, "float32"), ("splt", 96, "bfloat16"), ("px", 512, "bfloat16"),
                       ("s16", 16, "uint16"), ("dlo", 8, "uint16"), ("m16", 16, "uint16"), ("dl", HC, "uint16"),
                       ("gw", 16 * HC, "bfloat16")):
        _buf(_n + _x, _c, _t)
for _n, _c, _t in (("ones", 512, "bfloat16"), ("neg", 512, "bfloat16"), ("zz", 128, "bfloat16"), ("cols", 16, "float32"),
                   ("cand", 240, "bfloat16"), ("cs", 144, "bfloat16"), ("rk", 128, "float32"), ("acc", 8, "float32"),
                   ("bj", 8, "uint16"), ("cmp", HC, "bfloat16"), ("jrow", HC, "float32"), ("jb", 8, "float32"),
                   ("shf", 8, "float16"), ("xi", CAP, "float32"), ("hb", 448, "bfloat16"), ("of", 96, "bfloat16"),
                   ("beh", HC, "bfloat16"), ("dd", 2 * CAP, "int32"),
                   ("i16", 32, "bfloat16"), ("shj", 56, "int32"), ("shr", 28, "uint16"),
                   ("qk", 2048, "bfloat16"), ("lo", 896, "float16"), ("cd", 960, "bfloat16"), ("n8", 128, "float32"),
                   ("pi", 2, "int32"), ("bk", 2048, "bfloat16"), ("ak", 2048, "bfloat16"), ("mk", 2048, "bfloat16"),
                   ("tk", 1024, "bfloat16"), ("z", 896, "bfloat16"), ("f", 896, "bfloat16"), ("x", 896, "float16"),
                   ("gp", 896, "bfloat16"), ("pr", 896, "bfloat16"), ("tl", 56, "uint16"), ("eo", 3 * CM, "float32")):
    _buf(_n, _c, _t)
SQ = ("ga", "gm", "ngm", "ii", "ni", "ino", "mp", "mn", "i7", "i8", "c1k", "up", "su", "nb", "t3", "t4", "om", "d8k", "n4k", "m8k", "ith",
      "sel0", "sel1", "pm", "da", "db")
_buf("mx", 128 * len(SQ), "bfloat16")
for _k in range(NG):
    _buf("g%d" % _k, 16 * CM, "bfloat16")
for _k in range(8):
    _buf("ps%d" % _k, 512, "float32", "psum")

NDMA = 100
SEMAPHORES = (["qv", "qs", "qt", "qg"] + ["%s%d%s" % (s, k, x) for s in ("ar", "sn") for k in range(1, 10) for x in "ab"]
              + ["ld%d" % k for k in range(NDMA)])

A = AluOpType
COPY = ActivationFunctionType.Copy
IDENT = ActivationFunctionType.Identity
SIGN = ActivationFunctionType.Sign
SEMQ = {"v": "qv", "s": "qs", "t": "qt", "g": "qg"}

CYC, PE, GATH, SCAT, VFIX, SFIX, JOIN = 0.83, 0.5, 1.27, 2.2, 35.0, 45.0, 55.0
WAKE, AHEAD, URGENT = 120.0, 300.0, 450.0
T_WAY, T_ROWS, T_BYTE, T_FIRST, BEHIND = 1200.0, 2800.0, 0.04, 2500.0, 6000.0


def size(name):
    return 2 if SCRATCH[name][2] in ("bfloat16", "float16", "uint16") else 4


def width(s):
    if s[0] == "ind":
        return 16 * width(s[2])
    return len(range(s[1], s[2], s[3] if len(s) > 3 else 1))


def ranges(s):
    if s[0] == "ind":
        return ranges(s[1]) + ranges(s[2])
    return [(s[0], s[1], s[2]) + (s[4:6] if len(s) == 6 else (0, 128))]


def natural(m, u):
    if m < HL:
        return HL * u + m
    r = (m - HL) // HC
    return L + CAP * r + HC * u + (m - HL - HC * r)


def plan():
    ops, acc, bank, spare, urgent = [], {}, {}, [False], [False]

    def add(how, reads, writes, late=None, low=False, grp=None, free=False):
        i = len(ops)
        deps = {}
        for lst, wr in ((reads, False), (writes, True)):
            for b, a0, a1, p0, p1 in lst:
                if b[:2] == "ps":
                    if b in bank and bank[b] != i:
                        deps.setdefault(bank[b], False)
                    bank[b] = i
                    continue
                if not free:
                    for c0, c1, q0, q1, kind, j in acc.get(b, ()):
                        if c0 < a1 and a0 < c1 and q0 < p1 and p0 < q1 and (wr or kind) and j != i:
                            deps[j] = True
        for lst, wr in ((writes, True), (reads, False)):
            for b, a0, a1, p0, p1 in lst:
                if b[:2] != "ps":
                    old = acc.get(b, [])
                    if wr:
                        old = [e for e in old if not (a0 <= e[0] and e[1] <= a1 and p0 <= e[2] and e[3] <= p1)]
                    acc[b] = old + [(a0, a1, p0, p1, wr, i)]
        ops.append({"how": how, "deps": deps, "late": late, "prio": 10 ** 6 if low or spare[0] else i, "grp": grp,
                    "urgent": urgent[0] and grp is None})
        return i

    def rw(out, ins):
        reads = [r for s in ins for r in ranges(s)]
        if out[0] == "ind":
            return reads + ranges(out[2]), ranges(out[1])
        return reads, ranges(out)

    def cost(q, out, ins, tt=False):
        n = width(out)
        if out[0] == "ind":
            return 50 + n * SCAT
        if ins and ins[0][0] == "ind":
            return (65 if q == "s" else 50) + n * GATH * (2 if tt else 1)
        full = [s for s in [out] + ins if width(s) == n]
        if q == "s":
            k = 1.0
        elif tt:
            k = 1.0 if any(s[0][:2] == "ps" for s in ins) else 2.0
        else:
            k = 0.5 if all(size(s[0]) == 2 for s in full) else 1.0
        return max(64, n * k) * CYC + (SFIX if q == "s" else VFIX)

    def one(q, out, ins, call, tt=False, low=False):
        r, w = rw(out, ins)
        return add({q: (cost(q, out, ins, tt), [call])}, r, w, low=low)

    def either(out, ins, vcall, scall, grp=None):
        r, w = rw(out, ins)
        return add({"v": (cost("v", out, ins), [vcall]), "s": (cost("s", out, ins), [scall])}, r, w, grp=grp)

    def ind(win, off):
        return ("ind", win, off)

    def tiles(*xs):
        return [x for x in xs if isinstance(x, tuple)]

    def vcopy(o, i):
        one("v", o, [i], ("copy", o, i))

    def copy(o, i, bias=0.0, grp=None):
        if bias == 0.0:
            either(o, [i], ("copy", o, i), ("act", o, i, COPY, 0.0), grp)
        else:
            either(o, [i] + tiles(bias), ("ts", o, i, bias, None, A.add, None), ("act", o, i, IDENT, bias), grp)

    def vtt(o, i0, i1, op):
        one("v", o, [i0, i1], ("tt", o, i0, i1, op), True)

    def vts(o, i0, s1, op0, s2=None, op1=None):
        one("v", o, [i0] + tiles(s1, s2), ("ts", o, i0, s1, s2, op0, op1))

    def mset(o, c):
        if not spare[0] or len(o) == 6 or SCRATCH[o[0]][2] == "int32":
            one("v", o, [], ("set", o, c))
            return
        for a in range(o[1], o[2], 512):
            p = (o[0], a, min(a + 512, o[2]))
            src = ("ones", 0, width(p))
            if width(p) > 64:
                one("v", p, [], ("set", p, c))
            else:
                add({"v": (cost("v", p, []), [("set", p, c)]), "s": (cost("s", p, []), [("act", p, src, IDENT, c, 0.0)])},
                    ranges(src), ranges(p))

    def scaled(o, i, c):
        either(o, [i] + tiles(c), ("ts", o, i, c, None, A.mult, None), ("act", o, i, IDENT, 0.0, c))

    def slots(x, a, w):
        a += HL if a < HL else EH - HL
        return ("ed" + x, a, a + w)

    def mms(lst):
        if len(lst) > RUN and width(lst[0][2]) > 96:
            for n in range(0, len(lst), RUN):
                mms(lst[n:n + RUN])
            return
        r, w, t = [], [], 0.0
        for o, l, rh, st, sp in lst:
            r += ranges(l) + ranges(rh)
            w += ranges(o)
            t += max(64, width(rh)) * PE * (4 if size(l[0]) == 4 else 1)
        add({"t": (t, [("mm",) + m for m in lst])}, r, w)

    def mm(o, l, r, start=True, stop=True):
        mms([(o, l, r, start, stop)])

    def total(o, terms, start=True, stop=True):
        mms([(o, l, r, start and n == 0, stop and n == len(terms) - 1) for n, (l, r) in enumerate(terms)])

    def asel(o, i, pat, op, fill, base, cm, low=True):
        add({"g": (190 + 2 * width(o) * CYC, [("asel", o, i, pat, op, fill, base, cm)])}, ranges(i), ranges(o), low=low)

    def iota(o, pat, base, cm, low=True):
        add({"g": (150 + 2 * width(o) * CYC, [("iota", o, pat, base, cm)])}, [], ranges(o), low=low)

    ndma = [0]

    def dma(pairs, q="y", after=None):
        r = [x for o, i in pairs if i[0] != "hbm" for x in ranges(i)]
        w = [x for o, i in pairs if o[0] != "hbm" for x in ranges(o)]
        sem = "ld%d" % ndma[0]
        ndma[0] += 1
        on = [i if o[0] == "hbm" else o for o, i in pairs]
        n = sum(width(s) * size(s[0]) * (1 if len(s) == 6 else 2) for s in on)
        j = add({q: (60.0 * len(pairs), [("dma", o, i) for o, i in pairs])}, r, w, late=(sem, 16 * len(pairs), T_WAY, 120.0 * len(pairs) + 0.16 * n))
        if after is not None:
            ops[j]["deps"][after] = True

    def wb(x, k):
        return "w9" + x if k == 9 else "w%d%s" % (k % 3, x)

    def col(w, a, b, *rest):
        return (w, PAD + a, PAD + b) + rest

    def part(s, u):
        return s[:3] + (1, 64 * u, 64 * u + 64)

    def blk(m, i):
        return (m, 128 * i, 128 * i + 128)

    def sq(m):
        return blk("mx", SQ.index(m))

    def cl(n):
        return ("cols", n, n + 1)

    looked = []

    def show(x, k, lst, wd, top=V):
        n = 7 * wd
        sb = "sb%d%s" % (k % 2, x)
        win = col(wb(x, k), 0, top)
        if k == 9:
            vtt((sb, 0, n), ind(win, (lst, 0, n // 16)), ("cd", 512, 960), A.min)
        else:
            h = n // 64 * 2
            copy((sb, 0, h * 16), ind(win, (lst, 0, h)))
            copy((sb, h * 16, n), ind(win, (lst, h, n // 16)))
        first = T_FIRST if (x, k) == ("a", 1) else 0.0
        land = [col(wb(x, k), V + d * 2 * SH, V + d * 2 * SH + wd) for d in range(N - 1)]
        i = add({"g": (300.0 + first, [("far", x, k, sb, wd, land)])}, ranges((sb, 0, n)) + (ranges(col("w9" + x, 0, WW)) if k == 7 else []), [],
                late=("sn%d%s" % (k, x), 7, first + T_WAY, T_ROWS + T_BYTE * 256 * wd))
        ops[i]["deps"].update({j: True for j in looked if k == 6})
        j = add({}, [], [r for s in land for r in ranges(s)], late=("ar%d%s" % (k, x), 7), free=True)
        ops[j]["with"] = i
        return i

    gi, si = [0], [0]

    def gather(x, k, a, w):
        G = "g%d" % (gi[0] % NG)
        gi[0] += 1
        win = col(wb(x, k), 0, WW)
        for p in range(0, w, PIECE):
            q = min(p + PIECE, w)
            copy((G, 16 * p, 16 * q), ind(win, ("el" + x, a + p, a + q)), grp=gi[0])
        return G

    def sums(w):
        si[0] += 1
        return ("ps%d" % (si[0] % 4), 0, w)

    def over_slots(m, G, w):
        return [(sq(m) if m == "i8" else blk(m, i), (G, i, 16 * w, 16)) for i in range(16)]

    def spread(x, k, a, w):
        tops, xh = TOPS[k > 5], ("xh" + x, a, a + w)
        if a >= tops[-1]:
            mms([(("ps7", w * u, w * u + w), sq("sel%d" % u), xh, True, True) for u in range(2)])
            for u in range(2):
                copy(col(wb(x, k), natural(a, u), natural(a, u) + w), ("ps7", w * u, w * u + w), -OFF)
        if (a < tops[-1] or k == 4) and a >= RND[k > 5]:
            vts(("xs" + x, HL + a, HL + a + w), xh, -OFF, A.add)
        if a + w in tops:
            lo = ((0,) + tops)[tops.index(a + w)]
            dma([(part(col(wb(x, k), HL * u + lo, HL * u + a + w), h), part(("xs" + x, HL + lo, HL + a + w), u))
                 for u in range(2) for h in range(2)])

    def smaller(x, k, a, w, terms):
        ps, own = sums(w), ("xh" + x, a, a + w)
        if a < RND[k > 4]:
            terms, own = terms + [(sq("mp"), ("ones", 0, w)), (sq("mn"), ("ones", 0, w))], ("xs" + x, HL + a, HL + a + w)
        total(ps, terms)
        vtt(own, ps, own, A.min)
        spread(x, k + 1, a, w)

    def clip(x, k, chunks):
        for a, w in chunks:
            G = gather(x, k, a, w)
            smaller(x, k, a, w, [(sq("c1k"), ("ones", 0, w))] + over_slots("i8", G, w))

    def select(x, r, k):
        w, nb, c0 = wb(x, k), BLK[r], BLK[0] * r
        urgent[0] = r == 0
        cand, own = ("cand", c0, c0 + nb), ("cand", c0, c0 + 96)
        total(("ps5", 128, 224), [(blk("bk", i), col(w, i, L, 16)) for i in range(16)] + ([(sq("d8k"), ("splt" + x, 0, 96))] if r else []))
        vts(own, ("ps5", 128, 224), ("thf" + x, 0, 1), A.is_ge)
        one("v", ("cs", 8, 8 + nb), [cand, ("zz", 0, nb)], ("scan", ("cs", 8, 8 + nb), cand, ("zz", 0, nb), 0.0))
        mm(("ps5", 0, nb), sq("gm"), ("cs", 8, 8 + nb))
        total(("ps7", 0, nb), [(sq("gm"), ("cs", 7, 7 + nb)), (sq("up"), cand)])
        if r == 0:
            total(("ps7", 128, 224), [(sq("gm"), ("cs", 7, 103)), (sq("su"), own), (sq("d8k"), own)])
        for m in range(HC // 16):
            o, i, b, s = ("gw" + x, 128 * m, 128 * m + nb), ("ps5", 0, nb), ("jb", m, m + 1), ("acc", m, m + 1)
            add({"s": (nb * CYC + 40, [("act", o, i, SIGN, b, 1.0, s)])}, ranges(i) + ranges(b), ranges(o) + ranges(s))
        copy(("rk", 0, nb), ("ps7", 0, nb))
        if r == 0:
            vts(("of", 0, 96), ("ps7", 128, 224), 8192.0, A.add, float(CAP), A.min)
        vts(("bj", 0, 8), ("acc", 0, 8), -0.5, A.mult, nb / 2, A.add)
        vtt(("cmp", 0, HC), ind(("rk", 0, nb), ("bj", 0, 8)), ("jrow", 0, HC), A.is_le)
        total(("ps5", 224, 232), [(("n8", 0, 128), ("acc", 0, 8))] + [(blk("bk", i), ("cmp", i, HC, 16)) for i in range(16)])
        vts(("shf", 0, 8), ("ps5", 224, 232), 8.0 * nb, A.add)
        vts(("dlo" + x, 0, 8), ("ps5", 224, 232), cl(9 + r), A.add)
        mms([(("ps5", 240 + 8 * u, 248 + 8 * u), sq("sel%d" % u), ("shf", 0, 8), True, True) for u in range(2)])
        vcopy(("s16" + x, 0, 16), ("ps5", 240, 256))

    def shown_halves(x):
        copy(("hb", 0, 448), ind(("of", 0, 96), ("shb" + x, 0, 28)))
        mm(("ps4", 0, 448), sq("ii"), ("hb", 0, 448))
        vtt(("hb", 0, 448), ("ps4", 0, 448), ("shm" + x, 0, 448), A.min)
        total(("ps4", 448, 476), [(blk("bk", i), ("hb", i, 448, 16)) for i in range(16)])
        for c in range(4):
            vts(("sl6" + x, 4 + c, 56, 8), ("ps4", 448 + c, 476, 4), float(L), A.add)

    def split(x, r, k):
        w, ps = wb(x, k), "ps5"
        S16, px = ("s16" + x, 0, 16), ("px" + x, 0, CAP)
        h0, m0 = L + CAP * r, HL + HC * r
        old = ind(("ed" + x, 0, EH), ("dlo" + x, 0, 8))
        codes = col(w if r == 0 else "w9" + x, 0, V)
        xi, beh, M16 = ("xi", 0, CAP), ("beh", 0, HC), ("m16" + x, 0, 16)

        def halved():
            src = ind(col(w, 0, V), S16)
            either(xi, [src], ("ts", xi, src, 0.5, 0.25, A.mult, A.add), ("act", xi, src, IDENT, 0.25, 0.5))
            if r == 0:
                vts(("px" + x, CAP, 2 * CAP), xi, MAGIC, A.add, -MAGIC - MARK, A.add)
            vts(px, xi, MAGIC, A.add, -MAGIC, A.add)

        if r:
            vcopy(ind(codes, S16), ("cd", CAP, 2 * CAP))
            mset(col("w9" + x, h0, V), 0.0)
            sent = show(x, 9, ("sl" + x), SH)
        else:
            w5 = wb(x, k + 1)
            halved()
            vcopy(ind(col(w5, 0, V), S16), ("px" + x, CAP, 2 * CAP))
            copy(col(w5, h0, h0 + CAP), px)
            shown_halves(x)
            sent = show(x, 5, "sl6" + x, 2 * SH)
        urgent[0] = False
        vcopy(("dl" + x, 0, HC), old)
        vts(M16, ("ps5", 240, 256), cl(11), A.add)
        if r == 0:
            vts(("splt" + x, 0, 96), ("of", 0, 96), float(CAP), A.is_lt)
        gi[0] += NG
        for p in range(0, HC, 32):
            copy(("gw" + x, 16 * p, 16 * p + 512), ind(col(w, 0, WW), ("dl" + x, p, p + 32)), grp=gi[0])
        vcopy(("dd", 0, CAP), ind(("ed" + x, 0, EH), M16))
        total((ps, 0, HC), over_slots("ak", "gw" + x, HC))
        vts(beh, (ps, 0, HC), cl(0), A.is_ge, float(NONE), A.mult)
        mms([((ps, HC + HC * u, CAP + HC * u), sq("sel%d" % u), beh, True, True) for u in range(2)])
        total((ps, 3 * HC, 4 * HC), [(sq("ino"), o128), (sq("ni"), beh)])
        vtt(("dd", CAP, 2 * CAP), (ps, HC, HC + CAP), ("dd", 0, CAP), A.max)
        vcopy(ind(("ed" + x, 0, EH), M16), ("dd", CAP, 2 * CAP))
        for u in range(2):
            vtt(part(slots(x, m0, HC), u), part((ps, 3 * HC, 4 * HC), u), part(("dd", HC * u, HC * u + HC), u), A.max)
        lists(x, r)
        if r:
            halved()
            vcopy(ind(col(w, 0, V), S16), px)
            copy(col(w, h0, V), px)
            row = 64 * "ab".index(x)
            dma([(("hbm", "yv", (row, row + 64), (a, a + V // 2)), part(col(w, a, a + V // 2), u)) for u, a in ((0, 0), (1, V // 2))])
        else:
            vcopy(ind(("xs" + x, 0, EH), M16), px)
            vts(("xh" + x, RND[1], HL), ("xs" + x, HL + RND[1], L), OFF, A.add)
            for u in range(2):
                vts(part(("xh" + x, HL, HL + HC), u), part(("px" + x, HC * u, HC * u + HC), u), OFF, A.add)
            vcopy(ind(codes, S16), ("cd", 0, CAP))
            dma([(col(w, V + 2 * SH * d, V + 2 * SH * d + SH), ("cd", 512 + SH * d, 512 + SH * d + SH)) for d in range(N - 1)],
                after=sent)

    def lists(x, r):
        for a, w in ((0, 256), (256, 512), (HL + HC * r, HC))[::1 - 2 * r]:
            vcopy(("el" + x, a, a + w), slots(x, a, w))
        n = HL + HC + HC * r
        vts(("em" + x, 0, n), ("el" + x, 0, n), float(NONE), A.is_equal, -1.0, A.mult)
        if r == 0:
            vts(("ec" + x, 0, n), ("el" + x, 0, n), float(MID), A.subtract)
            for a, w in ((0, 384), (384, 512)):
                ec = ("ec" + x, a, a + w)
                total(("ps5", 0, w), [(sq("n4k"), ("ones", 0, w)), (sq("m8k"), ("em" + x, a, a + w))])
                vtt(ec, ("ps5", 0, w), ec, A.min)

    def pointer_clip(x, k, spans):
        for span in spans:
            a0, a1 = span[0][0], span[-1][0] + span[-1][1]
            for a, w in span:
                f, z, lo, xx = [(b, a, a + w) for b in ("f", "z", "lo", "x")]
                G = gather(x, k, a, w)
                pq = sums(w)
                total(pq, [(sq("i7"), ("ones", 0, w))] + over_slots("qk", G, w))
                vts(z, pq, HIGH * MAGIC, A.add, -HIGH * MAGIC, A.add)
                vts(f, z, 0.0, A.is_lt, OFF / (2 * MARK), A.add)
                vtt(lo, pq, z, A.subtract)
                total(("ps4", 0, w), [(sq("ii"), ("ec" + x, a, a + w)), (sq("t4"), f)])
                vts(xx, ("ps4", 0, w), cl(12), A.add, -2048.0, A.max)
            n = (a1 - a0) // 16
            total(("ps6", 0, n), [(blk("bk", i), ("x", a0 + i, a1, 16)) for i in range(16)])
            vts(("tl", a0 // 16, a1 // 16), ("ps6", 0, n), float(15 * 2048 + MID + PAD), A.add)
            for a, w in span:
                tl = ("tl", a // 16, (a + w) // 16)
                copy(("gp", a, a + w), ind((wb(x, k), 0, PAD + WW), tl), MARK - 7 - 3.5)
                copy(("pr", a, a + w), ind((wb(x, k - 1), 0, PAD + WW), tl), cl(1))
                looked.append(len(ops) - 1)
            for a, w in span:
                f, lo, gp = [(b, a, a + w) for b in ("f", "lo", "gp")]
                smaller(x, k, a, w, [(sq("i8"), lo), (sq("om"), f), (sq("i8"), gp)])
                ed = slots(x, a, w)
                total(("ps6", 0, w), [(sq("t4"), ("em" + x, a, a + w)), (sq("pm"), ("pr", a, a + w))])
                vtt(ed, ("ps6", 0, w), ed, A.min)
                vcopy(("el" + x, a, a + w), ed)

    pi = [0]

    def pointer_last(x, chunks):
        row = 64 * "ab".index(x)
        for a, w in chunks:
            p = pi[0] % 3
            pi[0] += 1
            xx, eo = ("x", CM * p, CM * p + w), ("eo", CM * p, CM * p + w)
            ps, pt = sums(w), ("ps%d" % (4 + pi[0] % 2 * 2), 0, w)
            G = gather(x, 9, a, w)
            total(ps, over_slots("mk", G, w))
            vts(xx, ps, 0.0, A.max, -(NONE + BIG) / 16, A.add)
            total(pt, [(sq("t4"), ("em" + x, a, a + w)), (sq("ngm"), xx)])
            vtt(eo, pt, slots(x, a, w), A.min)
            dma([(("hbm", "ye", (row, row + 64), (natural(a, u), natural(a, u) + w)), part(eo, u)) for u in range(2)])

    for n, x in enumerate("ab"):
        rows = (64 * n, 64 * n + 64)
        dma([(part(("shi" + x, 0, 28), u), ("hbm", "sh", rows, (0, 28))) for u in range(2)])
        dma([(part(col(wb(x, 1), 0, L), 0), ("hbm", "v0", rows, (0, L)))])
        dma([(part(col(wb(x, 1), 0, L), 1), ("hbm", "v0", rows, (0, L)))], "s" if n == 0 else "y")
    for n, x in enumerate("ab"):
        rows = (64 * n, 64 * n + 64)
        dma([(part(slots(x, 0, HL), u), ("hbm", "e", rows, (HL * u, HL * u + HL))) for u in range(2)])
        dma([(part(("xs" + x, HL, L), u), ("hbm", "v0", rows, (HL * u, HL * u + HL))) for u in range(2)])
        dma([(part(("thi" + x, 0, 1), u), ("hbm", "th", rows, (0, 1))) for u in range(2)])

    G8 = [[0, 8], [1, 16]]
    o128 = ("ones", 0, 128)

    def zero_window(w):
        mset(col(w, L, V), 0.0)
        mset(col(w, NONE, WW), 0.0)
        for d in range(N - 1):
            b = V + d * 2 * SH + SH
            mset(col(w, b, b + SH), 0.0)

    mset(("ones", 0, 512), 1.0)
    asel(sq("ii"), o128, [[-1, 128]], A.is_equal, 0.0, 0, 1, False)
    for u in range(2):
        asel(sq("sel%d" % u), o128, [[0, 2], [-1, 64]], A.is_equal, 0.0, -64 * u, 1, False)
    asel(sq("ga"), o128, [[-16, 8], [0, 16]], A.is_ge, 0.0, 0, 1, False)
    asel(sq("gm"), sq("ga"), [[16, 8], [0, 16]], A.is_ge, 0.0, 15, -1, False)
    for x in "ab":
        vcopy(("sl" + x, 0, 28), ("shi" + x, 0, 28))
        show(x, 1, "sl" + x, SH, L)
    spare[0] = True
    for n, c in (("i8", 0.125), ("d8k", -8192.0), ("n4k", -BIG), ("i7", 7.0), ("ni", -1.0), ("ino", float(NONE)), ("mp", MAGIC)):
        scaled(sq(n), sq("ii"), c)
    for p0, p1, c in ((0, 32, 48.0), (32, 64, (OFF - 0.4375) / 32 - 48.0), (64, 128, 0.0)):
        mset(sq("c1k") + (1, p0, p1), c)
    mset(sq("mn"), 0.0)
    for p0, c in ((0, -MAGIC), (32, -1536.0), (64, 1536.0 - OFF)):
        mset(sq("mn") + (1, p0, p0 + 1), c)
    scaled(("n8", 0, 128), sq("ii"), -8.0)
    for x in "ab":
        vcopy(("el" + x, 0, HL), slots(x, 0, HL))
        vts(("xh" + x, RND[0], HL), ("xs" + x, HL + RND[0], L), OFF, A.add)
        for k in (1, 2, 3):
            zero_window(wb(x, k))
        mset((wb(x, 4), 0, PAD), 0.0)
    spare[0] = False
    for k in range(16):
        asel(blk("bk", k), sq("gm"), G8, A.is_equal, 0.0, -k, 0)
    asel(sq("up"), sq("gm"), [[1, 128]], A.is_ge, 0.0, 0, -1)
    asel(sq("su"), sq("gm"), [[1, 128]], A.is_gt, 0.0, 0, -1)
    asel(sq("ith"), sq("ii"), G8, A.is_equal, 0.0, 0, 0)
    iota(("pi", 0, 1), [[0, 1]], 0, 1, False)
    iota(("i16", 16, 32), [[1, 16]], 0, 0, False)
    iota(("jrow", 0, HC), [[1, HC]], 0, 0, False)
    iota(("jb", 0, 8), [[-16, 8]], 0, 0, False)
    iota(("gwa", 0, 512), [[-272, 2], [-16, 16], [0, 16]], 1392, 0, False)
    iota(("gwa", 1024, 1536), [[16, 2], [0, 16], [-1, 16]], 16, 0, False)
    iota(("gwa", 512, 960), [[-128, 7], [-16, 4], [0, 16]], 816, 0, False)
    iota(("gwa", 1536, 1984), [[0, 28], [-1, 16]], 16, 0, False)
    for x in "ab":
        rows = (64 * "ab".index(x), 64 * "ab".index(x) + 64)
        for a, b in ((0, HL), (L, L + 640), (L + 640, EH)):
            iota(("ed" + x, a, b), [[0, b - a]], NONE, 0)
        for a in range(0, WW, 592):
            iota(col("w9" + x, a, a + 592), [[0, 592]], 0, 0)
        dma([(part(("ed" + x, L * u, L * u + HL), 1 - u), ("hbm", "e", rows, (HL * u, HL * u + HL))) for u in range(2)])

    def by_slot(m, src, steps):
        for a in range(0, 2048, 512):
            t0, t1, out = ("tk", 0, 512), ("tk", 512, 1024), (m, a, a + 512)
            cur = src
            for op, fill in steps:
                nxt = t1 if cur == t0 else t0
                asel(nxt, cur, [[-1, 4], [0, 8], [1, 16]], op, fill, -(a // 128), 0)
                cur = nxt
            nxt = t1 if cur == t0 else t0
            asel(nxt, cur, [[0, 4], [-16, 8], [0, 16]], A.is_ge, 0.0, 0, 1)
            asel(out, nxt, [[0, 4], [16, 8], [0, 16]], A.is_ge, 0.0, 15, -1)

    spare[0] = True
    mset(("neg", 0, 512), -512.0)
    by_slot("ak", ("ones", 0, 512), [(A.is_gt, -1.0)])
    for a in range(0, 2048, 512):
        asel(("tk", 0, 512), ("ones", 0, 512), [[0, 4], [-1, 128]], A.is_equal, 0.0, 0, 1)
        asel(("qk", a, a + 512), ("tk", 0, 512), [[-255, 4], [-16, 8], [256, 16]], A.not_equal, HIGH, -15 - 255 * (a // 128), 1)
    by_slot("mk", ("neg", 0, 512), [(A.is_gt, 0.25), (A.is_ge, 0.0)])

    def more_constants():
        for n, c in (("nb", -BIG), ("om", MARK / 8), ("ngm", -1.0), ("m8k", -2 * BIG)):
            scaled(sq(n), sq("gm"), c)
        asel(sq("t3"), sq("nb"), [[1, 128]], A.is_ge, 0.0, 0, -1)
        asel(sq("t4"), sq("t3"), [[-1, 128]], A.not_equal, BIG, 0, 1)
        one("v", cl(0), [sq("ith")], ("sum", cl(0), sq("ith")))
        r16 = ("pi", 1, 2)
        vts(r16, ("pi", 0, 1), 15, A.bitwise_and)
        mset(("zz", 0, 128), 0.0)
        mset(("cs", 0, 8), 0.0)
        mset(("cand", 96, 112), 1.0)
        mset(("cand", 208, 224), 0.0)
        mset(("cand", 224, 240), 1.0)
        vts(cl(1), r16, 8.0, A.is_ge, (NONE + BIG) / 16, A.mult)
        vts(cl(2), r16, 4.0, A.is_lt)
        vts(cl(3), r16, 8.0, A.is_lt)
        vtt(cl(4), cl(3), cl(2), A.subtract)
        vts(cl(5), cl(3), -2.25, A.mult, 2.0, A.add)
        vts(cl(6), ("pi", 0, 1), 64.0, A.is_ge, -float(HL), A.mult)
        vcopy(cl(8), r16)
        for r in range(2):
            vts(cl(9 + r), cl(6), 8.0 * BLK[r] + HL, A.add)
        vts(cl(11), cl(6), float(HL), A.add)
        vts(cl(12), r16, BIG * OFF / (2 * MARK), A.mult, -BIG - BIG * OFF / (2 * MARK), A.add)
        vts(cl(7), ("pi", 0, 1), 64.0, A.is_ge, float(HC), A.mult)
        vts(cl(13), cl(7), 0.5, A.add)
        vts(("jb", 0, 8), ("jb", 0, 8), cl(8), A.subtract, cl(13), A.subtract)
        copy(("jrow", 0, HC), ("jrow", 0, HC), cl(7))
        scaled(sq("pm"), sq("gm"), cl(5))
        scaled(sq("da"), sq("ii"), cl(2))
        scaled(sq("db"), sq("ii"), cl(4))
        for a, w in ((0, 512), (512, 448)):
            total(("ps6", 0, w), [(sq("da"), ("gwa", a, a + w)), (sq("db"), ("gwa", 1024 + a, 1024 + a + w))])
            copy(("cd", a, a + w), ("ps6", 0, w))
        vts(("i16", 0, 16), ("i16", 16, 32), cl(8), A.is_equal, float(CAP), A.mult)

    def tables(x):
        vts(("shj", 0, 28), ("shi" + x, 0, 28), 4, A.logical_shift_right)
        vcopy(("shb" + x, 0, 28), ("shj", 0, 28))
        vts(("shj", 28, 56), ("shi" + x, 0, 28), 15, A.bitwise_and)
        vcopy(("shr", 0, 28), ("shj", 28, 56))
        copy(("shm" + x, 0, 448), ind(("i16", 0, 16), ("shr", 0, 28)))
        vcopy(("thf" + x, 0, 1), ("thi" + x, 0, 1))
        mset((wb(x, 5), 0, PAD), -MARK)
        for c in range(4):
            vcopy(("sl6" + x, c, 56, 8), ("sl" + x, c, 28, 4))

    def step(x, k):
        if k == 5:
            pointer_clip(x, 5, C5)
        else:
            clip(x, k, C0 if k < 4 else C1)
        sent = show(x, k + 1, ("sl" if k < 4 else "sl6") + x, SH if k < 4 else 2 * SH, L if k < 4 else V)
        if k == 5:
            dma([(part(("ed" + x, L * u, L * u + HL), 1 - u), part(slots(x, 0, HL), u)) for u in range(2)], after=sent)
        if k == 3:
            dma([(col(wb(x, 5), 0, L), col(wb(x, 4), 0, L))])

    more_constants()
    for x in "ab":
        tables(x)
    spare[0] = False
    for k in (1, 2, 3, 5, 6, 7):
        for x in "ab":
            step(x, k)
            if k in (3, 7):
                select(x, k // 4, k + 1)
                split(x, k // 4, k + 1)
    for x in "ab":
        pointer_last(x, C9)
    for o in reversed(ops):
        for j in o["deps"]:
            if ops[j]["prio"] > len(ops):
                ops[j]["need"] = min(ops[j].get("need", 10 ** 6), o.get("need", o["prio"]))
    for o in ops:
        o["prio"] = o.get("need", o["prio"])
    return ops


def arrange(ops):
    n = len(ops)
    after = [[] for _ in range(n)]
    left = [0] * n
    for i, o in enumerate(ops):
        pre = set(o["deps"]) | ({o["with"]} if "with" in o else set())
        left[i] = len(pre)
        for j in pre:
            after[j].append(i)
    ready = [0.0] * n
    end = [0.0] * n
    free = {q: 0.0 for q in "vstgy"}
    pool = {q: set() for q in free}
    todo = {q: sum(q in o["how"] for o in ops) for q in free}
    last = {q: 0 for q in list(free) + [None]}
    order, rows, sent = [], [0.0], [-1500.0]

    def release(i):
        o = ops[i]
        if not o["how"]:
            finish(i, None, ops[o["with"]]["start"])
            return
        ready[i] = max([0.0] + [end[j] + (WAKE if hard or ops[j]["q"] not in o["how"] else 0.0) for j, hard in o["deps"].items()])
        for q in o["how"]:
            pool[q].add(i)

    def finish(i, q, t):
        o = ops[i]
        o["q"], o["start"] = q, t
        busy = o["how"][q][0] if q else 0.0
        if q and o["grp"] is not None and abs(last[q] - i) == 1 and ops[last[q]]["grp"] == o["grp"]:
            busy -= JOIN
        last[q] = i
        if not q:
            end[i] = end[o["with"]] + T_WAY
        elif o["late"]:
            rows[0] = max(rows[0], t + o["late"][2]) + o["late"][3]
            end[i] = rows[0] + (0.0 if q == "g" else T_WAY)
        else:
            end[i] = t + busy
        if q == "g" and o["late"]:
            sent[0] = t + busy
        if q:
            free[q] = t + busy
            for p in o["how"]:
                pool[p].discard(i)
                todo[p] -= 1
        order.append(i)
        for j in after[i]:
            left[j] -= 1
            if left[j] == 0:
                release(j)

    for i in [i for i in range(n) if left[i] == 0]:
        release(i)
    while any(todo.values()):
        q = min((p for p in free if todo[p]), key=lambda p: (free[p], not pool[p]))
        t = free[q]
        now = [i for i in pool[q] if ready[i] <= t]
        if q == "g":
            now = [i for i in now if ops[i]["late"] or t + ops[i]["how"][q][0] <= sent[0] + BEHIND or t > sent[0] + 4 * BEHIND]
        if not now:
            free[q] = min([ready[i] for i in pool[q] if ready[i] > t] + [free[p] for p in free if free[p] > t and todo[p]] + [t + 200.0])
            continue
        best = min(now, key=lambda i: ops[i]["prio"])
        soon = [i for i in pool[q] if ops[i]["prio"] < ops[best]["prio"] and t < ready[i] <= t + (
            URGENT if ops[i]["urgent"] else AHEAD if len(ops[i]["how"]) == 1 else 0.0)]
        if soon and ops[best]["how"][q][0] > AHEAD:
            best = min(soon, key=lambda i: ready[i])
            t = ready[best]
        elif q == "s" and ops[best]["grp"] is not None:
            best = max(i for i in now if ops[i]["grp"] == ops[best]["grp"])
        finish(best, q, t)
    order.sort(key=lambda i: ops[i]["start"])
    return order, max(end)


PLAN = []


def rank_program(g, core, T, topo):
    rank = T.rank_of(core)
    if rank is None:
        return
    if not PLAN:
        ops_ = plan()
        PLAN.extend([ops_, arrange(ops_)[0]])
    ops, order = PLAN
    eng = {"v": g.vector, "s": g.scalar, "t": g.tensor, "g": g, "y": g.sync}

    def ap(s):
        if not isinstance(s, tuple):
            return s
        if s[0] == "ind":
            return ap(s[1]).indirect(ap(s[2]))
        if s[0] == "hbm":
            return T[s[1]][s[2][0]:s[2][1], s[3][0]:s[3][1]]
        if len(s) == 6:
            return T[s[0]][s[4]:s[5], s[1]:s[2]]
        if len(s) == 4:
            return T[s[0]][:, s[1]:s[2]:s[3]]
        return T[s[0]][:, s[1]:s[2]]

    def far(x, k, sb, wd, land):
        tr = []
        for d in range(1, N):
            dst = T.cores[(rank + d) % N]
            a = topo.addr(dst)
            tr.append(RemoteDMATransfer(dst_ids=[DstId(rid=a[0], pnc=a[1])], dma_engine_mask=1 << topo.engines(core, dst)[d - 1],
                                        remote_sem=T.sem["ar%d%s" % (k, x)], src=T[sb][:, (d - 1) * wd:d * wd], dst=ap(land[d - 1])))
        g.remote_dma_fused(tr, local_sem=T.sem["sn%d%s" % (k, x)])

    def issue(e, c):
        k, a = c[0], [ap(s) for s in c[1:]]
        if k == "copy":
            return e.tensor_copy(a[0], a[1])
        if k == "tt":
            return e.tensor_tensor(a[0], a[1], a[2], a[3])
        if k == "ts":
            return e.tensor_scalar(*(a[:5] if a[5] is None else a))
        if k == "set":
            return e.memset(a[0], a[1])
        if k == "act":
            if len(a) == 6:
                return e.activation(*a[:5], accum_out=a[5])
            return e.activation(a[0], a[1], a[2]) if a[2] == COPY else e.activation(*(a + [1.0])[:5])
        if k == "mm":
            return e.matmul(*a)
        if k == "scan":
            return e.tensor_tensor_scan(a[0], a[1], a[2], a[3], A.add, A.add)
        if k == "sum":
            return e.tensor_reduce(a[0], a[1], AxisListType.X, A.add)
        if k == "asel":
            return e.affine_select(*a)
        if k == "iota":
            if SCRATCH[c[1][0]][2] == "int32":
                return e.iota(*a)
            return e.iota(*a, allow_small_or_imprecise_dtypes=True)
        return e.dma_start(a[0], a[1])

    queue = {q: [i for i in order if ops[i]["q"] == q] for q in eng}
    place = {i: n for q in queue for n, i in enumerate(queue[q])}
    cnt = {q: 0 for q in SEMQ}
    know = {q: {} for q in eng}
    tok, total = {}, {}

    def need(q, t):
        sem, val, snap = t
        if know[q].get(sem, 0) >= val:
            return
        eng[q].wait_ge(T.sem[sem], val)
        for s_, v_ in snap.items():
            if know[q].get(s_, 0) < v_:
                know[q][s_] = v_
        know[q][sem] = val

    for i in order:
        o = ops[i]
        q = o["q"]
        if i in tok:
            continue
        if q is None:
            tok[i] = (o["late"][0], o["late"][1], {})
            total[o["late"][0]] = o["late"][1]
            continue
        run, calls = [i], o["how"][q][1]
        if o["grp"] is not None:
            for j in queue[q][place[i] + 1:]:
                if ops[j]["grp"] != o["grp"] or abs(j - run[-1]) != 1 or j in run or not all(d in tok for d in ops[j]["deps"]):
                    break
                run.append(j)
            lo, hi = ops[min(run)]["how"][q][1][0], ops[max(run)]["how"][q][1][0]
            calls = [(lo[0], lo[1][:2] + hi[1][2:], lo[2][:2] + (lo[2][2][:2] + hi[2][2][2:],)) + lo[3:]]
        best = {}
        for j in run:
            for d, hard in ops[j]["deps"].items():
                if (hard or ops[d]["q"] != q) and (tok[d][0] not in best or best[tok[d][0]][1] < tok[d][1]):
                    best[tok[d][0]] = tok[d]
        for t in sorted(best.values(), key=lambda t: -len(t[2])):
            need(q, t)
        snap = dict(know[q])
        if o["late"]:
            sem, val = o["late"][:2]
            for c in calls:
                if c[0] == "far":
                    far(*c[1:])
                else:
                    issue(eng[q], c).then_inc(T.sem[sem], 16)
        else:
            sem = SEMQ[q]
            for c in calls:
                issue(eng[q], c).then_inc(T.sem[sem], 1)
            cnt[q] += len(calls)
            val = cnt[q]
        total[sem] = val
        for j in run:
            tok[j] = (sem, val, snap)

    for sem in sorted(total):
        if know["y"].get(sem, 0) < total[sem]:
            g.sync.wait_ge(T.sem[sem], total[sem])
